import numpy as np, ml_dtypes
CORES = [24,25,26,27,28,29,30,31]
N = 8
BF = ml_dtypes.bfloat16
S, L, RO, WEAR = 4096, 192, 2, 16
def near(rng, home, h):
    q = S // 16
    return np.take_along_axis(np.broadcast_to(home, (N, 8, S)), h * q + rng.integers(0, q, h.shape), 2)
def parts(rng):
    home = np.argsort(rng.random((8, S)), axis=1); hab = np.zeros((8, S), np.int64)
    np.put_along_axis(hab, home, np.broadcast_to(np.arange(S) // (S // 16), (8, S)), 1)
    base = rng.integers(0, 256, (N, 8, 16, 16))
    x = np.clip(np.take_along_axis(base, hab[None, :, None, :], 3) + rng.integers(-60, 61, (N, 8, 16, S)), 0, 255)
    lab = np.argsort(rng.random((N, 8, L)), axis=2); inv = np.argsort(lab, axis=2)
    h = np.broadcast_to((lab % 16)[:, :, None, :], (N, 8, 16, L)).reshape(N, 8, 16 * L)
    m = np.where(rng.random(h.shape) < 0.75, near(rng, home, h), rng.integers(0, S, h.shape)).reshape(N, 8, 16, L)
    h = np.broadcast_to(hab[None, :, None, :], (N, 8, 16, S)).reshape(N, 8, 16 * S)
    nb = np.where(rng.random(h.shape) < 0.6, near(rng, home, h), rng.integers(0, S, h.shape)).reshape(N, 8, 16, S)
    v = hab[None] + 16 * rng.integers(0, L // 16, (N, 8, S))
    own = np.where(rng.random((N, 8, S)) < 0.6, np.take_along_axis(inv, v, 2), rng.integers(0, L, (N, 8, S)))
    return x, nb, m, own, rng.integers(600, 1100, (N, 8))
def pack(x, nb, m, own, th):
    return {"x0": x.reshape(N, 128, S).astype(np.float32).astype(BF), "nb": nb.reshape(N, 128, S).astype(np.int32), "m0": m.reshape(N, 128, L).astype(np.int32),
            "own0": own.reshape(N, 8, S).astype(np.int32), "th": th.reshape(N, 8, 1).astype(np.int32)}
def setup_inputs(rng):
    return pack(*parts(rng))
def setup_inputs_ties(rng):
    x, nb, m, own, th = parts(rng); step = rng.choice(np.array([1, 5, 40]), (N, 8, 1, 1))
    lo = ((256 - 3 * step) * rng.random((N, 8, 1, 1)) * (rng.random((N, 8, 1, 1)) < 0.7)).astype(np.int64)
    x = lo + step * rng.integers(0, 4, x.shape)
    pool = rng.integers(0, S, (N, 8, 3, L)); few = np.take_along_axis(pool, rng.integers(0, 3, m.shape), 2)
    m = np.where(rng.random((N, 8, 1, L)) < 0.7, few, rng.integers(0, S, m.shape))
    th = step[:, :, 0, 0] * rng.integers(14, 19, (N, 8))
    z = int(rng.integers(0, 8)); o = rng.permutation(S); cold, warm = o[:S // 2], o[S // 2:]; h = rng.integers(140, 250, N)
    is_cold = np.zeros(S, bool); is_cold[cold] = True
    x[:, z] = np.where(is_cold, 0, h[:, None, None]) + rng.integers(0, 2, (N, 16, S))
    three = cold[rng.integers(0, S // 2, (N, 3, L))]; m[:, z] = np.take_along_axis(three, rng.integers(0, 3, (N, 16, L)), 1)
    nb[:, z] = warm[rng.integers(0, S - S // 2, (N, 16, S))]; th[:, z] = 16 * h + rng.integers(3, 9, N)
    return pack(x, nb, m, own, th)
def setup_inputs_corners(rng):
    x, nb, m, own, th = parts(rng); K = S // L; ev = (K + 1) // 2; od = K // 2
    q = int(rng.integers(0, N)); p = (q - 1) % N; u = (q - 2) % N; la = np.arange(L); st = np.arange(S)
    turn = [rng.permutation(8) for r in range(N)]; turn[u] = turn[p]
    for r in range(N):
        for i, g in enumerate(turn[r]):
            if i == 0: own[r, g] = int(rng.choice(np.array([0, L - 1, L // 2])))
            if i == 1:
                own[r, g] = rng.permutation(L)[st % L]; m[r, g] = la + L * rng.integers(0, K, (16, L))
            if i == 2: m[r, g] = rng.choice(np.array([0, S - 1, int(rng.integers(0, S))]), (1, L))
            if i == 3: nb[r, g] = st[None, :]
            if i == 4: nb[r, g] = (S - 1) * rng.integers(0, 2, (1, S))
            if i == 5:
                th[r, g] = 0; x[r, g] = rng.integers(0, WEAR + 2, (16, S))
            if i == 6:
                th[r, g] = 4080; own[r, g] = (L - 1) * rng.integers(0, 2, S); m[r, g] = (S - 1) * rng.integers(0, 2, (16, L))
            if i == 7: x[r, g] = int(rng.choice(np.array([0, 7, 255])))
    x[q] = np.where((st // L) % 2 == 0, rng.integers(0, 9, (8, 16, S)), 255 - rng.integers(0, 9, (8, 16, S)))
    x[q] = np.where(st // L == 1, rng.integers(18, 21, (8, 16, S)), x[q])
    nb[q] = rng.integers(0, L, (8, 16, S)) + 2 * L * rng.integers(0, ev, (8, 16, S)); th[q] = 200
    own[q] = np.argsort(rng.random((8, L)), axis=1)[:, st % L]
    m[q] = la + L * (2 * rng.integers(1, od, (8, 16, L)) + 1); m[p] = la + 2 * L * rng.integers(0, ev, (8, 16, L))
    m[u, int(turn[u][0])] = L + la
    return pack(x, nb, m, own, th)
def setup_inputs_ends(rng):
    home = 1 + np.argsort(rng.random((8, S - 3)), axis=1)[:, :L]; homes = np.broadcast_to(home, (N, 8, L))
    c = rng.choice(np.array([0, 1, 8, 15, 16]), (N, 8)); c[0, 0] = 0; c[0, 1] = 16; c[N - 1] = rng.choice(np.array([1, 8, 15]), 8)
    x = 255 * rng.integers(0, 2, (N, 8, 16, S))
    x[..., 0] = 255 * (np.argsort(rng.random((N, 8, 16)), axis=2) < c[:, :, None]); x[..., S - 1] = 255 - x[..., 0]; x[..., S - 2] = 255
    np.put_along_axis(x, np.broadcast_to(home[None, :, None, :], (N, 8, 16, L)), 0, 3)
    nb = (S - 1) * rng.integers(0, 2, (N, 8, 16, S))
    nb = np.where(rng.random(nb.shape) < 0.15, np.take_along_axis(homes, rng.integers(0, L, (N, 8, 16 * S)), 2).reshape(nb.shape), nb)
    side = rng.integers(0, 2, (N, 8, S)); nb[:, :, 15] = (S - 1) * side; nb[:, :, 0] = (S - 1) * (1 - side)
    sig = np.argsort(rng.random((N, 8, L)), axis=2); own = (L - 1) * rng.integers(0, 2, (N, 8, S)); np.put_along_axis(own, homes, sig, 2)
    mix = (S - 1) * rng.integers(0, 2, (N, 8, 16, L)); kind = rng.choice(np.array([0, 1, 2, 3, 3, 3]), (N, 8, 1, L)); kind[N - 2] = 3; kind[N - 1] = rng.integers(0, 2, (8, 1, L))
    place = np.argsort(rng.random((N, 8, 16, L)), axis=2); place[:, :, :, L - 1] = np.array([2, 3, 4, 5, 6, 7, 8, 9, 10, 11, 12, 13, 14, 15, 0, 1])
    two = rng.random((N, 8, 1, L)) < 0.5; two[..., L - 1] = True
    far = np.where((place == 1) | ((place == 2) & two), S - 2, mix)
    keep = np.where((place == 0) | ((place == 3) & two), home[None, :, None, :], far)
    m = np.where(kind == 0, 0, np.where(kind == 1, S - 1, np.where(kind == 2, mix, keep)))
    th = 4080 * rng.integers(0, 2, (N, 8)); th[:, 2] = 0; th[:, 7] = 4080
    i = int(rng.integers(0, 7)); th[N - 1] = 4080; th[N - 1, i] = 0
    g = (i + 1 + int(rng.integers(0, 6))) % 7; a = int(rng.integers(0, L)); nb[N - 1, g, :, home[g, a]] = m[N - 1, g, 0, sig[N - 1, g, a]]
    return pack(x, nb, m, own, th)
def setup_inputs_spread(rng):
    x, nb, m, own, th = parts(rng)
    x = np.minimum(np.exp2(8 * rng.random((N, 8, 1, S))) * rng.random((N, 8, 16, S)) * 1.25, 255.0).astype(np.int64) * (rng.random((N, 8, 1, S)) > 0.0625)
    m = np.minimum((S * rng.random((N, 8, 16, L)) ** (1 + 3 * rng.random((N, 8, 1, L)))).astype(np.int64), S - 1)
    m = np.where(rng.random((N, 8, 1, L)) < 0.5, m, S - 1 - m)
    u = np.minimum((S * rng.random((N, 4, 16, S)) ** 2).astype(np.int64), S - 1); nb[:, 1::2] = u
    own = np.minimum((L * rng.random((N, 8, S)) ** 2).astype(np.int64), L - 1)
    return pack(x, nb, m, own, np.exp2(8 + 3 * rng.random((N, 8))).astype(np.int64))
def check_inputs(d):
    bad = []
    for k, lo, hi in (("x0", 0, 255), ("nb", 0, S - 1), ("m0", 0, S - 1), ("own0", 0, L - 1), ("th", 0, 4080)):
        try:
            v = np.asarray(d[k]).astype(np.float32).astype(np.float64)
            if not np.all((v >= lo) & (v <= hi)): bad.append("range of " + k)
            elif not np.all(v == np.floor(v)): bad.append("whole numbers of " + k)
        except Exception:
            bad.append("form of " + k)
    return bad
def centre(x, m):
    v = np.take_along_axis(x, m.reshape(8, 1, 16 * L), 2).reshape(8, 16, 16, L)
    c = (np.max(v, axis=2) + np.min(v, axis=2)) >> 1
    d = np.add.reduce(np.abs(v - c[:, :, None, :]), axis=1)
    return c, np.argmin(d, axis=1), np.argmax(d, axis=1)
def reference(x0, nb, m0, own0, th):
    X = x0.astype(np.float32).astype(np.int32).reshape(N, 8, 16, S); nbs = nb.astype(np.int64).reshape(N, 8, 16, S)
    M = m0.astype(np.int64).reshape(N, 8, 16, L); O = own0.astype(np.int64).reshape(N, 8, S); T = th.astype(np.int64).reshape(N, 8)
    wins = np.zeros(N, np.int64); lane = np.broadcast_to(np.arange(L), (8, L)); grp = np.broadcast_to(np.arange(8)[:, None], (8, L))
    for t in range(RO):
        res, back = [], []; now = np.zeros(N, np.int64)
        for q in range(N):
            p = (q - 1 - t % (N - 1)) % N
            ci, ki, fi = centre(X[q], M[p]); cr, kr, fr = centre(X[q], M[q])
            s = np.take_along_axis(M[p], ki[:, None, :], 1)[:, 0]
            b = np.take_along_axis(O[q], s, 1)
            low = np.full((8, L), L); np.minimum.at(low, (grp, b), lane)
            fight = np.take_along_axis(low, b, 1) == lane
            n = np.take_along_axis(nbs[q], s[:, None, :], 2)
            v = np.take_along_axis(X[q], n.reshape(8, 1, 16 * L), 2).reshape(8, 16, 16, L)
            ei = np.add.reduce(np.abs(v - ci[:, :, None, :]), axis=1)
            er = np.add.reduce(np.abs(v - np.take_along_axis(cr, b[:, None, :], 2)[:, :, None, :]), axis=1)
            lim = T[q][:, None, None] + (wins[q] & 63)
            won = np.count_nonzero(ei < lim, axis=1) > np.count_nonzero(er < lim, axis=1)
            e = np.where(won[:, None, :], ei, er)
            best = np.take_along_axis(n, np.argmin(e, axis=1)[:, None, :], 1)[:, 0]
            worst = np.take_along_axis(n, np.argmax(e, axis=1)[:, None, :], 1)[:, 0]
            g, a = np.nonzero(fight); w = won[g, a]; bb = b[g, a]; ss = s[g, a]
            res.append((q, g, fr[g, bb], bb, np.where(w, worst[g, a], best[g, a])))
            back.append((p, g, np.where(w, fi[g, a], ki[g, a]), a, np.where(w, best[g, a], worst[g, a])))
            O[q][g, ss] = np.where(w, np.where(bb + 1 == L, 0, bb + 1), bb)
            if t < RO - 1: X[q][g, :, ss] = np.maximum(X[q][g, :, ss] - WEAR, 0)
            now[q] = np.count_nonzero(w)
        for r, g, k, a, z in res + back: M[r][g, k, a] = z
        wins = now
    return {"ym": M.reshape(N, 128, L).astype(np.float32), "yown": O.astype(np.float32)}

@@ -1,0 +1,555 @@
+from concourse.bass import DstId, RemoteDMATransfer
+from concourse.mybir import AluOpType, ActivationFunctionType
+
+OP = AluOpType
+AF = ActivationFunctionType
+F32, BF, I32, U16 = "float32", "bfloat16", "int32", "uint16"
+BIG = float(2 ** 26)
+
+OWN_TILES = {
+    F32: "IC0:192 IC1:192 RC0:384 RC1:384 MR0:192 MR1:192 inA:192 inB:192 inM:192 inC:192 yo:192",
+    BF: "X:4288 ow:4288 FW:4288 ob:256 VI:3072 VR:3072 V2:3072 XI:3072 NI:3072 XR:3072 NR:3072 CZI:3072 CZR:3072 "
+        "CXI:3072 CXR:3072 CXB:3072 DA:3072 DB:3072 m01:1536 m512:1536 mB:1024 meq:2128 EQ:2128 EC:2128 CRc:192 mR:192",
+    I32: "nbw:4096 od:256 mi32:192 thi:1",
+    U16: "oR0:192 oI0:192",
+}
+POOLS = {
+    F32: "pf:1 pp1:1 p15:1 p16:1 cc:128 kk:256 c16:12 IDf:8/8 dA:256/96 B6:6/96 oneF:96/8 aC:24 Q1:256/96 Q23:512/96 "
+         "KI:1024/96 FI:1024/96 KR:768/96 FR:1024/96 FD:256/96 t16:16/96 kfl:48/96 dk:16/96 dw:16/96 "
+         "ZS:256/96 SXm:256/96 SW:24 sI:192 sR:192 du:12 f2:24 l1:24 l2:24 l3:24 fp:192 mRa:192 ZL:512/96 LX:512/96 thA:16/96 w4:64/96 "
+         "mk:192 s1:64/96 s2:64/96 zr:192 wc:1 wk:1/96 thD:8/8 thf:1/8 mb0:192 mb1:192",
+    BF: "BI1:8 BI2:8 BN1:8 BN2:8 ID:128 IDn:128 ID2:128 ID64:128 dW:192 LT:192 j64:256/1 j128:256/1 one1:128/1 oneB:96 HL:384 bf:192 bd:192 bs:192 "
+        "ZW:192 bx:192 ff:192 ZR:256/96 RX:256/96 FM:512/96 CN:512/96 ZK:512/96 KX:512/96 ZZ:1024/96 ZX:1024/96 ox:192 oy:192 ov:192 xg:192 "
+        "wf:192 wg:192 wb:1 V0:192",
+    I32: "pI:1 pJ:1 CiI:192 CiR:192 HL32:384 eD:16/96 fD:16/96 eI:48/96 e63:32/96 kc:48/96 n32:192 s3:64/96 s4:64/96 wi:1/96 wj:1/96 mw:192 mv:192 a32:192",
+    U16: "oI1:192 oR1:192 sL:12 nL:192 bU:192 Lb:12 LS:24 aU:192",
+}
+SCRATCH, SHAPE, PLACE = {}, {}, {}
+for _d, _names in OWN_TILES.items():
+    for _n in _names.split():
+        _n, _w = _n.split(":")
+        _p = 8 if _n == "thi" else 128
+        SCRATCH[_n] = ("sbuf", [_p, int(_w)], _d)
+        SHAPE[_n], PLACE[_n] = (_p, int(_w)), (_n, 0)
+for _d, _names in POOLS.items():
+    _at = 0
+    for _n in _names.split():
+        _n, _w = _n.split(":")
+        _w = (_w + "/128").split("/")
+        SHAPE[_n], PLACE[_n] = (int(_w[1]), int(_w[0])), ("pool_" + _d, _at)
+        _at += -(-int(_w[0]) // 16) * 16
+    SCRATCH["pool_" + _d] = ("sbuf", [128, _at], _d)
+SCRATCH["odr"] = ("dram", [8, 4096], BF)
+PSUM = ["b%d" % _i for _i in range(8)]
+for _n in PSUM:
+    SCRATCH[_n] = ("psum", [128, 512], F32)
+    SHAPE[_n], PLACE[_n] = (128, 512), (_n, 0)
+SEMAPHORES = ["qv", "qa", "qp", "qg"] + ["d%d" % i for i in range(16)] + ["rM", "rA", "rB", "rR", "rC"] + ["l%d" % i for i in range(5)]
+
+
+def rank_program(g, core, T, topo):
+    rank = T.rank_of(core)
+    if rank is None:
+        return
+    n_ranks = len(T.cores)
+    S = T.sem
+    queue = {"v": g.vector, "a": g.scalar, "p": g.tensor, "g": g, "s": g.sync}
+    count = {"v": 0, "a": 0, "p": 0, "g": 0}
+    known = {"v": {}, "a": {}, "p": {}, "g": {}, "s": {}}
+    snap = {}
+    log = {}
+    ndma = [0]
+
+    def R(name, lo=0, hi=None, step=1, p=None):
+        shape = SHAPE[name]
+        hi = shape[1] if hi is None else hi
+        p = shape[0] if p is None else p
+        buf, at = PLACE[name]
+        ap = T[buf][0:p, at + lo:at + hi:step] if step > 1 else T[buf][0:p, at + lo:at + hi]
+        return (ap, [(name, lo, hi)])
+
+    def A(name, lo=0, hi=None, step=1):
+        return R(name, lo, hi, step, 96)
+
+    def IND(win, lo, hi, off, c0, c1):
+        buf, at = PLACE[off]
+        return (T[win][:, lo:hi].indirect(T[buf][:, at + c0:at + c1]), [(win, lo, hi), (off, c0, c1)])
+
+    def learn(q, sem, val):
+        k = known[q]
+        for s2, v2 in snap.get((sem, val), {}).items():
+            k[s2] = max(k.get(s2, 0), v2)
+        k[sem] = max(k.get(sem, 0), val)
+
+    def need(q, reads, writes, skip_own=False):
+        deps = {}
+        for lst, wr in ((reads, False), (writes, True)):
+            for name, lo, hi in lst:
+                for e in log.get(name, ()):
+                    if name in PSUM and e[1] != q:
+                        hit = True
+                    else:
+                        hit = (wr or e[0]) and e[4] < hi and lo < e[5]
+                    if hit and not (skip_own and e[1] == q):
+                        deps[e[2]] = max(deps.get(e[2], 0), e[3])
+        for sem, val in sorted(deps.items(), key=lambda d: -len(snap.get(d, {}))):
+            if known[q].get(sem, 0) < val:
+                queue[q].wait_ge(S[sem], val)
+                learn(q, sem, val)
+
+    def note(q, sem, val, reads, writes):
+        for lst, wr in ((reads, False), (writes, True)):
+            for name, lo, hi in lst:
+                old = log.setdefault(name, [])
+                if wr:
+                    old[:] = [e for e in old if not (lo <= e[4] and e[5] <= hi)]
+                old.append([wr, q, sem, val, lo, hi])
+
+    def spans(refs):
+        return [s for r in refs for s in r[1]]
+
+    def emit(q, call, outs, ins, skip_own=False):
+        rd, wr = spans(ins), spans(outs)
+        need(q, rd, wr, skip_own)
+        count[q] += 1
+        sem = "q" + q
+        call().then_inc(S[sem], 1)
+        snap[(sem, count[q])] = dict(known[q])
+        note(q, sem, count[q], rd, wr)
+
+    def ind_out(o):
+        return (o[0], o[1][:1]), (o[0], o[1][1:])
+
+    def tt(o, a, b, op):
+        emit("v", lambda: g.vector.tensor_tensor(o[0], a[0], b[0], op), [o], [a, b])
+
+    def tt_scatter(o, a, b, op):
+        w, l = ind_out(o)
+        emit("v", lambda: g.vector.tensor_tensor(o[0], a[0], b[0], op), [w], [a, b, l])
+
+    def ts(o, a, s1, op0, s2=None, op1=None):
+        sc1 = s1[0] if isinstance(s1, tuple) else s1
+        ins = [a] + ([s1] if isinstance(s1, tuple) else [])
+        if op1 is None:
+            emit("v", lambda: g.vector.tensor_scalar(o[0], a[0], sc1, None, op0), [o], ins)
+        else:
+            emit("v", lambda: g.vector.tensor_scalar(o[0], a[0], sc1, s2, op0, op1), [o], ins)
+
+    def cp(o, a):
+        emit("v", lambda: g.vector.tensor_copy(o[0], a[0]), [o], [a])
+
+    def cp_scatter(o, a):
+        w, l = ind_out(o)
+        emit("v", lambda: g.vector.tensor_copy(o[0], a[0]), [w], [a, l])
+
+    def ms(o, c):
+        emit("v", lambda: g.vector.memset(o[0], c), [o], [])
+
+    def scan(o, d0, d1, op0, op1):
+        emit("v", lambda: g.vector.tensor_tensor_scan(o[0], d0[0], d1[0], 0.0, op0, op1), [o], [d0, d1])
+
+    def act(o, a, func=AF.Copy, bias=0.0, scale=1.0, acc=None):
+        ins = [a] + ([scale] if isinstance(scale, tuple) else [])
+        sc = scale[0] if isinstance(scale, tuple) else scale
+        if acc is None:
+            emit("a", lambda: g.scalar.activation(o[0], a[0], func, bias=bias, scale=sc), [o], ins)
+        else:
+            emit("a", lambda: g.scalar.activation(o[0], a[0], func, bias=bias, scale=sc, accum_out=acc[0]), [o, acc], ins)
+
+    def mm(o, l, r, start=True, stop=True):
+        emit("p", lambda: g.tensor.matmul(o[0], l[0], r[0], start, stop), [o], [l, r], True)
+
+    def iota(o, pat, base=0, cm=0, flag=True):
+        kw = {"allow_small_or_imprecise_dtypes": True} if flag else {}
+        emit("g", lambda: g.iota(o[0], pat, base, cm, **kw), [o], [])
+
+    def dma(q, pairs):
+        rd, wr = spans([b for a, b in pairs]), spans([a for a, b in pairs])
+        need(q, rd, wr)
+        sem = "d%d" % ndma[0]
+        ndma[0] += 1
+        for a, b in pairs:
+            queue[q].dma_start(a[0], b[0]).then_inc(S[sem], 16)
+        snap[(sem, 16 * len(pairs))] = dict(known[q])
+        note("dma", sem, 16 * len(pairs), rd, wr)
+
+    def ext(t):
+        return (t[:], [])
+
+    nloc = [0]
+    loc_done = []
+
+    def send(src, outs):
+        need("g", [(src, 0, 192)], [])
+        ls = "l%d" % nloc[0]
+        nloc[0] += 1
+        total = 0
+        tr = []
+        for i, (d, land, rs) in enumerate(outs):
+            dst = T.cores[d]
+            rid, pid, _ = topo.addr(dst)
+            es = topo.engines(core, dst)
+            m = len(es) // len(outs)
+            es = es[i * m:(i + 1) * m]
+            total += m
+            tr.append((rid, pid, sum(1 << e for e in es), land, rs))
+        if len(tr) == 1:
+            rid, pid, mask, land, rs = tr[0]
+            g.remote_dma(T[land][:], T[src][:], S[rs], S[ls], pid, rid, mask)
+        else:
+            g.remote_dma_fused([RemoteDMATransfer(dst_ids=[DstId(rid=rid, pnc=pid)], dma_engine_mask=mask, remote_sem=S[rs],
+                                                  src=T[src][:], dst=T[land][:]) for rid, pid, mask, land, rs in tr], local_sem=S[ls])
+        snap[(ls, total)] = dict(known["g"])
+        note("rem", ls, total, [(src, 0, 192)], [])
+        loc_done.append((ls, total))
+
+    def landed(land, sem, val):
+        note("rem", sem, val, [], [(land, 0, 192)])
+
+    up1, up2 = (rank + 1) % n_ranks, (rank + 2) % n_ranks
+    dn1, dn2 = (rank - 1) % n_ranks, (rank - 2) % n_ranks
+    n16 = len(topo.engines(core, T.cores[up1]))
+    H = (0, 1)
+
+    dma("s", [(R("mi32"), ext(T.m0))])
+    dma("s", [(R("X", 0, 4096), ext(T.x0))])
+    dma("a", [(R("od"), ext(T.own0))])
+    dma("a", [(R("thi"), ext(T.th))])
+    dma("s", [(R("nbw"), ext(T.nb))])
+    iota(R("pI"), [[0, 1]], 0, 1, False)
+    iota(R("kk"), [[0, 16], [1, 16]])
+    iota(R("cc"), [[1, 128]])
+    iota(R("c16"), [[16, 12]])
+    iota(R("a32"), [[1, 192]], 0, 0, False)
+    ms(R("m01"), 1.0)
+    ms(R("m01", 0, 1536, 16), 0.0)
+    ms(R("m512"), 0.0)
+    ms(R("m512", 0, 1536, 16), 512.0)
+    for h in H:
+        act(R("CZI", 1536 * h, 1536 * h + 1536), R("m01"), AF.Copy, 0.0, 0.0)
+    cp(R("oR0"), R("mi32"))
+    send("oR0", [(up1, "oI0", "rM")])
+    landed("oI0", "rM", n16)
+    for name, c in (("CZR", 0), ("EQ", 0), ("meq", 1), ("ZR", 0), ("ZL", 0), ("ZK", 0), ("RC0", 0), ("RC1", 0)):
+        iota(R(name), [[0, SHAPE[name][1]]], c)
+    iota(R("FW", 0, 4096), [[0, 4096]], 1)
+    iota(R("FW", 4096, 4288), [[0, 192]], 0)
+    ts(R("pJ"), R("pI"), 15, OP.bitwise_and)
+    cp(R("p15"), R("pJ"))
+    cp(R("pf"), R("pI"))
+    ts(R("pJ"), R("pI"), 4, OP.arith_shift_right)
+    cp(R("p16"), R("pJ"))
+    ts(R("ID"), R("cc"), R("pf"), OP.is_equal)
+    for name, c in (("BI1", 1024.0), ("BI2", 2048.0), ("BN1", -1024.0), ("BN2", -2048.0)):
+        ts(R(name), R("cc", 0, 8), R("p16"), OP.is_equal, c, OP.mult)
+    for name, c in (("IDn", -1.0), ("ID2", 2.0), ("ID64", 64.0)):
+        ts(R(name), R("ID"), c, OP.mult)
+    ms(R("one1"), 1.0)
+    ts(R("j64"), R("kk", 0, 256, 1, 1), 64.0, OP.mult)
+    ts(R("j128"), R("kk", 0, 256, 1, 1), 128.0, OP.mult)
+    ms(R("mB"), 0.0)
+    ms(R("mB", 0, 1024, 16), BIG)
+    ms(R("ZS"), 0.0)
+    ts(R("dA"), A("kk"), R("p15", p=96), OP.is_equal)
+    ts(R("B6"), A("cc", 0, 6), R("p16", p=96), OP.is_equal)
+    cp(R("ob"), R("od"))
+    dma("s", [((T.odr[:], [("odr", 0, 4096)]), R("ob"))])
+    dma("s", [((T.ow[r:128:16, 0:4096], [("ow", 0, 4096)]), (T.odr[:], [("odr", 0, 4096)])) for r in range(16)])
+    ts(R("IDf"), R("cc", 0, 8, 1, 8), R("pf", p=8), OP.is_equal)
+    ts(R("dW"), R("kk", 0, 192), R("p15"), OP.is_equal)
+    ts(R("LT"), R("kk", 0, 192), R("p15"), OP.is_ge, 1000.0, OP.mult)
+    ms(R("ZW"), 0.0)
+    ms(R("ZZ"), 0.0)
+    cp(R("aU"), R("a32"))
+    ts(R("aC", 0, 12), R("c16"), R("p15"), OP.add, 4096.0, OP.add)
+    ts(R("aC", 12, 24), R("c16"), R("p15"), OP.add, 192.0, OP.add)
+    ts(R("pp1"), R("p15"), 1.0, OP.add)
+
+    def thresholds():
+        ms(R("oneF"), 1.0)
+        cp(R("thf"), R("thi"))
+        ts(R("thD"), R("IDf"), R("thf"), OP.mult)
+        mm(R("b6", 0, 8, 1, 96), R("oneF"), R("thD"))
+        for h in H:
+            ts(R("thA", 8 * h, 8 * h + 8), A("b6", 0, 8), 1024.0, OP.mult)
+
+    def late_constants():
+        ms(R("X", 4096, 4288), 0.0)
+        ms(R("ow", 4096, 4288), 0.0)
+        ms(R("oneB"), 1.0)
+        cp(R("mb0"), R("mi32"))
+
+    def half(name, h, step=1):
+        return R(name, 1536 * h, 1536 * h + 1536, step)
+
+    def gather(v, off, h):
+        act(half(v, h), IND("X", 0, 4096, off, 96 * h, 96 * h + 96))
+
+    def begin(bank):
+        mm(A(bank, 0, 256), R("one1", 0, 96), R("j64"), True, False)
+
+    def group_sum(bank, src, w, h, stop=False):
+        for k in range(16):
+            mm(A(bank, 128 * h + k, 128 * h + 128, 16), R(src, 1536 * h + k, 1536 * h + 1536, 16), R(w), False, stop and k == 15)
+
+    def digits(bank, at, i, h, w, start=False, stop=False):
+        mm(A(bank, at + 128 * h, at + 128 * h + 128), R("HL", 192 * i + 96 * h, 192 * i + 96 * h + 96), R(w), start, stop)
+
+    def split(m32):
+        ts(R("HL32", 0, 192), R(m32), 6, OP.arith_shift_right)
+        ts(R("HL32", 192, 384), R(m32), 63, OP.bitwise_and)
+        cp(R("HL"), R("HL32"))
+
+    def payload(wide):
+        for h in H:
+            digits("b2", 0, 1, h, "ID", True, False)
+            digits("b2", 0, 0, h, "IDn", False, True)
+        act(R("Q1"), A("b2", 0, 256))
+        for i in range(2 if wide else 1):
+            mm(A("b4", 256 * i, 256 * i + 256), R("one1", 0, 96), R("j128"), True, False)
+            for h in H:
+                digits("b4", 256 * i, 0, h, "ID" if i else "ID2", False, h == 1 and not i)
+                if i:
+                    digits("b4", 256 * i, 1, h, "ID", False, h == 1)
+        n = 512 if wide else 256
+        act(R("Q23", 0, n), A("b4", 0, n))
+
+    def extremes(v, mx, mn, h):
+        scan(half(mx, h), R("m01"), half(v, h), OP.mult, OP.max)
+        scan(half(mn, h), R("m512"), half(v, h), OP.add, OP.min)
+
+    def centres(mx, mn, s, ci, cz):
+        tt(R(s), R(mx, 15, 3072, 16), R(mn, 15, 3072, 16), OP.add)
+        ts(R(ci), R(s), 0.5, OP.mult, -0.25, OP.add)
+        cp(R(cz, 0, 3072, 16), R(ci))
+
+    def spread(cx, cz, h):
+        scan(half(cx, h), R("m01"), half(cz, h), OP.mult, OP.add)
+
+    def larger(v, first, cx, c0, d, h):
+        tt(half(v, h, 16), first, half(c0, h, 16), OP.max)
+        scan(half(d, h), half(cx, h), half(v, h), OP.min, OP.max)
+
+    def seg(f, lo, hi):
+        return A(f, lo + 15, hi, 16)
+
+    def play(t):
+        oI, oR, mb = "oI%d" % t, "oR%d" % t, "mb%d" % t
+        IC, RC, MR = "IC%d" % t, "RC%d" % t, "MR%d" % t
+        last = t == 1
+        m96 = R("m01", 0, 256, 1, 96)
+        m96x2 = R("m01", 0, 512, 1, 96)
+        mB1 = A("mB", 0, 256)
+        if t == 0:
+            thresholds()
+            cp(R("mw"), R(oI))
+        gather("VI", oI, 0)
+        act(R("VI", 1536, 2304), IND("X", 0, 4096, oI, 96, 144))
+        cp(R("VI", 2304, 3072), IND("X", 0, 4096, oI, 144, 192))
+        split("mw")
+        for h in H:
+            extremes("VI", "XI", "NI", h)
+        begin("b0")
+        for h in H:
+            digits("b0", 0, 0, h, "ID")
+        payload(False)
+        gather("VR", oR, 0)
+        for h in H:
+            group_sum("b0", "VI", "BN1", h)
+        gather("VR", oR, 1)
+        centres("XI", "NI", "sI", "CiI", "CZI")
+        for h in H:
+            spread("CXI", "CZI", h)
+            larger("VI", half("VI", h, 16), "CXI", "CZI", "DA", h)
+            group_sum("b0", "DA", "BI2", h, h == 1)
+        extremes("VR", "XR", "NR", 0)
+        u, a0 = A("b3", 0, 256), A("b0", 0, 256)
+        scan(R("FI", 0, 256), mB1, a0, OP.add, OP.min)
+        tt(R("KI", 0, 256), a0, R("Q1"), OP.add)
+        scan(R("FI", 256, 512), mB1, R("KI", 0, 256), OP.add, OP.min)
+        cp(R("eI", 0, 32), seg("FI", 0, 512))
+        ts(R("e63"), R("eI", 0, 32), 63, OP.bitwise_and)
+        tt(R("KI", 512, 768), R("Q23", 0, 256), a0, OP.subtract)
+        ts(R("t16"), R("e63", 0, 16), 64.0, OP.mult)
+        tt(R("ZS", 0, 256, 16), R("t16"), R("e63", 16, 32), OP.add)
+        scan(u, m96, R("ZS"), OP.mult, OP.add)
+        tt(R("SXm"), u, R("dA"), OP.mult)
+        for h in H:
+            mm(R("b7", 6 * h, 6 * h + 6), R("SXm", 128 * h, 128 * h + 128), R("B6"))
+        cp(R("sL"), R("b7", 0, 12))
+        begin("b5")
+        for h in H:
+            group_sum("b5", "VR", "BI1", h)
+        cp(R("nL"), IND("nbw", 0, 4096, "sL", 0, 12))
+        act(R("SW", 0, 12), R("b7", 0, 12))
+        for h in H:
+            gather("V2", "nL", h)
+            act(R("V0", 96 * h, 96 * h + 96), half("V2", h, 16))
+        cp(R("bf"), IND("ow", 0, 4096, "sL", 0, 12))
+        cp(R("bU"), R("bf"))
+        mm(R("b6", 0, 192), R("ID"), R("bf"), True, False)
+        mm(R("b6", 0, 192), R("ID"), R("LT"), False, True)
+        extremes("VR", "XR", "NR", 1)
+        centres("XR", "NR", "sR", "CiR", "CZR")
+        cp(R("CRc"), R("CiR"))
+        for h in H:
+            act(half("CXB", h), IND("CRc", 0, 192, "bU", 96 * h, 96 * h + 96))
+        cp(R("n32"), R("nL"))
+        split("n32")
+        for bank in ("b0", "b1"):
+            begin(bank)
+            for h in H:
+                digits(bank, 0, 0, h, "ID")
+        for h in H:
+            for bank in ("b0", "b1"):
+                group_sum(bank, "V2", "BN1", h)
+        scan(R("FI", 512, 768), mB1, R("KI", 512, 768), OP.add, OP.min)
+        payload(True)
+        act(half("CXR", 1), IND("CRc", 0, 192, "aU", 96, 192))
+        cp(R("eI", 32, 48), seg("FI", 512, 768))
+        ts(R("kc"), R("eI"), 6, OP.arith_shift_right, 15, OP.bitwise_and)
+        cp(R("kfl"), R("kc"))
+        tt(R("dk"), R("kfl", 32, 48), R("kfl", 0, 16), OP.subtract)
+        if t == 0:
+            ms(R("meq", 0, 1936, 176), 0.0)
+            ms(R("meq", 1936, 2128, 16), 0.0)
+        tt(R("bd"), R("bf"), R("dW"), OP.mult)
+        scan(R("bs"), R("m01", 0, 192), R("bd"), OP.mult, OP.add)
+        cp(R("SW", 12, 24), R("bs", 15, 192, 16))
+        cp(R("ZW", 0, 192, 16), R("bs", 15, 192, 16))
+        cp(R("Lb"), R("SW", 12, 24))
+        for c in range(1, 12):
+            e = 176 * c
+            ts(R("EQ", e - 16 * c, e), R("bf", 0, 16 * c), R("SW", 12 + c, 13 + c), OP.is_equal)
+        scan(R("bx"), R("m01", 0, 192), R("ZW"), OP.mult, OP.add)
+        tt(R("EQ", 1936, 2128), R("b6", 0, 192), R("bx"), OP.is_equal)
+        scan(R("EC"), R("meq"), R("EQ"), OP.mult, OP.add)
+        cp(R("du"), R("EC", 1951, 2128, 16))
+        tt(R("du", 1, 12), R("du", 1, 12), R("EC", 175, 1936, 176), OP.add)
+        ts(R("f2", 0, 12), R("du"), 0.0, OP.is_equal)
+        ts(R("f2", 12, 24), R("du"), 0.0, OP.is_equal)
+        tt(R("l1"), R("SW"), R("aC"), OP.subtract)
+        tt(R("l2"), R("l1"), R("f2"), OP.mult)
+        tt(R("l3"), R("l2"), R("aC"), OP.add)
+        cp(R("LS"), R("l3"))
+        for h in H:
+            larger("V2", R("V0", 96 * h, 96 * h + 96), "CXI", "CZI", "DA", h)
+            group_sum("b0", "DA", "BI2", h, h == 1)
+        act(R("ff"), IND("FW", 0, 4288, "LS", 0, 12))
+        act(R("fp"), R("ff"), AF.Identity, -1.0, R("pp1"))
+        if not last:
+            act(R("xg"), IND("X", 0, 4096, "sL", 0, 12), AF.Relu, -16.0)
+        for h in H:
+            larger("V2", R("V0", 96 * h, 96 * h + 96), "CXB", "CXB", "DB", h)
+            group_sum("b1", "DB", "BI2", h, h == 1)
+        for i, cz in ((0, "CZI"), (1, "CXB")):
+            for h in H:
+                mm(A("b7", 16 + 16 * i + 8 * h, 24 + 16 * i + 8 * h), half(cz, h, 16), R("BI1"))
+        if t == 0:
+            late_constants()
+        spread("CXR", "CZR", 0)
+        for h in H:
+            larger("VR", half("VR", h, 16), "CXR", "CZR", "DA", h)
+            group_sum("b5", "DA", "BN2", h, h == 1)
+        ui, ur = a0, A("b1", 0, 256)
+        q1, q2, q3 = R("Q1"), R("Q23", 0, 256), R("Q23", 256, 512)
+        scan(R("FI", 0, 256), mB1, ui, OP.add, OP.min)
+        tt(R("KI", 256, 512), q2, ui, OP.subtract)
+        tt(R("KI", 512, 768), ui, q1, OP.add)
+        tt(R("KI", 768, 1024), q3, ui, OP.subtract)
+        scan(R("FI", 256, 1024), A("mB", 256, 1024), R("KI", 256, 1024), OP.add, OP.min)
+        if not last:
+            cp_scatter(IND("X", 0, 4288, "LS", 0, 12), R("xg"))
+        for i in (0, 1):
+            tt(R("ZL", 256 * i, 256 * i + 256, 16), A("b7", 16 + 16 * i, 32 + 16 * i), R("thA"), OP.add)
+        scan(R("LX"), m96x2, R("ZL"), OP.mult, OP.add)
+        tt(R("FM", 0, 256), ui, R("LX", 0, 256), OP.is_lt)
+        tt(R("FM", 256, 512), ur, R("LX", 256, 512), OP.is_lt)
+        scan(R("CN"), m96x2, R("FM"), OP.mult, OP.add)
+        tt(R("w4", 0, 16), seg("CN", 0, 256), seg("CN", 256, 512), OP.is_gt)
+        for i in (1, 2, 3):
+            act(R("w4", 16 * i, 16 * i + 16), R("w4", 0, 16))
+        act(R("ZK", 256, 512, 16), R("w4", 0, 16))
+        tt(R("dw"), R("dk"), R("w4", 0, 16), OP.mult)
+        tt(R("ZK", 0, 256, 16), R("dw"), R("kfl", 0, 16), OP.add)
+        tt(R("KR", 0, 256), q2, ur, OP.subtract)
+        scan(R("FR", 256, 512), mB1, ur, OP.add, OP.min)
+        scan(R("KX"), m96x2, R("ZK"), OP.mult, OP.add)
+        tt(R("KR", 256, 512), q3, ur, OP.subtract)
+        tt(R("KR", 512, 768), ur, q1, OP.add)
+        scan(R("FR", 0, 256), mB1, R("KR", 0, 256), OP.add, OP.min)
+        scan(R("FR", 512, 1024), A("mB", 0, 512), R("KR", 256, 768), OP.add, OP.min)
+        scan(R("FD"), mB1, A("b5", 0, 256), OP.add, OP.min)
+        cp(R("eD"), seg("FD", 0, 256))
+        ts(R("fD"), R("eD"), 6, OP.arith_shift_right, 15, OP.bitwise_and)
+        cp(R("ZR", 0, 256, 16), R("fD"))
+        scan(R("RX"), m96, R("ZR"), OP.mult, OP.add)
+        for h in H:
+            mm(R("b6", 96 * h, 96 * h + 96), R("RX", 128 * h, 128 * h + 128), R("ID", 0, 96, 1, 96))
+        ts(R("mR"), R("b6", 0, 192), R("p15"), OP.is_equal)
+        act(R("mRa"), IND("mR", 0, 192, "Lb", 0, 12))
+        for i in range(4):
+            mm(R("b6", 96 * i, 96 * i + 96), R("KX", 128 * i, 128 * i + 128), R("ID", 0, 96, 1, 96))
+        tt(R("s1"), seg("FI", 0, 1024), seg("FR", 0, 1024), OP.subtract)
+        tt(R("s2"), R("s1"), R("w4"), OP.mult)
+        tt(R("s3"), R("s2"), seg("FR", 0, 1024), OP.add)
+        ts(R("s4"), R("s3"), 63, OP.bitwise_and)
+        ts(R("ZZ", 0, 512, 16), R("s4", 0, 32), 128.0, OP.add)
+        cp(R("ZZ", 512, 1024, 16), R("s4", 32, 64))
+        for i, bank in ((0, "b5"), (1, "b4")) if last else ((1, "b4"), (0, "b5")):
+            for d in (0, 512):
+                scan(R("ZX", d + 256 * i, d + 256 * i + 256), m96, R("ZZ", d + 256 * i, d + 256 * i + 256), OP.mult, OP.add)
+            for h in H:
+                for d, w in ((0, "ID64"), (512, "ID")):
+                    mm(R(bank, 96 * h, 96 * h + 96), R("ZX", d + 256 * i + 128 * h, d + 256 * i + 128 * h + 128), R(w, 0, 96, 1, 96), d == 0, d > 0)
+        tt(R("ox"), R("bf"), R("b6", 192, 384), OP.add)
+        ts(R("oy"), R("ox"), 192.0, OP.is_lt)
+        tt(R("ov"), R("ox"), R("oy"), OP.mult)
+        act(R("zr"), R("b4", 0, 192), AF.Identity, -4096.0)
+        tt(R("mk"), R("b6", 0, 192), R("fp"), OP.is_equal)
+        tt(R(IC), R("b5", 0, 192), R("mk"), OP.mult)
+        if not last:
+            send(IC, [(dn1, "inA", "rA"), (up1, "inB", "rB")])
+        else:
+            send(IC, [(dn2, "inC", "rC")])
+        tt_scatter(IND(RC, 0, 384, "LS", 12, 24), R("zr"), R("mRa"), OP.mult)
+        tt(R(MR), R(RC, 0, 192), R(mb), OP.max)
+        if not last:
+            send(MR, [(up2, "inM", "rR")])
+        cp_scatter(IND("ow", 0, 4288, "LS", 0, 12), R("ov"))
+        if last:
+            dma("g", [((T.yown[:], []), (T.ow[0:128:16, 0:4096], [("ow", 0, 4096)]))])
+            return
+        tt(R("wf"), R("b6", 192, 384), R("ff"), OP.mult)
+        act(R("wg"), R("wf"), acc=R("wc"))
+        act(R("wb"), R("wc"))
+        mm(A("b7", 48, 49), R("oneB"), R("wb"))
+        ts(R("wi"), A("b7", 48, 49), 0.0625, OP.mult)
+        ts(R("wj"), R("wi"), 63, OP.bitwise_and)
+        ts(R("wk"), R("wj"), 1024.0, OP.mult)
+
+    def merged(old, new, words):
+        tt(R("mv"), R(old), R(new), OP.max)
+        ts(R(words), R("mv"), 4095, OP.bitwise_and)
+
+    play(0)
+    landed("inA", "rA", n16 // 2)
+    landed("inB", "rB", n16 // 2)
+    landed("inM", "rR", n16)
+    merged("MR0", "inA", "mi32")
+    cp(R("oR1"), R("mi32"))
+    merged("inM", "inB", "mw")
+    cp(R("oI1"), R("mw"))
+    cp(R("mb1"), R("mi32"))
+    ts(R("thA"), R("thA"), R("wk"), OP.add)
+    play(1)
+    landed("inC", "rC", n16)
+    merged("MR1", "inC", "mi32")
+    cp(R("yo"), R("mi32"))
+    dma("s", [((T.ym[:], []), R("yo"))])
+    for q in ("v", "a", "p", "g"):
+        g.wait_ge(S["q" + q], count[q])
+    for sem, val in loc_done:
+        g.wait_ge(S[sem], val)
+    g.wait_ge(S["d%d" % (ndma[0] - 2)], 16)
+    g.sync.wait_ge(S["d%d" % (ndma[0] - 1)], 16)

@@ -3,34 +3,34 @@ from concourse.mybir import AluOpType, ActivationFunctionType
 
 OP = AluOpType
 AF = ActivationFunctionType
-F32, BF, I32, U16 = "float32", "bfloat16", "int32", "uint16"
+F32, BF, I32, U16, F16 = "float32", "bfloat16", "int32", "uint16", "float16"
 BIG = float(2 ** 26)
+KILL = float(2 ** 18)
+R1, R32, R4096 = 1.5 * 2 ** 23, 1.5 * 2 ** 28, 1.5 * 2 ** 35
+MID = 2047.5
 
 OWN_TILES = {
-    F32: "IC0:192 IC1:192 RC0:384 RC1:384 MR0:192 MR1:192 inA:192 inB:192 inM:192 inC:192 yo:192",
-    BF: "X:4288 ow:4288 FW:4288 ob:256 VI:3072 VR:3072 V2:3072 XI:3072 NI:3072 XR:3072 NR:3072 CZI:3072 CZR:3072 "
-        "CXI:3072 CXR:3072 CXB:3072 DA:3072 DB:3072 m01:1536 m512:1536 mB:1024 meq:2128 EQ:2128 EC:2128 CRc:192 mR:192",
-    I32: "nbw:4096 od:256 mi32:192 thi:1",
+    F32: "ow:4288 IC0:192 IC1:192 MR0:384 MR1:384 inA:192 inB:192 inM:192 inC:192 yo:192 ob:256",
+    BF: "X:4288 VI:3072 VR:3072 V2:3072 XI:3072 NI:3072 XR:3072 NR:3072 CXI:3072 CXR:3072 DA:3072 DR:3072 D2:3072 DB:3072 "
+        "CZ:768 m01:768 m512:768 FK:2048 LO:2048 EX:1536 EQ:2304 QR:192",
+    I32: "nbw:4096 od:256 mi32:192 thi:8",
     U16: "oR0:192 oI0:192",
 }
 POOLS = {
-    F32: "pf:1 pp1:1 p15:1 p16:1 cc:128 kk:256 c16:12 IDf:8/8 dA:256/96 B6:6/96 oneF:96/8 aC:24 Q1:256/96 Q23:512/96 "
-         "KI:1024/96 FI:1024/96 KR:768/96 FR:1024/96 FD:256/96 t16:16/96 kfl:48/96 dk:16/96 dw:16/96 "
-         "ZS:256/96 SXm:256/96 SW:24 sI:192 sR:192 du:12 f2:24 l1:24 l2:24 l3:24 fp:192 mRa:192 ZL:512/96 LX:512/96 thA:16/96 w4:64/96 "
-         "mk:192 s1:64/96 s2:64/96 zr:192 wc:1 wk:1/96 thD:8/8 thf:1/8 mb0:192 mb1:192",
-    BF: "BI1:8 BI2:8 BN1:8 BN2:8 ID:128 IDn:128 ID2:128 ID64:128 dW:192 LT:192 j64:256/1 j128:256/1 one1:128/1 oneB:96 HL:384 bf:192 bd:192 bs:192 "
-        "ZW:192 bx:192 ff:192 ZR:256/96 RX:256/96 FM:512/96 CN:512/96 ZK:512/96 KX:512/96 ZZ:1024/96 ZX:1024/96 ox:192 oy:192 ov:192 xg:192 "
-        "wf:192 wg:192 wb:1 V0:192",
-    I32: "pI:1 pJ:1 CiI:192 CiR:192 HL32:384 eD:16/96 fD:16/96 eI:48/96 e63:32/96 kc:48/96 n32:192 s3:64/96 s4:64/96 wi:1/96 wj:1/96 mw:192 mv:192 a32:192",
-    U16: "oI1:192 oR1:192 sL:12 nL:192 bU:192 Lb:12 LS:24 aU:192",
+    F32: "p15:1 e0:1 e192:1 eB:1 cc:16 aC:24 EQm:16 LTm:16 IDf:128 FS:768 FK1:576 rr:48 SW:24 l1:24 Mg:192 zr:192 xa:192 ya:192 wc:1 lim0:1 lim:1",
+    BF: "ONE:128 BLK:128 BK8:128 ID:128 IDh:128 I13:128 IDk:128 IDn:128 W64:144 W32:144 Wm:144 W1:144 W8:144 mB:192 mD:192 "
+        "krow:192/1 kap:128/1 kan:128/1 cq:128/1 cm:128/1 ch:128/1 cI:128/1 cR:128/1 one:192/1 zrow:128/1 "
+        "UU:36 VV:36 SS:36 PP:36 RR:36 kR:12 won:12 b0:192 bf:192 cnt:384 Cb:192 CT:256 QG:192 QK:192 FM:384 CN:384 wf:192 wb:1 xg:192",
+    F16: "M16:192 n16:192 S0:192 S1:192 th16:1",
+    I32: "pI:1 pJ:1 wi:1 wj:1 mw:192 mv:192",
+    U16: "oI1:192 oR1:192 sL:12 nL:192 Lb:12 Lc:12 LS:24",
 }
 SCRATCH, SHAPE, PLACE = {}, {}, {}
 for _d, _names in OWN_TILES.items():
     for _n in _names.split():
         _n, _w = _n.split(":")
-        _p = 8 if _n == "thi" else 128
-        SCRATCH[_n] = ("sbuf", [_p, int(_w)], _d)
-        SHAPE[_n], PLACE[_n] = (_p, int(_w)), (_n, 0)
+        SCRATCH[_n] = ("sbuf", [128, int(_w)], _d)
+        SHAPE[_n], PLACE[_n] = (128, int(_w)), (_n, 0)
 for _d, _names in POOLS.items():
     _at = 0
     for _n in _names.split():
@@ -39,12 +39,11 @@ for _d, _names in POOLS.items():
         SHAPE[_n], PLACE[_n] = (int(_w[1]), int(_w[0])), ("pool_" + _d, _at)
         _at += -(-int(_w[0]) // 16) * 16
     SCRATCH["pool_" + _d] = ("sbuf", [128, _at], _d)
-SCRATCH["odr"] = ("dram", [8, 4096], BF)
-PSUM = ["b%d" % _i for _i in range(8)]
+PSUM = ["b%d_" % _i for _i in range(8)]
 for _n in PSUM:
     SCRATCH[_n] = ("psum", [128, 512], F32)
     SHAPE[_n], PLACE[_n] = (128, 512), (_n, 0)
-SEMAPHORES = ["qv", "qa", "qp", "qg"] + ["d%d" % i for i in range(16)] + ["rM", "rA", "rB", "rR", "rC"] + ["l%d" % i for i in range(5)]
+SEMAPHORES = ["qv", "qa", "qp", "qg"] + ["d%d" % i for i in range(8)] + ["rM", "rA", "rB", "rR", "rC"] + ["l%d" % i for i in range(4)]
 
 
 def rank_program(g, core, T, topo):
@@ -59,6 +58,7 @@ def rank_program(g, core, T, topo):
     snap = {}
     log = {}
     ndma = [0]
+    B0, B1, B2, B3, B4, B5, B6, B7 = PSUM
 
     def R(name, lo=0, hi=None, step=1, p=None):
         shape = SHAPE[name]
@@ -67,9 +67,6 @@ def rank_program(g, core, T, topo):
         buf, at = PLACE[name]
         ap = T[buf][0:p, at + lo:at + hi:step] if step > 1 else T[buf][0:p, at + lo:at + hi]
         return (ap, [(name, lo, hi)])
-
-    def A(name, lo=0, hi=None, step=1):
-        return R(name, lo, hi, step, 96)
 
     def IND(win, lo, hi, off, c0, c1):
         buf, at = PLACE[off]
@@ -106,7 +103,10 @@ def rank_program(g, core, T, topo):
                 old.append([wr, q, sem, val, lo, hi])
 
     def spans(refs):
-        return [s for r in refs for s in r[1]]
+        return [s for r in refs if isinstance(r, tuple) for s in r[1]]
+
+    def ap(x):
+        return x[0] if isinstance(x, tuple) else x
 
     def emit(q, call, outs, ins, skip_own=False):
         rd, wr = spans(ins), spans(outs)
@@ -128,12 +128,10 @@ def rank_program(g, core, T, topo):
         emit("v", lambda: g.vector.tensor_tensor(o[0], a[0], b[0], op), [w], [a, b, l])
 
     def ts(o, a, s1, op0, s2=None, op1=None):
-        sc1 = s1[0] if isinstance(s1, tuple) else s1
-        ins = [a] + ([s1] if isinstance(s1, tuple) else [])
         if op1 is None:
-            emit("v", lambda: g.vector.tensor_scalar(o[0], a[0], sc1, None, op0), [o], ins)
+            emit("v", lambda: g.vector.tensor_scalar(o[0], a[0], ap(s1), None, op0), [o], [a, s1])
         else:
-            emit("v", lambda: g.vector.tensor_scalar(o[0], a[0], sc1, s2, op0, op1), [o], ins)
+            emit("v", lambda: g.vector.tensor_scalar(o[0], a[0], ap(s1), ap(s2), op0, op1), [o], [a, s1, s2])
 
     def cp(o, a):
         emit("v", lambda: g.vector.tensor_copy(o[0], a[0]), [o], [a])
@@ -149,29 +147,29 @@ def rank_program(g, core, T, topo):
         emit("v", lambda: g.vector.tensor_tensor_scan(o[0], d0[0], d1[0], 0.0, op0, op1), [o], [d0, d1])
 
     def act(o, a, func=AF.Copy, bias=0.0, scale=1.0, acc=None):
-        ins = [a] + ([scale] if isinstance(scale, tuple) else [])
-        sc = scale[0] if isinstance(scale, tuple) else scale
         if acc is None:
-            emit("a", lambda: g.scalar.activation(o[0], a[0], func, bias=bias, scale=sc), [o], ins)
+            emit("a", lambda: g.scalar.activation(o[0], a[0], func, bias=ap(bias), scale=ap(scale)), [o], [a, bias, scale])
         else:
-            emit("a", lambda: g.scalar.activation(o[0], a[0], func, bias=bias, scale=sc, accum_out=acc[0]), [o, acc], ins)
+            emit("a", lambda: g.scalar.activation(o[0], a[0], func, bias=ap(bias), scale=ap(scale), accum_out=acc[0]), [o, acc], [a, bias, scale])
 
-    def mm(o, l, r, start=True, stop=True):
+    def mm(o, l, r, start=False, stop=False):
         emit("p", lambda: g.tensor.matmul(o[0], l[0], r[0], start, stop), [o], [l, r], True)
 
     def iota(o, pat, base=0, cm=0, flag=True):
         kw = {"allow_small_or_imprecise_dtypes": True} if flag else {}
         emit("g", lambda: g.iota(o[0], pat, base, cm, **kw), [o], [])
 
-    def dma(q, pairs):
-        rd, wr = spans([b for a, b in pairs]), spans([a for a, b in pairs])
+    def select(o, a, pat, op, base, cm):
+        emit("g", lambda: g.affine_select(o[0], a[0], pat, op, 0.0, base, cm), [o], [a])
+
+    def dma(q, a, b):
+        rd, wr = spans([b]), spans([a])
         need(q, rd, wr)
         sem = "d%d" % ndma[0]
         ndma[0] += 1
-        for a, b in pairs:
-            queue[q].dma_start(a[0], b[0]).then_inc(S[sem], 16)
-        snap[(sem, 16 * len(pairs))] = dict(known[q])
-        note("dma", sem, 16 * len(pairs), rd, wr)
+        queue[q].dma_start(a[0], b[0]).then_inc(S[sem], 16)
+        snap[(sem, 16)] = dict(known[q])
+        note("dma", sem, 16, rd, wr)
 
     def ext(t):
         return (t[:], [])
@@ -195,10 +193,10 @@ def rank_program(g, core, T, topo):
             tr.append((rid, pid, sum(1 << e for e in es), land, rs))
         if len(tr) == 1:
             rid, pid, mask, land, rs = tr[0]
-            g.remote_dma(T[land][:], T[src][:], S[rs], S[ls], pid, rid, mask)
+            g.remote_dma(T[land][:], T[src][:, 0:192], S[rs], S[ls], pid, rid, mask)
         else:
             g.remote_dma_fused([RemoteDMATransfer(dst_ids=[DstId(rid=rid, pnc=pid)], dma_engine_mask=mask, remote_sem=S[rs],
-                                                  src=T[src][:], dst=T[land][:]) for rid, pid, mask, land, rs in tr], local_sem=S[ls])
+                                                  src=T[src][:, 0:192], dst=T[land][:]) for rid, pid, mask, land, rs in tr], local_sem=S[ls])
         snap[(ls, total)] = dict(known["g"])
         note("rem", ls, total, [(src, 0, 192)], [])
         loc_done.append((ls, total))
@@ -209,344 +207,329 @@ def rank_program(g, core, T, topo):
     up1, up2 = (rank + 1) % n_ranks, (rank + 2) % n_ranks
     dn1, dn2 = (rank - 1) % n_ranks, (rank - 2) % n_ranks
     n16 = len(topo.engines(core, T.cores[up1]))
-    H = (0, 1)
 
-    dma("s", [(R("mi32"), ext(T.m0))])
-    dma("s", [(R("X", 0, 4096), ext(T.x0))])
-    dma("a", [(R("od"), ext(T.own0))])
-    dma("a", [(R("thi"), ext(T.th))])
-    dma("s", [(R("nbw"), ext(T.nb))])
+    dma("s", R("mi32"), ext(T.m0))
+    dma("s", R("X", 0, 4096), ext(T.x0))
+    dma("a", R("od"), ext(T.own0))
+    ms(R("thi"), 0)
+    dma("a", (T.thi[0:128:16, 0:1], [("thi", 0, 8)]), ext(T.th))
+    dma("s", R("nbw"), ext(T.nb))
+    ms(R("ONE"), 1.0)
     iota(R("pI"), [[0, 1]], 0, 1, False)
-    iota(R("kk"), [[0, 16], [1, 16]])
-    iota(R("cc"), [[1, 128]])
-    iota(R("c16"), [[16, 12]])
-    iota(R("a32"), [[1, 192]], 0, 0, False)
+    iota(R("cc"), [[1, 16]])
+    select(R("ID"), R("ONE"), [[-1, 128]], OP.is_equal, 0, 1)
+    select(R("BLK"), R("ONE"), [[-16, 8], [0, 16]], OP.is_ge, 0, 1)
+    select(R("BLK"), R("BLK"), [[16, 8], [0, 16]], OP.is_ge, 15, -1)
     ms(R("m01"), 1.0)
-    ms(R("m01", 0, 1536, 16), 0.0)
+    ms(R("EX", p=96), -1.0)
+    ms(R("m01", 0, 768, 16), 0.0)
     ms(R("m512"), 0.0)
-    ms(R("m512", 0, 1536, 16), 512.0)
-    for h in H:
-        act(R("CZI", 1536 * h, 1536 * h + 1536), R("m01"), AF.Copy, 0.0, 0.0)
+    ms(R("m512", 0, 768, 16), 512.0)
+    for i in range(3):
+        act(R("ow", 768 * i, 768 * i + 768), R("m01"), AF.Copy, 0.0, 0.0)
     cp(R("oR0"), R("mi32"))
     send("oR0", [(up1, "oI0", "rM")])
     landed("oI0", "rM", n16)
-    for name, c in (("CZR", 0), ("EQ", 0), ("meq", 1), ("ZR", 0), ("ZL", 0), ("ZK", 0), ("RC0", 0), ("RC1", 0)):
-        iota(R(name), [[0, SHAPE[name][1]]], c)
-    iota(R("FW", 0, 4096), [[0, 4096]], 1)
-    iota(R("FW", 4096, 4288), [[0, 192]], 0)
+    iota(R("ow", 2304, 4288), [[0, 1984]])
+    iota(R("krow"), [[0, 12], [1, 16]], -15)
+    iota(R("kap"), [[0, 8], [-1, 16]], 15)
+    iota(R("kan"), [[0, 8], [1, 16]], -15)
+    select(R("EX", p=96), R("EX", p=96), [[-1, 96], [0, 16]], OP.is_equal, 0, 1)
+    ms(R("CZ"), 0.0)
     ts(R("pJ"), R("pI"), 15, OP.bitwise_and)
     cp(R("p15"), R("pJ"))
-    cp(R("pf"), R("pI"))
-    ts(R("pJ"), R("pI"), 4, OP.arith_shift_right)
-    cp(R("p16"), R("pJ"))
-    ts(R("ID"), R("cc"), R("pf"), OP.is_equal)
-    for name, c in (("BI1", 1024.0), ("BI2", 2048.0), ("BN1", -1024.0), ("BN2", -2048.0)):
-        ts(R(name), R("cc", 0, 8), R("p16"), OP.is_equal, c, OP.mult)
-    for name, c in (("IDn", -1.0), ("ID2", 2.0), ("ID64", 64.0)):
+    ts(R("EQm"), R("cc"), R("p15"), OP.is_equal)
+    ts(R("LTm"), R("cc"), R("p15"), OP.is_gt)
+    for name, c in (("W64", 64.0), ("W32", 32.0), ("Wm", -32.0), ("W1", 1.0), ("W8", 8192.0)):
+        ms(R(name), 0.0)
+        ts(R(name, 15, 143, 16), R("BLK", 0, 128, 16), c, OP.mult)
+    for name, c in (("IDh", 0.5), ("I13", 2.0 ** -13), ("IDk", -KILL), ("IDn", -1.0)):
         ts(R(name), R("ID"), c, OP.mult)
-    ms(R("one1"), 1.0)
-    ts(R("j64"), R("kk", 0, 256, 1, 1), 64.0, OP.mult)
-    ts(R("j128"), R("kk", 0, 256, 1, 1), 128.0, OP.mult)
-    ms(R("mB"), 0.0)
-    ms(R("mB", 0, 1024, 16), BIG)
-    ms(R("ZS"), 0.0)
-    ts(R("dA"), A("kk"), R("p15", p=96), OP.is_equal)
-    ts(R("B6"), A("cc", 0, 6), R("p16", p=96), OP.is_equal)
+    for name, c in (("one", 1.0), ("cq", -0.25), ("cm", -2048.0), ("ch", 0.5), ("cI", 163840.0), ("cR", 98304.0), ("zrow", 0.0)):
+        ms(R(name), c)
+    for j in range(16):
+        act(R("FK", 128 * j, 128 * j + 128), R("BLK"), AF.Copy, 0.0, R("EQm", j, j + 1))
     cp(R("ob"), R("od"))
-    dma("s", [((T.odr[:], [("odr", 0, 4096)]), R("ob"))])
-    dma("s", [((T.ow[r:128:16, 0:4096], [("ow", 0, 4096)]), (T.odr[:], [("odr", 0, 4096)])) for r in range(16)])
-    ts(R("IDf"), R("cc", 0, 8, 1, 8), R("pf", p=8), OP.is_equal)
-    ts(R("dW"), R("kk", 0, 192), R("p15"), OP.is_equal)
-    ts(R("LT"), R("kk", 0, 192), R("p15"), OP.is_ge, 1000.0, OP.mult)
-    ms(R("ZW"), 0.0)
-    ms(R("ZZ"), 0.0)
-    cp(R("aU"), R("a32"))
-    ts(R("aC", 0, 12), R("c16"), R("p15"), OP.add, 4096.0, OP.add)
-    ts(R("aC", 12, 24), R("c16"), R("p15"), OP.add, 192.0, OP.add)
-    ts(R("pp1"), R("p15"), 1.0, OP.add)
-
-    def thresholds():
-        ms(R("oneF"), 1.0)
-        cp(R("thf"), R("thi"))
-        ts(R("thD"), R("IDf"), R("thf"), OP.mult)
-        mm(R("b6", 0, 8, 1, 96), R("oneF"), R("thD"))
-        for h in H:
-            ts(R("thA", 8 * h, 8 * h + 8), A("b6", 0, 8), 1024.0, OP.mult)
+    dma("s", (T.ow[0:128:16, 0:4096], [("ow", 0, 4096)]), R("ob"))
+    ms(R("mB"), 0.0)
+    ms(R("mB", 0, 192, 16), BIG)
+    ms(R("mD"), 2.0)
+    ms(R("mD", 0, 192, 16), -BIG)
+    ts(R("BK8"), R("BLK"), 8192.0, OP.mult)
 
     def late_constants():
+        for r in range(1, 16):
+            act(R("LO", 128 * r, 128 * r + 128), R("BLK"), AF.Copy, 0.0, R("LTm", r, r + 1))
+        cp(R("IDf"), R("ID"))
         ms(R("X", 4096, 4288), 0.0)
-        ms(R("ow", 4096, 4288), 0.0)
-        ms(R("oneB"), 1.0)
-        cp(R("mb0"), R("mi32"))
+        ms(R("MR0", 192, 384), 0.0)
+        ms(R("MR1", 192, 384), 0.0)
+        cp(R("MR0", 0, 192), R("mi32"))
+        iota(R("aC", 0, 12), [[16, 12]], 2049)
+        iota(R("aC", 12, 24), [[16, 12]], -1855)
+        ts(R("aC"), R("aC"), R("p15"), OP.add, -0.5, OP.add)
+        cp(R("e0"), R("EQm", 0, 1))
+        ts(R("e192"), R("EQm", 0, 1), 192.0, OP.mult)
+        ts(R("eB"), R("EQm", 0, 1), -192.0 * 191.0, OP.mult)
+        ts(R("th16"), R("thi", 0, 1), -2048.0, OP.add)
+        mm(R(B7, 0, 1), R("BLK"), R("th16"), True, True)
+        ts(R("lim0"), R(B7, 0, 1), 32.0, OP.mult, 32.0 * 32768.0 - 15.5, OP.add)
 
-    def half(name, h, step=1):
-        return R(name, 1536 * h, 1536 * h + 1536, step)
+    def part(name, q, step=1):
+        return R(name, 768 * q, 768 * q + 768, step)
 
-    def gather(v, off, h):
-        act(half(v, h), IND("X", 0, 4096, off, 96 * h, 96 * h + 96))
+    def gather(v, off, lo, hi, eng=act):
+        eng(R(v, 16 * lo, 16 * hi), IND("X", 0, 4096, off, lo, hi))
 
-    def begin(bank):
-        mm(A(bank, 0, 256), R("one1", 0, 96), R("j64"), True, False)
+    def row(bank, n, l, r="one", start=True, stop=False):
+        mm(R(bank, 0, n), R(l, 0, 128), R(r, 0, n), start, stop)
 
-    def group_sum(bank, src, w, h, stop=False):
-        for k in range(16):
-            mm(A(bank, 128 * h + k, 128 * h + 128, 16), R(src, 1536 * h + k, 1536 * h + 1536, 16), R(w), False, stop and k == 15)
+    def group_sum(bank, src, w, j0, j1, stop=False):
+        for j in range(j0, j1):
+            mm(R(bank, 0, 192), R(w, 15 - j, 143 - j), R(src, 192 * j, 192 * j + 192), False, stop and j == j1 - 1)
 
-    def digits(bank, at, i, h, w, start=False, stop=False):
-        mm(A(bank, at + 128 * h, at + 128 * h + 128), R("HL", 192 * i + 96 * h, 192 * i + 96 * h + 96), R(w), start, stop)
+    def from_keys(bank, src):
+        for j in range(16):
+            mm(R(bank, 12 * j, 12 * j + 12), R("FK", 128 * j, 128 * j + 128), src, False, j == 15)
 
-    def split(m32):
-        ts(R("HL32", 0, 192), R(m32), 6, OP.arith_shift_right)
-        ts(R("HL32", 192, 384), R(m32), 63, OP.bitwise_and)
-        cp(R("HL"), R("HL32"))
+    def to_list(bank, src, w, n=192, start=False):
+        for j in range(16):
+            mm(R(bank, 0, n // 16), R(w, 15 - j, 143 - j), R(src, j, n, 16), start and j == 0, j == 15)
 
-    def payload(wide):
-        for h in H:
-            digits("b2", 0, 1, h, "ID", True, False)
-            digits("b2", 0, 0, h, "IDn", False, True)
-        act(R("Q1"), A("b2", 0, 256))
-        for i in range(2 if wide else 1):
-            mm(A("b4", 256 * i, 256 * i + 256), R("one1", 0, 96), R("j128"), True, False)
-            for h in H:
-                digits("b4", 256 * i, 0, h, "ID" if i else "ID2", False, h == 1 and not i)
-                if i:
-                    digits("b4", 256 * i, 1, h, "ID", False, h == 1)
-        n = 512 if wide else 256
-        act(R("Q23", 0, n), A("b4", 0, n))
+    def extremes(v, mx, mn, q):
+        scan(part(mx, q), R("m01"), part(v, q), OP.mult, OP.max)
+        scan(part(mn, q), R("m512"), part(v, q), OP.add, OP.min)
+        bank = PSUM[6 + q % 2]
+        row(bank, 48, "cq")
+        mm(R(bank, 0, 48), R("IDh"), R(mx, 768 * q + 15, 768 * q + 768, 16))
+        mm(R(bank, 0, 48), R("IDh"), R(mn, 768 * q + 15, 768 * q + 768, 16), False, True)
 
-    def extremes(v, mx, mn, h):
-        scan(half(mx, h), R("m01"), half(v, h), OP.mult, OP.max)
-        scan(half(mn, h), R("m512"), half(v, h), OP.add, OP.min)
+    def centres(cx, q):
+        ts(R("CZ", 0, 768, 16), R(PSUM[6 + q % 2], 0, 48), R1, OP.add, R1, OP.subtract)
+        scan(part(cx, q), R("m01"), R("CZ"), OP.mult, OP.add)
 
-    def centres(mx, mn, s, ci, cz):
-        tt(R(s), R(mx, 15, 3072, 16), R(mn, 15, 3072, 16), OP.add)
-        ts(R(ci), R(s), 0.5, OP.mult, -0.25, OP.add)
-        cp(R(cz, 0, 3072, 16), R(ci))
+    def larger(v, cx, d, q):
+        tt(part(v, q, 16), part(v, q, 16), part(cx, q, 16), OP.max)
+        scan(part(d, q), part(cx, q), part(v, q), OP.min, OP.max)
 
-    def spread(cx, cz, h):
-        scan(half(cx, h), R("m01"), half(cz, h), OP.mult, OP.add)
+    def least(f, at, bank):
+        scan(R(f, at, at + 192), R("mB"), R(bank, 0, 192), OP.add, OP.min)
 
-    def larger(v, first, cx, c0, d, h):
-        tt(half(v, h, 16), first, half(c0, h, 16), OP.max)
-        scan(half(d, h), half(cx, h), half(v, h), OP.min, OP.max)
+    def largest(f, at, bank):
+        scan(R(f, at, at + 192), R("mD"), R(bank, 0, 192), OP.add, OP.max)
 
-    def seg(f, lo, hi):
-        return A(f, lo + 15, hi, 16)
+    def rest(o, f, lo, hi, turn=False):
+        n = (hi - lo) // 16
+        ends = R(f, lo + 15, hi, 16)
+        ts(R("rr", 0, n), ends, R32, OP.add, R32, OP.subtract)
+        if turn:
+            tt(o, R("rr", 0, n), ends, OP.subtract)
+        else:
+            tt(o, ends, R("rr", 0, n), OP.subtract)
+
+    def clamp(o, bank):
+        ts(o, R(bank, 0, 192), -0.25, OP.max, 0.25, OP.min)
 
     def play(t):
-        oI, oR, mb = "oI%d" % t, "oR%d" % t, "mb%d" % t
-        IC, RC, MR = "IC%d" % t, "RC%d" % t, "MR%d" % t
+        oI, oR = "oI%d" % t, "oR%d" % t
+        IC, MR = "IC%d" % t, "MR%d" % t
         last = t == 1
-        m96 = R("m01", 0, 256, 1, 96)
-        m96x2 = R("m01", 0, 512, 1, 96)
-        mB1 = A("mB", 0, 256)
-        if t == 0:
-            thresholds()
-            cp(R("mw"), R(oI))
-        gather("VI", oI, 0)
-        act(R("VI", 1536, 2304), IND("X", 0, 4096, oI, 96, 144))
-        cp(R("VI", 2304, 3072), IND("X", 0, 4096, oI, 144, 192))
-        split("mw")
-        for h in H:
-            extremes("VI", "XI", "NI", h)
-        begin("b0")
-        for h in H:
-            digits("b0", 0, 0, h, "ID")
-        payload(False)
-        gather("VR", oR, 0)
-        for h in H:
-            group_sum("b0", "VI", "BN1", h)
-        gather("VR", oR, 1)
-        centres("XI", "NI", "sI", "CiI", "CZI")
-        for h in H:
-            spread("CXI", "CZI", h)
-            larger("VI", half("VI", h, 16), "CXI", "CZI", "DA", h)
-            group_sum("b0", "DA", "BI2", h, h == 1)
-        extremes("VR", "XR", "NR", 0)
-        u, a0 = A("b3", 0, 256), A("b0", 0, 256)
-        scan(R("FI", 0, 256), mB1, a0, OP.add, OP.min)
-        tt(R("KI", 0, 256), a0, R("Q1"), OP.add)
-        scan(R("FI", 256, 512), mB1, R("KI", 0, 256), OP.add, OP.min)
-        cp(R("eI", 0, 32), seg("FI", 0, 512))
-        ts(R("e63"), R("eI", 0, 32), 63, OP.bitwise_and)
-        tt(R("KI", 512, 768), R("Q23", 0, 256), a0, OP.subtract)
-        ts(R("t16"), R("e63", 0, 16), 64.0, OP.mult)
-        tt(R("ZS", 0, 256, 16), R("t16"), R("e63", 16, 32), OP.add)
-        scan(u, m96, R("ZS"), OP.mult, OP.add)
-        tt(R("SXm"), u, R("dA"), OP.mult)
-        for h in H:
-            mm(R("b7", 6 * h, 6 * h + 6), R("SXm", 128 * h, 128 * h + 128), R("B6"))
-        cp(R("sL"), R("b7", 0, 12))
-        begin("b5")
-        for h in H:
-            group_sum("b5", "VR", "BI1", h)
-        cp(R("nL"), IND("nbw", 0, 4096, "sL", 0, 12))
-        act(R("SW", 0, 12), R("b7", 0, 12))
-        for h in H:
-            gather("V2", "nL", h)
-            act(R("V0", 96 * h, 96 * h + 96), half("V2", h, 16))
-        cp(R("bf"), IND("ow", 0, 4096, "sL", 0, 12))
-        cp(R("bU"), R("bf"))
-        mm(R("b6", 0, 192), R("ID"), R("bf"), True, False)
-        mm(R("b6", 0, 192), R("ID"), R("LT"), False, True)
-        extremes("VR", "XR", "NR", 1)
-        centres("XR", "NR", "sR", "CiR", "CZR")
-        cp(R("CRc"), R("CiR"))
-        for h in H:
-            act(half("CXB", h), IND("CRc", 0, 192, "bU", 96 * h, 96 * h + 96))
-        cp(R("n32"), R("nL"))
-        split("n32")
-        for bank in ("b0", "b1"):
-            begin(bank)
-            for h in H:
-                digits(bank, 0, 0, h, "ID")
-        for h in H:
-            for bank in ("b0", "b1"):
-                group_sum(bank, "V2", "BN1", h)
-        scan(R("FI", 512, 768), mB1, R("KI", 512, 768), OP.add, OP.min)
-        payload(True)
-        act(half("CXR", 1), IND("CRc", 0, 192, "aU", 96, 192))
-        cp(R("eI", 32, 48), seg("FI", 512, 768))
-        ts(R("kc"), R("eI"), 6, OP.arith_shift_right, 15, OP.bitwise_and)
-        cp(R("kfl"), R("kc"))
-        tt(R("dk"), R("kfl", 32, 48), R("kfl", 0, 16), OP.subtract)
-        if t == 0:
-            ms(R("meq", 0, 1936, 176), 0.0)
-            ms(R("meq", 1936, 2128, 16), 0.0)
-        tt(R("bd"), R("bf"), R("dW"), OP.mult)
-        scan(R("bs"), R("m01", 0, 192), R("bd"), OP.mult, OP.add)
-        cp(R("SW", 12, 24), R("bs", 15, 192, 16))
-        cp(R("ZW", 0, 192, 16), R("bs", 15, 192, 16))
-        cp(R("Lb"), R("SW", 12, 24))
-        for c in range(1, 12):
-            e = 176 * c
-            ts(R("EQ", e - 16 * c, e), R("bf", 0, 16 * c), R("SW", 12 + c, 13 + c), OP.is_equal)
-        scan(R("bx"), R("m01", 0, 192), R("ZW"), OP.mult, OP.add)
-        tt(R("EQ", 1936, 2128), R("b6", 0, 192), R("bx"), OP.is_equal)
-        scan(R("EC"), R("meq"), R("EQ"), OP.mult, OP.add)
-        cp(R("du"), R("EC", 1951, 2128, 16))
-        tt(R("du", 1, 12), R("du", 1, 12), R("EC", 175, 1936, 176), OP.add)
-        ts(R("f2", 0, 12), R("du"), 0.0, OP.is_equal)
-        ts(R("f2", 12, 24), R("du"), 0.0, OP.is_equal)
-        tt(R("l1"), R("SW"), R("aC"), OP.subtract)
-        tt(R("l2"), R("l1"), R("f2"), OP.mult)
-        tt(R("l3"), R("l2"), R("aC"), OP.add)
-        cp(R("LS"), R("l3"))
-        for h in H:
-            larger("V2", R("V0", 96 * h, 96 * h + 96), "CXI", "CZI", "DA", h)
-            group_sum("b0", "DA", "BI2", h, h == 1)
-        act(R("ff"), IND("FW", 0, 4288, "LS", 0, 12))
-        act(R("fp"), R("ff"), AF.Identity, -1.0, R("pp1"))
-        if not last:
-            act(R("xg"), IND("X", 0, 4096, "sL", 0, 12), AF.Relu, -16.0)
-        for h in H:
-            larger("V2", R("V0", 96 * h, 96 * h + 96), "CXB", "CXB", "DB", h)
-            group_sum("b1", "DB", "BI2", h, h == 1)
-        for i, cz in ((0, "CZI"), (1, "CXB")):
-            for h in H:
-                mm(A("b7", 16 + 16 * i + 8 * h, 24 + 16 * i + 8 * h), half(cz, h, 16), R("BI1"))
+        KI, KR, KE, KB = B0, B1, B2, B3
+        lim = R("lim" if t else "lim0")
+        gather("VR", oR, 0, 48)
+        gather("VI", oI, 144, 192, cp)
+        for q in range(3):
+            gather("VI", oI, 48 * q, 48 * q + 48)
+        for q in range(1, 4):
+            gather("VR", oR, 48 * q, 48 * q + 48)
+        for bank in (KI, KE, KR, KB):
+            row(bank, 192, "one", "krow")
+        order = (3, 0, 1, 2)
+        for i in range(5):
+            if i < 4:
+                group_sum(KI, "VI", "Wm", 4 * order[i], 4 * order[i] + 4)
+                extremes("VI", "XI", "NI", order[i])
+            if i == 0:
+                ts(R("M16"), R(oI), -2048.0, OP.add)
+            if i > 0:
+                q = order[i - 1]
+                centres("CXI", q)
+                larger("VI", "CXI", "DA", q)
+                group_sum(KI, "DA", "W64", 4 * q, 4 * q + 4, i == 4)
         if t == 0:
             late_constants()
-        spread("CXR", "CZR", 0)
-        for h in H:
-            larger("VR", half("VR", h, 16), "CXR", "CZR", "DA", h)
-            group_sum("b5", "DA", "BN2", h, h == 1)
-        ui, ur = a0, A("b1", 0, 256)
-        q1, q2, q3 = R("Q1"), R("Q23", 0, 256), R("Q23", 256, 512)
-        scan(R("FI", 0, 256), mB1, ui, OP.add, OP.min)
-        tt(R("KI", 256, 512), q2, ui, OP.subtract)
-        tt(R("KI", 512, 768), ui, q1, OP.add)
-        tt(R("KI", 768, 1024), q3, ui, OP.subtract)
-        scan(R("FI", 256, 1024), A("mB", 256, 1024), R("KI", 256, 1024), OP.add, OP.min)
+        extremes("VR", "XR", "NR", 0)
+        least("FK1", 0, KI)
+        row(B4, 192, "kap")
+        mm(R(B4, 0, 192), R("I13"), R("M16"))
+        rest(R("VV", 24, 36), "FK1", 0, 192)
+        from_keys(B4, R("VV", 24, 36))
+        centres("CXR", 0)
+        clamp(R("S0"), B4)
+        row(B5, 12, "cm")
+        row(B5, 12, "ch", "one", False)
+        to_list(B5, "S0", "W8")
+        extremes("VR", "XR", "NR", 1)
+        ts(R("rr", 0, 12), R(B5, 0, 12), R4096, OP.add, R4096, OP.subtract)
+        tt(R("SW", 0, 12), R(B5, 0, 12), R("rr", 0, 12), OP.subtract)
+        ts(R("sL"), R("SW", 0, 12), MID, OP.add)
+        act(R("b0"), IND("ow", 0, 4096, "sL", 0, 12))
+        cp(R("nL"), IND("nbw", 0, 4096, "sL", 0, 12))
+        to_list(B5, "b0", "W1", 192, True)
+        mm(R(B4, 0, 192), R("BLK"), R("b0"), True, True)
+        gather("V2", "nL", 0, 32)
+        act(R("bf"), R(B4, 0, 192))
+        group_sum(KE, "CXI", "Wm", 0, 16)
+        centres("CXR", 1)
+        extremes("VR", "XR", "NR", 2)
+        ts(R("SW", 12, 24), R(B5, 0, 12), -MID, OP.add)
+        ts(R("Lc"), R(B5, 0, 12), 16.0, OP.mult)
+        cp(R("Lb"), R(B5, 0, 12))
+        gather("V2", "nL", 32, 64)
+        extremes("VR", "XR", "NR", 3)
+        group_sum(KR, "VR", "Wm", 0, 16)
+        centres("CXR", 2)
+        centres("CXR", 3)
+        gather("V2", "nL", 64, 96)
+        act_gather_pool("Cb", "CXR", 3072, "Lc")
+        for h in (0, 1):
+            mm(R(B4, 128 * h, 128 * h + 128, 1, 96), R("Cb", 96 * h, 96 * h + 96), R("ID"), True, True)
+        gather("V2", "nL", 96, 128)
+        act(R("CT", p=96), R(B4, 0, 256, 1, 96))
+        for c in range(12):
+            ts(R("EQ", 208 * c, 192 * c + 192), R("bf", 16 * c, 192), -MID, OP.add, R("SW", 12 + c, 13 + c), OP.is_equal)
+        row(B6, 192, "zrow")
+        for c in range(11):
+            mm(R(B6, 16 * c + 16, 192), R("BLK"), R("EQ", 208 * c + 16, 192 * c + 192))
+        for r in range(1, 16):
+            mm(R(B6, r, 192, 16), R("LO", 128 * r, 128 * r + 128), R("EQ", r, 2304, 208), False, r == 15)
+        gather("V2", "nL", 128, 160)
+        gather("V2", "nL", 160, 192)
+        for q in range(4):
+            larger("VR", "CXR", "DR", q)
+        group_sum(KE, "V2", "Wm", 0, 8)
+        blocks = (0, 2, 5, 8, 10, 13, 16)
+        for i in range(7):
+            if i < 6:
+                bank = PSUM[4 + i % 2]
+                mm(R(bank), R("ID"), R("V2", 512 * i, 512 * i + 512), True)
+                mm(R(bank), R("CT", 128 * (i // 3), 128 * (i // 3) + 128, 1, 96), R("EX", 512 * (i % 3), 512 * (i % 3) + 512, 1, 96), False, True)
+                act(R("DB", 512 * i, 512 * i + 512), R(bank), AF.Abs)
+            if i == 0:
+                for h in (0, 1):
+                    act(R("cnt", 192 * h, 192 * h + 192), R(B6, 0, 192))
+                group_sum(KR, "DR", "W64", 0, 8)
+            if i == 1:
+                group_sum(KE, "V2", "Wm", 8, 16)
+                mm(R(B7, 0, 24), R("IDf"), R("SW"), True)
+                to_list(B7, "cnt", "W8", 384)
+            if i == 2:
+                group_sum(KR, "DR", "W64", 8, 16, True)
+                largest("FK1", 192, KI)
+                ts(R("n16"), R("nL"), -2048.0, OP.add)
+                for q in (0, 1):
+                    larger("V2", "CXI", "D2", q)
+                tt(R("l1"), R(B7, 0, 24), R("aC"), OP.min)
+                ts(R("LS"), R("l1"), MID, OP.add)
+                largest("FK1", 384, KR)
+                rest(R("UU", 24, 36), "FK1", 192, 384)
+                rest(R("kR"), "FK1", 384, 576, True)
+            if i == 3:
+                group_sum(KE, "D2", "W64", 0, 8)
+            if i == 5:
+                for q in (2, 3):
+                    larger("V2", "CXI", "D2", q)
+                row(B7, 192, "kap")
+                from_keys(B7, R("kR"))
+            if i > 0:
+                group_sum(KB, "DB", "W32", blocks[i - 1], blocks[i], i == 6)
+        group_sum(KE, "D2", "W64", 8, 16, True)
+        act(R("FM", 192, 384), R(KB, 0, 192), AF.Sign, lim, -1.0)
+        row(B0, 192, "kan")
+        mm(R(B0, 0, 192), R("I13"), R("n16"))
+        row(B1, 192, "kap")
+        mm(R(B1, 0, 192), R("I13"), R("n16"))
+        row(B4, 192, "kap")
+        mm(R(B5, 0, 192), R("IDn"), R("cnt", 0, 192), True)
+        row(B6, 192, "cI")
+        mm(R(B6, 0, 192), R("IDk"), R("cnt", 0, 192))
+        largest("FS", 384, KB)
+        least("FS", 576, KB)
+        act(R("FM", 0, 192), R(KE, 0, 192), AF.Sign, lim, -1.0)
+        act(R("QR"), R(B7, 0, 192), AF.Square)
+        rest(R("VV", 0, 24), "FS", 384, 768)
+        least("FS", 0, KE)
+        largest("FS", 192, KE)
+        scan(R("CN"), R("m01", 0, 384), R("FM"), OP.mult, OP.add)
+        act_gather_pool("QG", "QR", 192, "Lb")
+        act_gather_pool("Mg", MR, 192, "Lb")
         if not last:
-            cp_scatter(IND("X", 0, 4288, "LS", 0, 12), R("xg"))
-        for i in (0, 1):
-            tt(R("ZL", 256 * i, 256 * i + 256, 16), A("b7", 16 + 16 * i, 32 + 16 * i), R("thA"), OP.add)
-        scan(R("LX"), m96x2, R("ZL"), OP.mult, OP.add)
-        tt(R("FM", 0, 256), ui, R("LX", 0, 256), OP.is_lt)
-        tt(R("FM", 256, 512), ur, R("LX", 256, 512), OP.is_lt)
-        scan(R("CN"), m96x2, R("FM"), OP.mult, OP.add)
-        tt(R("w4", 0, 16), seg("CN", 0, 256), seg("CN", 256, 512), OP.is_gt)
-        for i in (1, 2, 3):
-            act(R("w4", 16 * i, 16 * i + 16), R("w4", 0, 16))
-        act(R("ZK", 256, 512, 16), R("w4", 0, 16))
-        tt(R("dw"), R("dk"), R("w4", 0, 16), OP.mult)
-        tt(R("ZK", 0, 256, 16), R("dw"), R("kfl", 0, 16), OP.add)
-        tt(R("KR", 0, 256), q2, ur, OP.subtract)
-        scan(R("FR", 256, 512), mB1, ur, OP.add, OP.min)
-        scan(R("KX"), m96x2, R("ZK"), OP.mult, OP.add)
-        tt(R("KR", 256, 512), q3, ur, OP.subtract)
-        tt(R("KR", 512, 768), ur, q1, OP.add)
-        scan(R("FR", 0, 256), mB1, R("KR", 0, 256), OP.add, OP.min)
-        scan(R("FR", 512, 1024), A("mB", 0, 512), R("KR", 256, 768), OP.add, OP.min)
-        scan(R("FD"), mB1, A("b5", 0, 256), OP.add, OP.min)
-        cp(R("eD"), seg("FD", 0, 256))
-        ts(R("fD"), R("eD"), 6, OP.arith_shift_right, 15, OP.bitwise_and)
-        cp(R("ZR", 0, 256, 16), R("fD"))
-        scan(R("RX"), m96, R("ZR"), OP.mult, OP.add)
-        for h in H:
-            mm(R("b6", 96 * h, 96 * h + 96), R("RX", 128 * h, 128 * h + 128), R("ID", 0, 96, 1, 96))
-        ts(R("mR"), R("b6", 0, 192), R("p15"), OP.is_equal)
-        act(R("mRa"), IND("mR", 0, 192, "Lb", 0, 12))
-        for i in range(4):
-            mm(R("b6", 96 * i, 96 * i + 96), R("KX", 128 * i, 128 * i + 128), R("ID", 0, 96, 1, 96))
-        tt(R("s1"), seg("FI", 0, 1024), seg("FR", 0, 1024), OP.subtract)
-        tt(R("s2"), R("s1"), R("w4"), OP.mult)
-        tt(R("s3"), R("s2"), seg("FR", 0, 1024), OP.add)
-        ts(R("s4"), R("s3"), 63, OP.bitwise_and)
-        ts(R("ZZ", 0, 512, 16), R("s4", 0, 32), 128.0, OP.add)
-        cp(R("ZZ", 512, 1024, 16), R("s4", 32, 64))
-        for i, bank in ((0, "b5"), (1, "b4")) if last else ((1, "b4"), (0, "b5")):
-            for d in (0, 512):
-                scan(R("ZX", d + 256 * i, d + 256 * i + 256), m96, R("ZZ", d + 256 * i, d + 256 * i + 256), OP.mult, OP.add)
-            for h in H:
-                for d, w in ((0, "ID64"), (512, "ID")):
-                    mm(R(bank, 96 * h, 96 * h + 96), R("ZX", d + 256 * i + 128 * h, d + 256 * i + 128 * h + 128), R(w, 0, 96, 1, 96), d == 0, d > 0)
-        tt(R("ox"), R("bf"), R("b6", 192, 384), OP.add)
-        ts(R("oy"), R("ox"), 192.0, OP.is_lt)
-        tt(R("ov"), R("ox"), R("oy"), OP.mult)
-        act(R("zr"), R("b4", 0, 192), AF.Identity, -4096.0)
-        tt(R("mk"), R("b6", 0, 192), R("fp"), OP.is_equal)
-        tt(R(IC), R("b5", 0, 192), R("mk"), OP.mult)
+            act(R("xg"), IND("X", 0, 4096, "sL", 0, 12), AF.Relu, -16.0)
+        rest(R("UU", 0, 24), "FS", 0, 384)
+        tt(R("won"), R("CN", 15, 192, 16), R("CN", 207, 384, 16), OP.is_gt)
+        tt(R("SS"), R("UU"), R("VV"), OP.add)
+        for i in (0, 2, 1):
+            tt(R("PP", 12 * i, 12 * i + 12), R("SS", 12 * i, 12 * i + 12), R("won"), OP.mult)
+        tt(R("RR"), R("VV"), R("PP"), OP.subtract)
+        row(B7, 192, "cR")
+        mm(R(B7, 0, 192), R("IDk"), R("QG"))
+        from_keys(B0, R("RR", 0, 12))
+        from_keys(B4, R("RR", 24, 36))
+        clamp(R("S0"), B0)
+        act(R("QK"), R(B4, 0, 192), AF.Square)
+        from_keys(B1, R("RR", 12, 24))
+        mm(R(B6, 0, 192), R("BK8"), R("S0"))
+        mm(R(B6, 0, 192), R("IDk"), R("QK"), False, True)
+        clamp(R("S1"), B1)
+        act(R(IC), R(B6, 0, 192), AF.Relu)
         if not last:
             send(IC, [(dn1, "inA", "rA"), (up1, "inB", "rB")])
         else:
             send(IC, [(dn2, "inC", "rC")])
-        tt_scatter(IND(RC, 0, 384, "LS", 12, 24), R("zr"), R("mRa"), OP.mult)
-        tt(R(MR), R(RC, 0, 192), R(mb), OP.max)
+        mm(R(B7, 0, 192), R("BK8"), R("S1"), False, True)
+        from_keys(B5, R("won"))
+        act(R("zr"), R(B7, 0, 192), AF.Relu)
+        tt_scatter(IND(MR, 0, 384, "LS", 12, 24), R("zr"), R("Mg"), OP.max)
         if not last:
             send(MR, [(up2, "inM", "rR")])
-        cp_scatter(IND("ow", 0, 4288, "LS", 0, 12), R("ov"))
+        act(R("wf"), R(B5, 0, 192), AF.Relu, acc=R("wc"))
+        mm(R(B2, 0, 192), R("BLK"), R("b0"), True)
+        mm(R(B2, 0, 192), R("ID"), R("wf"), False, True)
+        if not last:
+            cp_scatter(IND("X", 0, 4288, "LS", 0, 12), R("xg"))
+        act(R("xa"), R(B2, 0, 192), AF.Copy, 0.0, R("e0"))
+        act(R("ya"), R(B2, 0, 192), AF.Relu, R("eB"), R("e192"))
+        tt_scatter(IND("ow", 0, 4288, "LS", 0, 12), R("xa"), R("ya"), OP.subtract)
         if last:
-            dma("g", [((T.yown[:], []), (T.ow[0:128:16, 0:4096], [("ow", 0, 4096)]))])
+            dma("a", (T.yown[:], []), (T.ow[0:128:16, 0:4096], [("ow", 0, 4096)]))
             return
-        tt(R("wf"), R("b6", 192, 384), R("ff"), OP.mult)
-        act(R("wg"), R("wf"), acc=R("wc"))
         act(R("wb"), R("wc"))
-        mm(A("b7", 48, 49), R("oneB"), R("wb"))
-        ts(R("wi"), A("b7", 48, 49), 0.0625, OP.mult)
-        ts(R("wj"), R("wi"), 63, OP.bitwise_and)
-        ts(R("wk"), R("wj"), 1024.0, OP.mult)
+        mm(R(B3, 0, 1), R("ONE"), R("wb"), True, True)
+
+    def act_gather_pool(o, win, n, off):
+        act(R(o), IND(win, 0, n, off, 0, 12))
 
     def merged(old, new, words):
-        tt(R("mv"), R(old), R(new), OP.max)
+        tt(R("mv"), R(old, 0, 192), R(new), OP.max)
         ts(R(words), R("mv"), 4095, OP.bitwise_and)
 
     play(0)
     landed("inA", "rA", n16 // 2)
     landed("inB", "rB", n16 // 2)
     landed("inM", "rR", n16)
+    ts(R("wi"), R(B3, 0, 1), 0.0625, OP.mult)
+    ts(R("wj"), R("wi"), 63, OP.bitwise_and)
+    ts(R("lim"), R("wj"), 32.0, OP.mult, R("lim0"), OP.add)
     merged("MR0", "inA", "mi32")
     cp(R("oR1"), R("mi32"))
     merged("inM", "inB", "mw")
     cp(R("oI1"), R("mw"))
-    cp(R("mb1"), R("mi32"))
-    ts(R("thA"), R("thA"), R("wk"), OP.add)
+    cp(R("MR1", 0, 192), R("mi32"))
     play(1)
     landed("inC", "rC", n16)
     merged("MR1", "inC", "mi32")
     cp(R("yo"), R("mi32"))
-    dma("s", [((T.ym[:], []), R("yo"))])
+    dma("s", (T.ym[:], []), R("yo"))
     for q in ("v", "a", "p", "g"):
         g.wait_ge(S["q" + q], count[q])
     for sem, val in loc_done:

@@ -4,25 +4,28 @@ from concourse.mybir import AluOpType, ActivationFunctionType
 OP = AluOpType
 AF = ActivationFunctionType
 F32, BF, I32, U16, F16 = "float32", "bfloat16", "int32", "uint16", "float16"
+SIZE = {F32: 4, I32: 4, BF: 2, U16: 2, F16: 2}
 BIG = float(2 ** 26)
 KILL = float(2 ** 18)
 R1, R32, R4096 = 1.5 * 2 ** 23, 1.5 * 2 ** 28, 1.5 * 2 ** 35
 MID = 2047.5
+CYCLE, WAKE, SLACK, HOP = 0.00087, 0.12, 0.05, 2.5
 
 OWN_TILES = {
     F32: "ow:4288 IC0:192 IC1:192 MR0:384 MR1:384 inA:192 inB:192 inM:192 inC:192 yo:192 ob:256",
     BF: "X:4288 VI:3072 VR:3072 V2:3072 XI:3072 NI:3072 XR:3072 NR:3072 CXI:3072 CXR:3072 DA:3072 DR:3072 D2:3072 DB:3072 "
-        "CZ:768 m01:768 m512:768 FK:2048 LO:2048 EX:1536 EQ:2304 QR:192",
+        "CZ:1536 m01:768 m512:768 FK:2048 LO:2048 EX:1536 EQ:2304 QR:192",
     I32: "nbw:4096 od:256 mi32:192 thi:8",
     U16: "oR0:192 oI0:192",
 }
 POOLS = {
-    F32: "p15:1 e0:1 e192:1 eB:1 cc:16 aC:24 EQm:16 LTm:16 IDf:128 FS:768 FK1:576 rr:48 SW:24 l1:24 Mg:192 zr:192 xa:192 ya:192 wc:1 lim0:1 lim:1",
+    F32: "p15:1 e0:1 e192:1 eB:1 cc:16 aC:24 EQm:16 LTm:16 IDf:128 FS:768 FK1:576 rS:48 rK:36 rs:12 SW:24 l1:24 Mg:192 zr:192 xa:192 ya:192 "
+         "wc:1 lim0:1 lim:1",
     BF: "ONE:128 BLK:128 BK8:128 ID:128 IDh:128 I13:128 IDk:128 IDn:128 W64:144 W32:144 Wm:144 W1:144 W8:144 mB:192 mD:192 "
         "krow:192/1 kap:128/1 kan:128/1 cq:128/1 cm:128/1 ch:128/1 cI:128/1 cR:128/1 one:192/1 zrow:128/1 "
         "UU:36 VV:36 SS:36 PP:36 RR:36 kR:12 won:12 b0:192 bf:192 cnt:384 Cb:192 CT:256 QG:192 QK:192 FM:384 CN:384 wf:192 wb:1 xg:192",
-    F16: "M16:192 n16:192 S0:192 S1:192 th16:1",
-    I32: "pI:1 pJ:1 wi:1 wj:1 mw:192 mv:192",
+    F16: "M16:192 n16:192 S0:192 S1:192 S2:192 th16:1",
+    I32: "pI:1 pJ:1 wi:1 wj:1 mw:192 mv:192 mu:192",
     U16: "oI1:192 oR1:192 sL:12 nL:192 Lb:12 Lc:12 LS:24",
 }
 SCRATCH, SHAPE, PLACE = {}, {}, {}
@@ -53,10 +56,6 @@ def rank_program(g, core, T, topo):
     n_ranks = len(T.cores)
     S = T.sem
     queue = {"v": g.vector, "a": g.scalar, "p": g.tensor, "g": g, "s": g.sync}
-    count = {"v": 0, "a": 0, "p": 0, "g": 0}
-    known = {"v": {}, "a": {}, "p": {}, "g": {}, "s": {}}
-    snap = {}
-    log = {}
     ndma = [0]
     B0, B1, B2, B3, B4, B5, B6, B7 = PSUM
 
@@ -66,41 +65,11 @@ def rank_program(g, core, T, topo):
         p = shape[0] if p is None else p
         buf, at = PLACE[name]
         ap = T[buf][0:p, at + lo:at + hi:step] if step > 1 else T[buf][0:p, at + lo:at + hi]
-        return (ap, [(name, lo, hi)])
+        return (ap, [(name, lo, hi)], -(-(hi - lo) // step), SIZE[SCRATCH[buf][2]], name in PSUM, False)
 
-    def IND(win, lo, hi, off, c0, c1):
+    def IND(win, n, off, c0=0, c1=12):
         buf, at = PLACE[off]
-        return (T[win][:, lo:hi].indirect(T[buf][:, at + c0:at + c1]), [(win, lo, hi), (off, c0, c1)])
-
-    def learn(q, sem, val):
-        k = known[q]
-        for s2, v2 in snap.get((sem, val), {}).items():
-            k[s2] = max(k.get(s2, 0), v2)
-        k[sem] = max(k.get(sem, 0), val)
-
-    def need(q, reads, writes, skip_own=False):
-        deps = {}
-        for lst, wr in ((reads, False), (writes, True)):
-            for name, lo, hi in lst:
-                for e in log.get(name, ()):
-                    if name in PSUM and e[1] != q:
-                        hit = True
-                    else:
-                        hit = (wr or e[0]) and e[4] < hi and lo < e[5]
-                    if hit and not (skip_own and e[1] == q):
-                        deps[e[2]] = max(deps.get(e[2], 0), e[3])
-        for sem, val in sorted(deps.items(), key=lambda d: -len(snap.get(d, {}))):
-            if known[q].get(sem, 0) < val:
-                queue[q].wait_ge(S[sem], val)
-                learn(q, sem, val)
-
-    def note(q, sem, val, reads, writes):
-        for lst, wr in ((reads, False), (writes, True)):
-            for name, lo, hi in lst:
-                old = log.setdefault(name, [])
-                if wr:
-                    old[:] = [e for e in old if not (lo <= e[4] and e[5] <= hi)]
-                old.append([wr, q, sem, val, lo, hi])
+        return (T[win][:, 0:n].indirect(T[buf][:, at + c0:at + c1]), [(win, 0, n), (off, c0, c1)], 16 * (c1 - c0), 4, False, True)
 
     def spans(refs):
         return [s for r in refs if isinstance(r, tuple) for s in r[1]]
@@ -108,43 +77,60 @@ def rank_program(g, core, T, topo):
     def ap(x):
         return x[0] if isinstance(x, tuple) else x
 
-    def emit(q, call, outs, ins, skip_own=False):
-        rd, wr = spans(ins), spans(outs)
-        need(q, rd, wr, skip_own)
-        count[q] += 1
-        sem = "q" + q
-        call().then_inc(S[sem], 1)
-        snap[(sem, count[q])] = dict(known[q])
-        note(q, sem, count[q], rd, wr)
+    calls = []
+    seen = {}
+    group = {}
 
-    def ind_out(o):
-        return (o[0], o[1][:1]), (o[0], o[1][1:])
+    def put(q, busy, late, outs, ins, issue, adds=False, after=()):
+        rd, wr = spans(ins), spans(outs)
+        deps = set(after)
+        for lst, w in ((rd, False), (wr, True)):
+            for name, lo, hi in lst:
+                for e in seen.get(name, ()):
+                    if name in PSUM and (q != e[1] or q == "p"):
+                        hit = not (adds and e[5])
+                    else:
+                        hit = (w or e[0]) and e[3] < hi and lo < e[4]
+                    if hit:
+                        deps.add(e[2])
+        for lst, w in ((rd, False), (wr, True)):
+            for name, lo, hi in lst:
+                old = seen.setdefault(name, [])
+                if w and not adds:
+                    old[:] = [e for e in old if not (lo <= e[3] and e[4] <= hi) and name not in PSUM]
+                old.append([w, q, len(calls), lo, hi, adds])
+        calls.append((q, busy, late, (wr + rd)[0], issue, deps))
+        return len(calls) - 1
+
+    def emit(q, call, outs, ins, each=1.0):
+        o = outs[0]
+        full = [x for x in ins if isinstance(x, tuple) and x[2] > 1] or [o]
+        if o[5]:
+            outs, ins = [(0, o[1][:1])], ins + [(0, o[1][1:])]
+            c = 60 + 3.5 * o[2]
+        elif full[0][5]:
+            c = 70 + 1.5 * o[2]
+        else:
+            c = max(64, o[2] * (0.5 if each == 0.5 and all(x[3] == 2 for x in full + [o]) else max(each, 1.0)))
+        put(q, c * CYCLE, c * CYCLE, outs, ins, call)
 
     def tt(o, a, b, op):
-        emit("v", lambda: g.vector.tensor_tensor(o[0], a[0], b[0], op), [o], [a, b])
-
-    def tt_scatter(o, a, b, op):
-        w, l = ind_out(o)
-        emit("v", lambda: g.vector.tensor_tensor(o[0], a[0], b[0], op), [w], [a, b, l])
+        emit("v", lambda: g.vector.tensor_tensor(o[0], a[0], b[0], op), [o], [a, b], 1.0 if a[4] or b[4] else 2.0)
 
     def ts(o, a, s1, op0, s2=None, op1=None):
         if op1 is None:
-            emit("v", lambda: g.vector.tensor_scalar(o[0], a[0], ap(s1), None, op0), [o], [a, s1])
+            emit("v", lambda: g.vector.tensor_scalar(o[0], a[0], ap(s1), None, op0), [o], [a, s1], 0.5)
         else:
-            emit("v", lambda: g.vector.tensor_scalar(o[0], a[0], ap(s1), ap(s2), op0, op1), [o], [a, s1, s2])
+            emit("v", lambda: g.vector.tensor_scalar(o[0], a[0], ap(s1), ap(s2), op0, op1), [o], [a, s1, s2], 0.5)
 
     def cp(o, a):
-        emit("v", lambda: g.vector.tensor_copy(o[0], a[0]), [o], [a])
-
-    def cp_scatter(o, a):
-        w, l = ind_out(o)
-        emit("v", lambda: g.vector.tensor_copy(o[0], a[0]), [w], [a, l])
+        emit("v", lambda: g.vector.tensor_copy(o[0], a[0]), [o], [a], 0.5)
 
     def ms(o, c):
-        emit("v", lambda: g.vector.memset(o[0], c), [o], [])
+        emit("v", lambda: g.vector.memset(o[0], c), [o], [], 0.5)
 
     def scan(o, d0, d1, op0, op1):
-        emit("v", lambda: g.vector.tensor_tensor_scan(o[0], d0[0], d1[0], 0.0, op0, op1), [o], [d0, d1])
+        emit("v", lambda: g.vector.tensor_tensor_scan(o[0], d0[0], d1[0], 0.0, op0, op1), [o], [d0, d1], 0.5)
 
     def act(o, a, func=AF.Copy, bias=0.0, scale=1.0, acc=None):
         if acc is None:
@@ -152,68 +138,131 @@ def rank_program(g, core, T, topo):
         else:
             emit("a", lambda: g.scalar.activation(o[0], a[0], func, bias=ap(bias), scale=ap(scale), accum_out=acc[0]), [o, acc], [a, bias, scale])
 
-    def mm(o, l, r, start=False, stop=False):
-        emit("p", lambda: g.tensor.matmul(o[0], l[0], r[0], start, stop), [o], [l, r], True)
+    def mm(o, l, r, start=False):
+        bank = o[1][0][0]
+        if start:
+            group[bank] = [0]
+        left = group[bank]
+        left[0] += 1
+
+        def issue():
+            left[0] -= 1
+            return g.tensor.matmul(o[0], l[0], r[0], start, left[0] == 0)
+        c = max(min(64, l[2]), r[2]) * (4 if l[3] == 4 else 1) * CYCLE / 2
+        put("p", c, c, [o], [l, r], issue, not start)
 
     def iota(o, pat, base=0, cm=0, flag=True):
         kw = {"allow_small_or_imprecise_dtypes": True} if flag else {}
-        emit("g", lambda: g.iota(o[0], pat, base, cm, **kw), [o], [])
+        c = 0.13 + 2 * o[2] * CYCLE
+        put("g", c, c, [o], [], lambda: g.iota(o[0], pat, base, cm, **kw))
 
     def select(o, a, pat, op, base, cm):
-        emit("g", lambda: g.affine_select(o[0], a[0], pat, op, 0.0, base, cm), [o], [a])
+        c = 0.17 + 2 * o[2] * CYCLE
+        put("g", c, c, [o], [a], lambda: g.affine_select(o[0], a[0], pat, op, 0.0, base, cm))
 
-    def dma(q, a, b):
-        rd, wr = spans([b]), spans([a])
-        need(q, rd, wr)
+    def dma(q, a, b, late, after=()):
         sem = "d%d" % ndma[0]
         ndma[0] += 1
-        queue[q].dma_start(a[0], b[0]).then_inc(S[sem], 16)
-        snap[(sem, 16)] = dict(known[q])
-        note("dma", sem, 16, rd, wr)
 
-    def ext(t):
-        return (t[:], [])
+        def issue():
+            queue[q].dma_start(a[0], b[0]).then_inc(S[sem], 16)
+            return (sem, 16)
+        put(q, 0.05, late, [a], [b], issue, False, after)
+        return sem
 
-    nloc = [0]
-    loc_done = []
+    def hbm(name):
+        return (T[name][:], [(name, 0, 1)])
 
-    def send(src, outs):
-        need("g", [(src, 0, 192)], [])
-        ls = "l%d" % nloc[0]
-        nloc[0] += 1
-        total = 0
+    sent = []
+
+    def send(src, outs, late=HOP):
+        ls = "l%d" % len(sent)
         tr = []
         for i, (d, land, rs) in enumerate(outs):
             dst = T.cores[d]
             rid, pid, _ = topo.addr(dst)
             es = topo.engines(core, dst)
             m = len(es) // len(outs)
-            es = es[i * m:(i + 1) * m]
-            total += m
-            tr.append((rid, pid, sum(1 << e for e in es), land, rs))
-        if len(tr) == 1:
-            rid, pid, mask, land, rs = tr[0]
-            g.remote_dma(T[land][:], T[src][:, 0:192], S[rs], S[ls], pid, rid, mask)
-        else:
-            g.remote_dma_fused([RemoteDMATransfer(dst_ids=[DstId(rid=rid, pnc=pid)], dma_engine_mask=mask, remote_sem=S[rs],
-                                                  src=T[src][:, 0:192], dst=T[land][:]) for rid, pid, mask, land, rs in tr], local_sem=S[ls])
-        snap[(ls, total)] = dict(known["g"])
-        note("rem", ls, total, [(src, 0, 192)], [])
-        loc_done.append((ls, total))
+            tr.append((rid, pid, sum(1 << e for e in es[i * m:(i + 1) * m]), land, rs))
+        sent.append((ls, m * len(outs)))
 
-    def landed(land, sem, val):
-        note("rem", sem, val, [], [(land, 0, 192)])
+        def issue():
+            if len(tr) == 1:
+                rid, pid, mask, land, rs = tr[0]
+                g.remote_dma(T[land][:], T[src][:, 0:192], S[rs], S[ls], pid, rid, mask)
+            else:
+                g.remote_dma_fused([RemoteDMATransfer(dst_ids=[DstId(rid=rid, pnc=pid)], dma_engine_mask=mask, remote_sem=S[rs],
+                                                      src=T[src][:, 0:192], dst=T[land][:]) for rid, pid, mask, land, rs in tr], local_sem=S[ls])
+            return (ls, m * len(outs))
+        me = put("g", 0.3, late, [], [R(src, 0, 192)], issue)
+        for d, land, rs in outs:
+            put("x", 0.0, 0.0, [R(land)], [], (rs, m), False, [me])
+        return me
+
+    def order():
+        n = len(calls)
+        way, users, left = [0.0] * n, [[] for _ in calls], [len(c[5]) for c in calls]
+        for i, c in enumerate(calls):
+            for d in c[5]:
+                users[d].append(i)
+        for i in range(n - 1, -1, -1):
+            way[i] = calls[i][2] + max([way[u] + WAKE for u in users[i]] + [0.0])
+        ready, free, out = [0.0] * n, {q: 0.0 for q in "vapgsx"}, []
+        can = {q: [i for i in range(n) if calls[i][0] == q and not left[i]] for q in free}
+        while len(out) < n:
+            t, q = min((max(free[q], min(ready[i] for i in lst)), q) for q, lst in can.items() if lst)
+            i = max((i for i in can[q] if ready[i] <= t + SLACK), key=lambda i: (way[i], -i))
+            can[q].remove(i)
+            t = max(t, ready[i])
+            free[q] = t + calls[i][1]
+            out.append(i)
+            for u in users[i]:
+                ready[u] = max(ready[u], t + calls[i][2] + (0.0 if q == "x" or q == calls[u][0] == "p" else WAKE))
+                left[u] -= 1
+                if not left[u]:
+                    can[calls[u][0]].append(u)
+        return out
+
+    def issue_all():
+        count = {q: 0 for q in "vapg"}
+        known = {q: {} for q in queue}
+        snap, done = {}, {}
+        for i in order():
+            q, _, _, lab, issue, deps = calls[i]
+            if q == "x":
+                done[i] = issue
+                continue
+            want = {}
+            for d in deps:
+                if not q == calls[d][0] == "p":
+                    sem, val = done[d]
+                    want[sem] = max(want.get(sem, 0), val)
+            k = known[q]
+            for sem, val in sorted(want.items(), key=lambda d: -len(snap.get(d, {}))):
+                if k.get(sem, 0) < val:
+                    queue[q].wait_ge(S[sem], val)
+                    for s2, v2 in snap.get((sem, val), {}).items():
+                        k[s2] = max(k.get(s2, 0), v2)
+                    k[sem] = val
+            r = issue()
+            if not isinstance(r, tuple):
+                count[q] += 1
+                r.then_inc(S["q" + q], 1)
+                r = ("q" + q, count[q])
+            done[i] = r
+            snap[r] = dict(k)
+        return count
 
     up1, up2 = (rank + 1) % n_ranks, (rank + 2) % n_ranks
     dn1, dn2 = (rank - 1) % n_ranks, (rank - 2) % n_ranks
-    n16 = len(topo.engines(core, T.cores[up1]))
 
-    dma("s", R("mi32"), ext(T.m0))
-    dma("s", R("X", 0, 4096), ext(T.x0))
-    dma("a", R("od"), ext(T.own0))
+    dma("s", R("mi32"), hbm("m0"), 2.5)
+    dma("s", R("X", 0, 4096), hbm("x0"), 6.0)
+    dma("a", R("od"), hbm("own0"), 2.5)
     ms(R("thi"), 0)
-    dma("a", (T.thi[0:128:16, 0:1], [("thi", 0, 8)]), ext(T.th))
-    dma("s", R("nbw"), ext(T.nb))
+    dma("a", (T.thi[0:128:16, 0:1], [("thi", 0, 8)]), hbm("th"), 8.0)
+    cp(R("oR0"), R("mi32"))
+    first = send("oR0", [(up1, "oI0", "rM")], 4.0)
     ms(R("ONE"), 1.0)
     iota(R("pI"), [[0, 1]], 0, 1, False)
     iota(R("cc"), [[1, 16]])
@@ -225,17 +274,16 @@ def rank_program(g, core, T, topo):
     ms(R("m01", 0, 768, 16), 0.0)
     ms(R("m512"), 0.0)
     ms(R("m512", 0, 768, 16), 512.0)
-    for i in range(3):
-        act(R("ow", 768 * i, 768 * i + 768), R("m01"), AF.Copy, 0.0, 0.0)
-    cp(R("oR0"), R("mi32"))
-    send("oR0", [(up1, "oI0", "rM")])
-    landed("oI0", "rM", n16)
-    iota(R("ow", 2304, 4288), [[0, 1984]])
+    for lo in range(0, 4288, 768):
+        hi = min(lo + 768, 4288)
+        act(R("ow", lo, hi), R("m512", 0, hi - lo), AF.Copy, 0.0, 0.0)
     iota(R("krow"), [[0, 12], [1, 16]], -15)
     iota(R("kap"), [[0, 8], [-1, 16]], 15)
     iota(R("kan"), [[0, 8], [1, 16]], -15)
-    select(R("EX", p=96), R("EX", p=96), [[-1, 96], [0, 16]], OP.is_equal, 0, 1)
-    ms(R("CZ"), 0.0)
+    for i in range(3):
+        select(R("EX", 512 * i, 512 * i + 512, 1, 96), R("EX", 512 * i, 512 * i + 512, 1, 96), [[-1, 32], [0, 16]], OP.is_equal, -32 * i, 1)
+    for i in range(2):
+        ms(R("CZ", 768 * i, 768 * i + 768), 0.0)
     ts(R("pJ"), R("pI"), 15, OP.bitwise_and)
     cp(R("p15"), R("pJ"))
     ts(R("EQm"), R("cc"), R("p15"), OP.is_equal)
@@ -250,63 +298,60 @@ def rank_program(g, core, T, topo):
     for j in range(16):
         act(R("FK", 128 * j, 128 * j + 128), R("BLK"), AF.Copy, 0.0, R("EQm", j, j + 1))
     cp(R("ob"), R("od"))
-    dma("s", (T.ow[0:128:16, 0:4096], [("ow", 0, 4096)]), R("ob"))
+    dma("s", (T.ow[0:128:16, 0:4096], [("ow", 0, 4096)]), R("ob"), 5.0)
+    dma("s", R("nbw"), (T.nb[:], [("ob", 0, 1), ("oR0", 0, 1)]), 10.0)
     ms(R("mB"), 0.0)
     ms(R("mB", 0, 192, 16), BIG)
     ms(R("mD"), 2.0)
     ms(R("mD", 0, 192, 16), -BIG)
     ts(R("BK8"), R("BLK"), 8192.0, OP.mult)
-
-    def late_constants():
-        for r in range(1, 16):
-            act(R("LO", 128 * r, 128 * r + 128), R("BLK"), AF.Copy, 0.0, R("LTm", r, r + 1))
-        cp(R("IDf"), R("ID"))
-        ms(R("X", 4096, 4288), 0.0)
-        ms(R("MR0", 192, 384), 0.0)
-        ms(R("MR1", 192, 384), 0.0)
-        cp(R("MR0", 0, 192), R("mi32"))
-        iota(R("aC", 0, 12), [[16, 12]], 2049)
-        iota(R("aC", 12, 24), [[16, 12]], -1855)
-        ts(R("aC"), R("aC"), R("p15"), OP.add, -0.5, OP.add)
-        cp(R("e0"), R("EQm", 0, 1))
-        ts(R("e192"), R("EQm", 0, 1), 192.0, OP.mult)
-        ts(R("eB"), R("EQm", 0, 1), -192.0 * 191.0, OP.mult)
-        ts(R("th16"), R("thi", 0, 1), -2048.0, OP.add)
-        mm(R(B7, 0, 1), R("BLK"), R("th16"), True, True)
-        ts(R("lim0"), R(B7, 0, 1), 32.0, OP.mult, 32.0 * 32768.0 - 15.5, OP.add)
+    for r in range(1, 16):
+        act(R("LO", 128 * r, 128 * r + 128), R("BLK"), AF.Copy, 0.0, R("LTm", r, r + 1))
+    cp(R("IDf"), R("ID"))
+    ms(R("X", 4096, 4288), 0.0)
+    ms(R("MR0", 192, 384), 0.0)
+    ms(R("MR1", 192, 384), 0.0)
+    cp(R("MR0", 0, 192), R("mi32"))
+    iota(R("aC", 0, 12), [[16, 12]], 2049)
+    iota(R("aC", 12, 24), [[16, 12]], -1855)
+    ts(R("aC"), R("aC"), R("p15"), OP.add, -0.5, OP.add)
+    cp(R("e0"), R("EQm", 0, 1))
+    ts(R("e192"), R("EQm", 0, 1), 192.0, OP.mult)
+    ts(R("eB"), R("EQm", 0, 1), -192.0 * 191.0, OP.mult)
+    ts(R("th16"), R("thi", 0, 1), -2048.0, OP.add)
+    mm(R(B4, 0, 1), R("BLK"), R("th16"), True)
+    ts(R("lim0"), R(B4, 0, 1), 32.0, OP.mult, 32.0 * 32768.0 - 15.5, OP.add)
 
     def part(name, q, step=1):
         return R(name, 768 * q, 768 * q + 768, step)
 
     def gather(v, off, lo, hi, eng=act):
-        eng(R(v, 16 * lo, 16 * hi), IND("X", 0, 4096, off, lo, hi))
+        eng(R(v, 16 * lo, 16 * hi), IND("X", 4096, off, lo, hi))
 
-    def row(bank, n, l, r="one", start=True, stop=False):
-        mm(R(bank, 0, n), R(l, 0, 128), R(r, 0, n), start, stop)
+    def row(bank, n, l, r="one", start=True):
+        mm(R(bank, 0, n), R(l, 0, 128), R(r, 0, n), start)
 
-    def group_sum(bank, src, w, j0, j1, stop=False):
+    def group_sum(bank, src, w, j0=0, j1=16):
         for j in range(j0, j1):
-            mm(R(bank, 0, 192), R(w, 15 - j, 143 - j), R(src, 192 * j, 192 * j + 192), False, stop and j == j1 - 1)
+            mm(R(bank, 0, 192), R(w, 15 - j, 143 - j), R(src, 192 * j, 192 * j + 192))
 
     def from_keys(bank, src):
         for j in range(16):
-            mm(R(bank, 12 * j, 12 * j + 12), R("FK", 128 * j, 128 * j + 128), src, False, j == 15)
+            mm(R(bank, 12 * j, 12 * j + 12), R("FK", 128 * j, 128 * j + 128), src)
 
     def to_list(bank, src, w, n=192, start=False):
         for j in range(16):
-            mm(R(bank, 0, n // 16), R(w, 15 - j, 143 - j), R(src, j, n, 16), start and j == 0, j == 15)
+            mm(R(bank, 0, n // 16), R(w, 15 - j, 143 - j), R(src, j, n, 16), start and j == 0)
 
-    def extremes(v, mx, mn, q):
+    def centres(v, mx, mn, cx, q):
         scan(part(mx, q), R("m01"), part(v, q), OP.mult, OP.max)
         scan(part(mn, q), R("m512"), part(v, q), OP.add, OP.min)
         bank = PSUM[6 + q % 2]
         row(bank, 48, "cq")
         mm(R(bank, 0, 48), R("IDh"), R(mx, 768 * q + 15, 768 * q + 768, 16))
-        mm(R(bank, 0, 48), R("IDh"), R(mn, 768 * q + 15, 768 * q + 768, 16), False, True)
-
-    def centres(cx, q):
-        ts(R("CZ", 0, 768, 16), R(PSUM[6 + q % 2], 0, 48), R1, OP.add, R1, OP.subtract)
-        scan(part(cx, q), R("m01"), R("CZ"), OP.mult, OP.add)
+        mm(R(bank, 0, 48), R("IDh"), R(mn, 768 * q + 15, 768 * q + 768, 16))
+        ts(part("CZ", q % 2, 16), R(bank, 0, 48), R1, OP.add, R1, OP.subtract)
+        scan(part(cx, q), R("m01"), part("CZ", q % 2), OP.mult, OP.add)
 
     def larger(v, cx, d, q):
         tt(part(v, q, 16), part(v, q, 16), part(cx, q, 16), OP.max)
@@ -319,13 +364,12 @@ def rank_program(g, core, T, topo):
         scan(R(f, at, at + 192), R("mD"), R(bank, 0, 192), OP.add, OP.max)
 
     def rest(o, f, lo, hi, turn=False):
-        n = (hi - lo) // 16
-        ends = R(f, lo + 15, hi, 16)
-        ts(R("rr", 0, n), ends, R32, OP.add, R32, OP.subtract)
+        ends, r = R(f, lo + 15, hi, 16), R("rS" if f == "FS" else "rK", lo // 16, hi // 16)
+        ts(r, ends, R32, OP.add, R32, OP.subtract)
         if turn:
-            tt(o, R("rr", 0, n), ends, OP.subtract)
+            tt(o, r, ends, OP.subtract)
         else:
-            tt(o, ends, R("rr", 0, n), OP.subtract)
+            tt(o, ends, r, OP.subtract)
 
     def clamp(o, bank):
         ts(o, R(bank, 0, 192), -0.25, OP.max, 0.25, OP.min)
@@ -336,203 +380,156 @@ def rank_program(g, core, T, topo):
         last = t == 1
         KI, KR, KE, KB = B0, B1, B2, B3
         lim = R("lim" if t else "lim0")
-        gather("VR", oR, 0, 48)
         gather("VI", oI, 144, 192, cp)
         for q in range(3):
             gather("VI", oI, 48 * q, 48 * q + 48)
-        for q in range(1, 4):
+        for q in range(4):
             gather("VR", oR, 48 * q, 48 * q + 48)
         for bank in (KI, KE, KR, KB):
             row(bank, 192, "one", "krow")
-        order = (3, 0, 1, 2)
-        for i in range(5):
-            if i < 4:
-                group_sum(KI, "VI", "Wm", 4 * order[i], 4 * order[i] + 4)
-                extremes("VI", "XI", "NI", order[i])
-            if i == 0:
-                ts(R("M16"), R(oI), -2048.0, OP.add)
-            if i > 0:
-                q = order[i - 1]
-                centres("CXI", q)
-                larger("VI", "CXI", "DA", q)
-                group_sum(KI, "DA", "W64", 4 * q, 4 * q + 4, i == 4)
-        if t == 0:
-            late_constants()
-        extremes("VR", "XR", "NR", 0)
+        group_sum(KI, "VI", "Wm")
+        group_sum(KR, "VR", "Wm")
+        ts(R("M16"), R(oI), -2048.0, OP.add)
+        for q in (3, 0, 1, 2):
+            centres("VI", "XI", "NI", "CXI", q)
+            larger("VI", "CXI", "DA", q)
+        group_sum(KI, "DA", "W64")
+        group_sum(KE, "CXI", "Wm")
+        for q in range(4):
+            centres("VR", "XR", "NR", "CXR", q)
+            larger("VR", "CXR", "DR", q)
+        group_sum(KR, "DR", "W64")
         least("FK1", 0, KI)
         row(B4, 192, "kap")
         mm(R(B4, 0, 192), R("I13"), R("M16"))
         rest(R("VV", 24, 36), "FK1", 0, 192)
         from_keys(B4, R("VV", 24, 36))
-        centres("CXR", 0)
-        clamp(R("S0"), B4)
+        clamp(R("S2"), B4)
         row(B5, 12, "cm")
         row(B5, 12, "ch", "one", False)
-        to_list(B5, "S0", "W8")
-        extremes("VR", "XR", "NR", 1)
-        ts(R("rr", 0, 12), R(B5, 0, 12), R4096, OP.add, R4096, OP.subtract)
-        tt(R("SW", 0, 12), R(B5, 0, 12), R("rr", 0, 12), OP.subtract)
+        to_list(B5, "S2", "W8")
+        ts(R("rs"), R(B5, 0, 12), R4096, OP.add, R4096, OP.subtract)
+        tt(R("SW", 0, 12), R(B5, 0, 12), R("rs"), OP.subtract)
         ts(R("sL"), R("SW", 0, 12), MID, OP.add)
-        act(R("b0"), IND("ow", 0, 4096, "sL", 0, 12))
-        cp(R("nL"), IND("nbw", 0, 4096, "sL", 0, 12))
+        act(R("b0"), IND("ow", 4096, "sL"))
+        cp(R("nL"), IND("nbw", 4096, "sL"))
+        largest("FK1", 192, KI)
+        largest("FK1", 384, KR)
+        rest(R("UU", 24, 36), "FK1", 192, 384)
+        rest(R("kR"), "FK1", 384, 576, True)
+        for i in range(6):
+            gather("V2", "nL", 32 * i, 32 * i + 32)
         to_list(B5, "b0", "W1", 192, True)
-        mm(R(B4, 0, 192), R("BLK"), R("b0"), True, True)
-        gather("V2", "nL", 0, 32)
+        mm(R(B4, 0, 192), R("BLK"), R("b0"), True)
         act(R("bf"), R(B4, 0, 192))
-        group_sum(KE, "CXI", "Wm", 0, 16)
-        centres("CXR", 1)
-        extremes("VR", "XR", "NR", 2)
-        ts(R("SW", 12, 24), R(B5, 0, 12), -MID, OP.add)
         ts(R("Lc"), R(B5, 0, 12), 16.0, OP.mult)
+        ts(R("SW", 12, 24), R(B5, 0, 12), -MID, OP.add)
         cp(R("Lb"), R(B5, 0, 12))
-        gather("V2", "nL", 32, 64)
-        extremes("VR", "XR", "NR", 3)
-        group_sum(KR, "VR", "Wm", 0, 16)
-        centres("CXR", 2)
-        centres("CXR", 3)
-        gather("V2", "nL", 64, 96)
-        act_gather_pool("Cb", "CXR", 3072, "Lc")
+        act(R("Cb"), IND("CXR", 3072, "Lc"))
         for h in (0, 1):
-            mm(R(B4, 128 * h, 128 * h + 128, 1, 96), R("Cb", 96 * h, 96 * h + 96), R("ID"), True, True)
-        gather("V2", "nL", 96, 128)
+            mm(R(B4, 128 * h, 128 * h + 128, 1, 96), R("Cb", 96 * h, 96 * h + 96), R("ID"), True)
         act(R("CT", p=96), R(B4, 0, 256, 1, 96))
+        ts(R("n16"), R("nL"), -2048.0, OP.add)
         for c in range(12):
             ts(R("EQ", 208 * c, 192 * c + 192), R("bf", 16 * c, 192), -MID, OP.add, R("SW", 12 + c, 13 + c), OP.is_equal)
         row(B6, 192, "zrow")
         for c in range(11):
             mm(R(B6, 16 * c + 16, 192), R("BLK"), R("EQ", 208 * c + 16, 192 * c + 192))
         for r in range(1, 16):
-            mm(R(B6, r, 192, 16), R("LO", 128 * r, 128 * r + 128), R("EQ", r, 2304, 208), False, r == 15)
-        gather("V2", "nL", 128, 160)
-        gather("V2", "nL", 160, 192)
+            mm(R(B6, r, 192, 16), R("LO", 128 * r, 128 * r + 128), R("EQ", r, 2304, 208))
+        for h in (0, 1):
+            act(R("cnt", 192 * h, 192 * h + 192), R(B6, 0, 192))
+        mm(R(B7, 0, 24), R("IDf"), R("SW"), True)
+        to_list(B7, "cnt", "W8", 384)
+        tt(R("l1"), R(B7, 0, 24), R("aC"), OP.min)
+        ts(R("LS"), R("l1"), MID, OP.add)
+        row(B7, 192, "kap")
+        from_keys(B7, R("kR"))
+        act(R("QR"), R(B7, 0, 192), AF.Square)
+        act(R("QG"), IND("QR", 192, "Lb"))
+        act(R("Mg"), IND(MR, 192, "Lb"))
+        group_sum(KE, "V2", "Wm")
+        for i in range(6):
+            bank = PSUM[4 + i % 2]
+            mm(R(bank), R("ID"), R("V2", 512 * i, 512 * i + 512), True)
+            mm(R(bank), R("CT", 128 * (i // 3), 128 * (i // 3) + 128, 1, 96), R("EX", 512 * (i % 3), 512 * (i % 3) + 512, 1, 96))
+            act(R("DB", 512 * i, 512 * i + 512), R(bank), AF.Abs)
+        group_sum(KB, "DB", "W32")
         for q in range(4):
-            larger("VR", "CXR", "DR", q)
-        group_sum(KE, "V2", "Wm", 0, 8)
-        blocks = (0, 2, 5, 8, 10, 13, 16)
-        for i in range(7):
-            if i < 6:
-                bank = PSUM[4 + i % 2]
-                mm(R(bank), R("ID"), R("V2", 512 * i, 512 * i + 512), True)
-                mm(R(bank), R("CT", 128 * (i // 3), 128 * (i // 3) + 128, 1, 96), R("EX", 512 * (i % 3), 512 * (i % 3) + 512, 1, 96), False, True)
-                act(R("DB", 512 * i, 512 * i + 512), R(bank), AF.Abs)
-            if i == 0:
-                for h in (0, 1):
-                    act(R("cnt", 192 * h, 192 * h + 192), R(B6, 0, 192))
-                group_sum(KR, "DR", "W64", 0, 8)
-            if i == 1:
-                group_sum(KE, "V2", "Wm", 8, 16)
-                mm(R(B7, 0, 24), R("IDf"), R("SW"), True)
-                to_list(B7, "cnt", "W8", 384)
-            if i == 2:
-                group_sum(KR, "DR", "W64", 8, 16, True)
-                largest("FK1", 192, KI)
-                ts(R("n16"), R("nL"), -2048.0, OP.add)
-                for q in (0, 1):
-                    larger("V2", "CXI", "D2", q)
-                tt(R("l1"), R(B7, 0, 24), R("aC"), OP.min)
-                ts(R("LS"), R("l1"), MID, OP.add)
-                largest("FK1", 384, KR)
-                rest(R("UU", 24, 36), "FK1", 192, 384)
-                rest(R("kR"), "FK1", 384, 576, True)
-            if i == 3:
-                group_sum(KE, "D2", "W64", 0, 8)
-            if i == 5:
-                for q in (2, 3):
-                    larger("V2", "CXI", "D2", q)
-                row(B7, 192, "kap")
-                from_keys(B7, R("kR"))
-            if i > 0:
-                group_sum(KB, "DB", "W32", blocks[i - 1], blocks[i], i == 6)
-        group_sum(KE, "D2", "W64", 8, 16, True)
-        act(R("FM", 192, 384), R(KB, 0, 192), AF.Sign, lim, -1.0)
-        row(B0, 192, "kan")
-        mm(R(B0, 0, 192), R("I13"), R("n16"))
-        row(B1, 192, "kap")
-        mm(R(B1, 0, 192), R("I13"), R("n16"))
+            larger("V2", "CXI", "D2", q)
+        group_sum(KE, "D2", "W64")
+        if not last:
+            act(R("xg"), IND("X", 4096, "sL"), AF.Relu, -16.0)
+            cp(IND("X", 4288, "LS"), R("xg"))
+        for bank, l in ((B0, "kan"), (B1, "kap")):
+            row(bank, 192, l)
+            mm(R(bank, 0, 192), R("I13"), R("n16"))
         row(B4, 192, "kap")
         mm(R(B5, 0, 192), R("IDn"), R("cnt", 0, 192), True)
         row(B6, 192, "cI")
         mm(R(B6, 0, 192), R("IDk"), R("cnt", 0, 192))
-        largest("FS", 384, KB)
-        least("FS", 576, KB)
-        act(R("FM", 0, 192), R(KE, 0, 192), AF.Sign, lim, -1.0)
-        act(R("QR"), R(B7, 0, 192), AF.Square)
-        rest(R("VV", 0, 24), "FS", 384, 768)
-        least("FS", 0, KE)
-        largest("FS", 192, KE)
-        scan(R("CN"), R("m01", 0, 384), R("FM"), OP.mult, OP.add)
-        act_gather_pool("QG", "QR", 192, "Lb")
-        act_gather_pool("Mg", MR, 192, "Lb")
-        if not last:
-            act(R("xg"), IND("X", 0, 4096, "sL", 0, 12), AF.Relu, -16.0)
-        rest(R("UU", 0, 24), "FS", 0, 384)
-        tt(R("won"), R("CN", 15, 192, 16), R("CN", 207, 384, 16), OP.is_gt)
-        tt(R("SS"), R("UU"), R("VV"), OP.add)
-        for i in (0, 2, 1):
-            tt(R("PP", 12 * i, 12 * i + 12), R("SS", 12 * i, 12 * i + 12), R("won"), OP.mult)
-        tt(R("RR"), R("VV"), R("PP"), OP.subtract)
         row(B7, 192, "cR")
         mm(R(B7, 0, 192), R("IDk"), R("QG"))
-        from_keys(B0, R("RR", 0, 12))
-        from_keys(B4, R("RR", 24, 36))
+        for i, bank in enumerate((KE, KB)):
+            act(R("FM", 192 * i, 192 * i + 192), R(bank, 0, 192), AF.Sign, lim, -1.0)
+            scan(R("CN", 192 * i, 192 * i + 192), R("m01", 0, 192), R("FM", 192 * i, 192 * i + 192), OP.mult, OP.add)
+            least("FS", 576 * i, bank)
+            largest("FS", 192 + 192 * i, bank)
+            rest(R("VV" if i else "UU", 0, 24), "FS", 384 * i, 384 * i + 384)
+        tt(R("won"), R("CN", 15, 192, 16), R("CN", 207, 384, 16), OP.is_gt)
+        for i, bank in enumerate((B0, B1, B4)):
+            u, v, s, p, r = (R(n, 12 * i, 12 * i + 12) for n in ("UU", "VV", "SS", "PP", "RR"))
+            tt(s, u, v, OP.add)
+            tt(p, s, R("won"), OP.mult)
+            tt(r, v, p, OP.subtract)
+            from_keys(bank, r)
         clamp(R("S0"), B0)
-        act(R("QK"), R(B4, 0, 192), AF.Square)
-        from_keys(B1, R("RR", 12, 24))
-        mm(R(B6, 0, 192), R("BK8"), R("S0"))
-        mm(R(B6, 0, 192), R("IDk"), R("QK"), False, True)
         clamp(R("S1"), B1)
+        act(R("QK"), R(B4, 0, 192), AF.Square)
+        mm(R(B6, 0, 192), R("BK8"), R("S0"))
+        mm(R(B6, 0, 192), R("IDk"), R("QK"))
         act(R(IC), R(B6, 0, 192), AF.Relu)
         if not last:
             send(IC, [(dn1, "inA", "rA"), (up1, "inB", "rB")])
         else:
             send(IC, [(dn2, "inC", "rC")])
-        mm(R(B7, 0, 192), R("BK8"), R("S1"), False, True)
-        from_keys(B5, R("won"))
+        mm(R(B7, 0, 192), R("BK8"), R("S1"))
         act(R("zr"), R(B7, 0, 192), AF.Relu)
-        tt_scatter(IND(MR, 0, 384, "LS", 12, 24), R("zr"), R("Mg"), OP.max)
+        tt(IND(MR, 384, "LS", 12, 24), R("zr"), R("Mg"), OP.max)
         if not last:
             send(MR, [(up2, "inM", "rR")])
+        from_keys(B5, R("won"))
         act(R("wf"), R(B5, 0, 192), AF.Relu, acc=R("wc"))
         mm(R(B2, 0, 192), R("BLK"), R("b0"), True)
-        mm(R(B2, 0, 192), R("ID"), R("wf"), False, True)
-        if not last:
-            cp_scatter(IND("X", 0, 4288, "LS", 0, 12), R("xg"))
+        mm(R(B2, 0, 192), R("ID"), R("wf"))
         act(R("xa"), R(B2, 0, 192), AF.Copy, 0.0, R("e0"))
         act(R("ya"), R(B2, 0, 192), AF.Relu, R("eB"), R("e192"))
-        tt_scatter(IND("ow", 0, 4288, "LS", 0, 12), R("xa"), R("ya"), OP.subtract)
-        if last:
-            dma("a", (T.yown[:], []), (T.ow[0:128:16, 0:4096], [("ow", 0, 4096)]))
-            return
-        act(R("wb"), R("wc"))
-        mm(R(B3, 0, 1), R("ONE"), R("wb"), True, True)
+        tt(IND("ow", 4288, "LS"), R("xa"), R("ya"), OP.subtract)
+        if not last:
+            act(R("wb"), R("wc"))
+            mm(R(B3, 0, 1), R("ONE"), R("wb"), True)
+            ts(R("wi"), R(B3, 0, 1), 0.0625, OP.mult)
+            ts(R("wj"), R("wi"), 63, OP.bitwise_and)
+            ts(R("lim"), R("wj"), 32.0, OP.mult, R("lim0"), OP.add)
 
-    def act_gather_pool(o, win, n, off):
-        act(R(o), IND(win, 0, n, off, 0, 12))
-
-    def merged(old, new, words):
-        tt(R("mv"), R(old, 0, 192), R(new), OP.max)
-        ts(R(words), R("mv"), 4095, OP.bitwise_and)
+    def merged(old, new, both, words):
+        tt(R(both), R(old, 0, 192), R(new), OP.max)
+        ts(R(words), R(both), 4095, OP.bitwise_and)
 
     play(0)
-    landed("inA", "rA", n16 // 2)
-    landed("inB", "rB", n16 // 2)
-    landed("inM", "rR", n16)
-    ts(R("wi"), R(B3, 0, 1), 0.0625, OP.mult)
-    ts(R("wj"), R("wi"), 63, OP.bitwise_and)
-    ts(R("lim"), R("wj"), 32.0, OP.mult, R("lim0"), OP.add)
-    merged("MR0", "inA", "mi32")
+    merged("MR0", "inA", "mv", "mi32")
     cp(R("oR1"), R("mi32"))
-    merged("inM", "inB", "mw")
-    cp(R("oI1"), R("mw"))
     cp(R("MR1", 0, 192), R("mi32"))
+    merged("inM", "inB", "mu", "mw")
+    cp(R("oI1"), R("mw"))
     play(1)
-    landed("inC", "rC", n16)
-    merged("MR1", "inC", "mi32")
+    merged("MR1", "inC", "mv", "mi32")
     cp(R("yo"), R("mi32"))
-    dma("s", (T.ym[:], []), R("yo"))
-    for q in ("v", "a", "p", "g"):
+    stores = [dma("a", hbm("yown"), (T.ow[0:128:16, 0:4096], [("ow", 0, 4096)]), 2.5), dma("s", hbm("ym"), R("yo"), 2.5)]
+    count = issue_all()
+    for q in count:
         g.wait_ge(S["q" + q], count[q])
-    for sem, val in loc_done:
+    for sem, val in sent:
         g.wait_ge(S[sem], val)
-    g.wait_ge(S["d%d" % (ndma[0] - 2)], 16)
-    g.sync.wait_ge(S["d%d" % (ndma[0] - 1)], 16)
+    g.wait_ge(S[stores[0]], 16)
+    g.sync.wait_ge(S[stores[1]], 16)

@@ -1,3 +1,4 @@
+import numpy as np
 from concourse.bass import DstId, RemoteDMATransfer
 from concourse.mybir import AluOpType, ActivationFunctionType
 
@@ -10,22 +11,27 @@ KILL = float(2 ** 18)
 R1, R32, R4096 = 1.5 * 2 ** 23, 1.5 * 2 ** 28, 1.5 * 2 ** 35
 MID = 2047.5
 CYCLE, WAKE, SLACK, HOP = 0.00087, 0.12, 0.05, 2.5
+ORDER = []
+FLAGS = dict(n1=24, n2=16, ai=(0,), ar=(0,), oi=(0, 1, 2, 3))
+SECOND = 1.0
+URGENT = {}
 
 OWN_TILES = {
     F32: "ow:4288 IC0:192 IC1:192 MR0:384 MR1:384 inA:192 inB:192 inM:192 inC:192 yo:192 ob:256",
     BF: "X:4288 VI:3072 VR:3072 V2:3072 XI:3072 NI:3072 XR:3072 NR:3072 CXI:3072 CXR:3072 DA:3072 DR:3072 D2:3072 DB:3072 "
-        "CZ:1536 m01:768 m512:768 FK:2048 LO:2048 EX:1536 EQ:2304 QR:192",
+        "CZI:3072 CZR:3072 m01:768 m512:768 LO:2048 EX:1536 EQ:2304 QR:192",
     I32: "nbw:4096 od:256 mi32:192 thi:8",
     U16: "oR0:192 oI0:192",
 }
 POOLS = {
-    F32: "p15:1 e0:1 e192:1 eB:1 cc:16 aC:24 EQm:16 LTm:16 IDf:128 FS:768 FK1:576 rS:48 rK:36 rs:12 SW:24 l1:24 Mg:192 zr:192 xa:192 ya:192 "
-         "wc:1 lim0:1 lim:1",
-    BF: "ONE:128 BLK:128 BK8:128 ID:128 IDh:128 I13:128 IDk:128 IDn:128 W64:144 W32:144 Wm:144 W1:144 W8:144 mB:192 mD:192 "
-        "krow:192/1 kap:128/1 kan:128/1 cq:128/1 cm:128/1 ch:128/1 cI:128/1 cR:128/1 one:192/1 zrow:128/1 "
-        "UU:36 VV:36 SS:36 PP:36 RR:36 kR:12 won:12 b0:192 bf:192 cnt:384 Cb:192 CT:256 QG:192 QK:192 FM:384 CN:384 wf:192 wb:1 xg:192",
-    F16: "M16:192 n16:192 S0:192 S1:192 S2:192 th16:1",
-    I32: "pI:1 pJ:1 wi:1 wj:1 mw:192 mv:192 mu:192",
+    F32: "p15:1 kc:1 e0:1 e192:1 eB:1 cc:16 aC:24 LTm:16 IDf:128 FS:1024/96 FK:768/96 rS:64/96 rK:48/96 rs:12 SW:24 l1:24 Mg:192 zr:192 "
+         "xa:192 ya:192 wc:1 lim:1/96",
+    BF: "ONE:128 BLK:128 BK8:128 ID:128 I13:128 IDk:128 IDn:128 G64:8 G32:8 Gm:8 W1:144 W8:144 mB:256/96 mD:256/96 "
+        "krow:256/1 TR:256/3 thd:3 e3:3/1 kap:128/1 kan:128/1 cm:128/1 ch:128/1 cI:128/1 cR:128/1 one:192/1 zrow:128/1 "
+        "UU:48/96 VV:32/96 SS:48/96 PP:48/96 ZZ:1536/96 ZX:1536/96 b0:192 bf:192 cnt:384 Cb:192 CT:256 QG:192 QK:192 FM:512/96 CN:512/96 "
+        "wf:192 wb:1 xg:192 CTI:256 CTR:256",
+    F16: "IDh:128 M16:192 n16:192 S0:192 S1:192 S2:192",
+    I32: "pI:1 pJ:1 wi:1/96 wj:1/96 td:2 mw:192 mv:192 mu:192",
     U16: "oI1:192 oR1:192 sL:12 nL:192 Lb:12 Lc:12 LS:24",
 }
 SCRATCH, SHAPE, PLACE = {}, {}, {}
@@ -87,7 +93,7 @@ def rank_program(g, core, T, topo):
         for lst, w in ((rd, False), (wr, True)):
             for name, lo, hi in lst:
                 for e in seen.get(name, ()):
-                    if name in PSUM and (q != e[1] or q == "p"):
+                    if name in PSUM and (q != e[1] or q in ("p", "av")):
                         hit = not (adds and e[5])
                     else:
                         hit = (w or e[0]) and e[3] < hi and lo < e[4]
@@ -138,18 +144,23 @@ def rank_program(g, core, T, topo):
         else:
             emit("a", lambda: g.scalar.activation(o[0], a[0], func, bias=ap(bias), scale=ap(scale), accum_out=acc[0]), [o, acc], [a, bias, scale])
 
-    def mm(o, l, r, start=False):
-        bank = o[1][0][0]
+    def mms(lst, start=False):
+        bank = lst[0][0][1][0][0]
         if start:
             group[bank] = [0]
         left = group[bank]
-        left[0] += 1
+        left[0] += len(lst)
 
         def issue():
-            left[0] -= 1
-            return g.tensor.matmul(o[0], l[0], r[0], start, left[0] == 0)
-        c = max(min(64, l[2]), r[2]) * (4 if l[3] == 4 else 1) * CYCLE / 2
-        put("p", c, c, [o], [l, r], issue, not start)
+            for i, (o, l, r) in enumerate(lst):
+                left[0] -= 1
+                ins = g.tensor.matmul(o[0], l[0], r[0], start and i == 0, left[0] == 0)
+            return ins
+        c = sum(max(min(64, l[2]), r[2]) * (4 if l[3] == 4 else 1) for o, l, r in lst) * CYCLE / 2
+        put("p", c, c, [m[0] for m in lst], [x for m in lst for x in m[1:]], issue, not start)
+
+    def mm(o, l, r, start=False):
+        mms([(o, l, r)], start)
 
     def iota(o, pat, base=0, cm=0, flag=True):
         kw = {"allow_small_or_imprecise_dtypes": True} if flag else {}
@@ -201,34 +212,42 @@ def rank_program(g, core, T, topo):
 
     def order():
         n = len(calls)
-        way, users, left = [0.0] * n, [[] for _ in calls], [len(c[5]) for c in calls]
+        users = [[] for _ in calls]
         for i, c in enumerate(calls):
             for d in c[5]:
                 users[d].append(i)
+        way = [0.0] * n
         for i in range(n - 1, -1, -1):
             way[i] = calls[i][2] + max([way[u] + WAKE for u in users[i]] + [0.0])
-        ready, free, out = [0.0] * n, {q: 0.0 for q in "vapgsx"}, []
-        can = {q: [i for i in range(n) if calls[i][0] == q and not left[i]] for q in free}
+        way = [w + URGENT.get(c[0] + "." + c[3][0], 0.0) - 1e-6 * i for i, (w, c) in enumerate(zip(way, calls))]
+        left, ready, free, out = [len(c[5]) for c in calls], [0.0] * n, {q: 0.0 for q in "vapgsx"}, []
+        can = {q: [i for i in range(n) if q in calls[i][0] and not left[i]] for q in free}
         while len(out) < n:
             t, q = min((max(free[q], min(ready[i] for i in lst)), q) for q, lst in can.items() if lst)
-            i = max((i for i in can[q] if ready[i] <= t + SLACK), key=lambda i: (way[i], -i))
-            can[q].remove(i)
+            i = max((i for i in can[q] if ready[i] <= t + SLACK), key=lambda i: way[i] - (0.0 if calls[i][0][0] == q else SECOND))
+            for e in calls[i][0]:
+                can[e].remove(i)
             t = max(t, ready[i])
             free[q] = t + calls[i][1]
-            out.append(i)
+            out.append((i, q))
             for u in users[i]:
                 ready[u] = max(ready[u], t + calls[i][2] + (0.0 if q == "x" or q == calls[u][0] == "p" else WAKE))
                 left[u] -= 1
                 if not left[u]:
-                    can[calls[u][0]].append(u)
+                    for e in calls[u][0]:
+                        can[e].append(u)
         return out
 
     def issue_all():
         count = {q: 0 for q in "vapg"}
         known = {q: {} for q in queue}
         snap, done = {}, {}
-        for i in order():
-            q, _, _, lab, issue, deps = calls[i]
+        if not ORDER:
+            ORDER.extend(order())
+        for i, q in ORDER:
+            qs, _, _, lab, issue, deps = calls[i]
+            if len(qs) > 1:
+                issue = issue[q]
             if q == "x":
                 done[i] = issue
                 continue
@@ -277,33 +296,36 @@ def rank_program(g, core, T, topo):
     for lo in range(0, 4288, 768):
         hi = min(lo + 768, 4288)
         act(R("ow", lo, hi), R("m512", 0, hi - lo), AF.Copy, 0.0, 0.0)
-    iota(R("krow"), [[0, 12], [1, 16]], -15)
+    iota(R("krow"), [[0, 16], [1, 16]], -15)
     iota(R("kap"), [[0, 8], [-1, 16]], 15)
     iota(R("kan"), [[0, 8], [1, 16]], -15)
     for i in range(3):
         select(R("EX", 512 * i, 512 * i + 512, 1, 96), R("EX", 512 * i, 512 * i + 512, 1, 96), [[-1, 32], [0, 16]], OP.is_equal, -32 * i, 1)
-    for i in range(2):
-        ms(R("CZ", 768 * i, 768 * i + 768), 0.0)
+    for i in range(4):
+        ms(R("CZI", 768 * i, 768 * i + 768), 0.0)
+        iota(R("CZR", 768 * i, 768 * i + 768), [[0, 768]])
     ts(R("pJ"), R("pI"), 15, OP.bitwise_and)
     cp(R("p15"), R("pJ"))
-    ts(R("EQm"), R("cc"), R("p15"), OP.is_equal)
+    ts(R("kc"), R("pJ"), -1.0, OP.mult, 15.0, OP.add)
     ts(R("LTm"), R("cc"), R("p15"), OP.is_gt)
-    for name, c in (("W64", 64.0), ("W32", 32.0), ("Wm", -32.0), ("W1", 1.0), ("W8", 8192.0)):
+    for name, c in (("W1", 1.0), ("W8", 8192.0)):
         ms(R(name), 0.0)
         ts(R(name, 15, 143, 16), R("BLK", 0, 128, 16), c, OP.mult)
-    for name, c in (("IDh", 0.5), ("I13", 2.0 ** -13), ("IDk", -KILL), ("IDn", -1.0)):
+    for name, c in (("G64", 64.0), ("G32", 32.0), ("Gm", -32.0)):
+        ts(R(name), R("BLK", 0, 128, 16), c, OP.mult)
+    for name, c in (("IDh", 511.0 / 1024.0), ("I13", 2.0 ** -13), ("IDk", -KILL), ("IDn", -1.0)):
         ts(R(name), R("ID"), c, OP.mult)
-    for name, c in (("one", 1.0), ("cq", -0.25), ("cm", -2048.0), ("ch", 0.5), ("cI", 163840.0), ("cR", 98304.0), ("zrow", 0.0)):
+    for name, c in (("one", 1.0), ("cm", -2048.0), ("ch", 0.5), ("cI", 163840.0), ("cR", 98304.0), ("zrow", 0.0)):
         ms(R(name), c)
-    for j in range(16):
-        act(R("FK", 128 * j, 128 * j + 128), R("BLK"), AF.Copy, 0.0, R("EQm", j, j + 1))
+    for i in range(2):
+        ms(R("ZZ", 768 * i, 768 * i + 768), 0.0)
     cp(R("ob"), R("od"))
     dma("s", (T.ow[0:128:16, 0:4096], [("ow", 0, 4096)]), R("ob"), 5.0)
     dma("s", R("nbw"), (T.nb[:], [("ob", 0, 1), ("oR0", 0, 1)]), 10.0)
     ms(R("mB"), 0.0)
-    ms(R("mB", 0, 192, 16), BIG)
+    ms(R("mB", 0, 256, 16), BIG)
     ms(R("mD"), 2.0)
-    ms(R("mD", 0, 192, 16), -BIG)
+    ms(R("mD", 0, 256, 16), -BIG)
     ts(R("BK8"), R("BLK"), 8192.0, OP.mult)
     for r in range(1, 16):
         act(R("LO", 128 * r, 128 * r + 128), R("BLK"), AF.Copy, 0.0, R("LTm", r, r + 1))
@@ -315,53 +337,109 @@ def rank_program(g, core, T, topo):
     iota(R("aC", 0, 12), [[16, 12]], 2049)
     iota(R("aC", 12, 24), [[16, 12]], -1855)
     ts(R("aC"), R("aC"), R("p15"), OP.add, -0.5, OP.add)
-    cp(R("e0"), R("EQm", 0, 1))
-    ts(R("e192"), R("EQm", 0, 1), 192.0, OP.mult)
-    ts(R("eB"), R("EQm", 0, 1), -192.0 * 191.0, OP.mult)
-    ts(R("th16"), R("thi", 0, 1), -2048.0, OP.add)
-    mm(R(B4, 0, 1), R("BLK"), R("th16"), True)
-    ts(R("lim0"), R(B4, 0, 1), 32.0, OP.mult, 32.0 * 32768.0 - 15.5, OP.add)
+    for name, c in (("e0", 1.0), ("e192", 192.0), ("eB", -192.0 * 191.0)):
+        ts(R(name), R("p15"), 0.0, OP.is_equal, c, OP.mult)
+    ts(R("td", 0, 1), R("thi", 0, 1), 6, OP.arith_shift_right)
+    ts(R("td", 1, 2), R("thi", 0, 1), 63, OP.bitwise_and)
+    ms(R("thd", 0, 1), 0.0)
+    ts(R("thd", 1, 2), R("td", 0, 1), -2048.0, OP.mult)
+    ts(R("thd", 2, 3), R("td", 1, 2), -32.0, OP.mult)
+    iota(R("e3"), [[-1, 3]], 1)
+    ts(R("e3"), R("e3"), 0.0, OP.max)
+    mms([(R(B5, 0, 128, 1, 3), R("thd"), R("BLK")), (R(B5, 0, 128, 1, 3), R("e3"), R("krow", 0, 128))], True)
+    for h in (0, 1):
+        cp(R("TR", 128 * h, 128 * h + 128), R(B5, 0, 128, 1, 3))
 
     def part(name, q, step=1):
         return R(name, 768 * q, 768 * q + 768, step)
 
-    def gather(v, off, lo, hi, eng=act):
-        eng(R(v, 16 * lo, 16 * hi), IND("X", 4096, off, lo, hi))
+    def either(o, a):
+        emit("av", {"a": lambda: g.scalar.activation(o[0], a[0], AF.Copy), "v": lambda: g.vector.tensor_copy(o[0], a[0])}, [o], [a])
+
+    def gather(v, off, n):
+        for lo in range(0, 192, n):
+            either(R(v, 16 * lo, 16 * (lo + n)), IND("X", 4096, off, lo, lo + n))
 
     def row(bank, n, l, r="one", start=True):
         mm(R(bank, 0, n), R(l, 0, 128), R(r, 0, n), start)
 
-    def group_sum(bank, src, w, j0=0, j1=16):
-        for j in range(j0, j1):
-            mm(R(bank, 0, 192), R(w, 15 - j, 143 - j), R(src, 192 * j, 192 * j + 192))
+    def group_sum(bank, src, w, halves=(0, 1)):
+        for h in halves:
+            for k0 in (0, 8):
+                mms([(R(bank, 128 * h + k, 128 * h + 128, 16, 96), R(src, 1536 * h + k, 1536 * h + 1536, 16), R(w)) for k in range(k0, k0 + 8)])
 
-    def from_keys(bank, src):
-        for j in range(16):
-            mm(R(bank, 12 * j, 12 * j + 12), R("FK", 128 * j, 128 * j + 128), src)
+    def Z(i):
+        return R("ZZ", 256 * i, 256 * i + 256, 16)
+
+    def from_keys(bank, i, start=False):
+        scan(R("ZX", 256 * i, 256 * i + 256), R("m01", 0, 256, 1, 96), R("ZZ", 256 * i, 256 * i + 256), OP.mult, OP.add)
+        lst = [(R(bank, 96 * h, 96 * h + 96), R("ZX", 256 * i + 128 * h, 256 * i + 128 * h + 128), R("ID", 0, 96, 1, 96)) for h in (0, 1)]
+        if start:
+            mms(lst[:1], True)
+            mms(lst[1:], True)
+        else:
+            mms(lst)
 
     def to_list(bank, src, w, n=192, start=False):
-        for j in range(16):
-            mm(R(bank, 0, n // 16), R(w, 15 - j, 143 - j), R(src, j, n, 16), start and j == 0)
+        mms([(R(bank, 0, n // 16), R(w, 15 - j, 143 - j), R(src, j, n, 16)) for j in range(16)], start)
 
-    def centres(v, mx, mn, cx, q):
+    turn = [0]
+
+    def extremes(v, mx, mn, q):
         scan(part(mx, q), R("m01"), part(v, q), OP.mult, OP.max)
         scan(part(mn, q), R("m512"), part(v, q), OP.add, OP.min)
-        bank = PSUM[6 + q % 2]
-        row(bank, 48, "cq")
-        mm(R(bank, 0, 48), R("IDh"), R(mx, 768 * q + 15, 768 * q + 768, 16))
-        mm(R(bank, 0, 48), R("IDh"), R(mn, 768 * q + 15, 768 * q + 768, 16))
-        ts(part("CZ", q % 2, 16), R(bank, 0, 48), R1, OP.add, R1, OP.subtract)
-        scan(part(cx, q), R("m01"), part("CZ", q % 2), OP.mult, OP.add)
+
+    def centres(mx, mn, cz, q, n=1):
+        turn[0] += 1
+        bank = PSUM[6 + turn[0] % 2]
+        o = R(bank, 0, 48 * n)
+        mms([(o, R("IDh"), R(m, 768 * q + 15, 768 * (q + n), 16)) for m in (mx, mn)], True)
+        ts(R(cz, 768 * q, 768 * (q + n), 16), R(bank, 0, 48 * n), R1, OP.add, R1, OP.subtract)
+
+    def turned(mx, mn, ct, h):
+        turn[0] += 1
+        o = R(PSUM[6 + turn[0] % 2], 0, 128, 1, 96)
+        mms([(o, R(m, 1536 * h + 15, 1536 * h + 1536, 16), R("IDh")) for m in (mx, mn)], True)
+        ts(R(ct, 128 * h, 128 * h + 128, 1, 96), o, R1, OP.add, R1, OP.subtract)
+
+    def spread(cz, cx, q):
+        scan(part(cx, q), R("m01"), part(cz, q), OP.mult, OP.add)
+
+    def apart(v, ct, d, h, banks):
+        for i in range(3 * h, 3 * h + 3):
+            bank = banks[i % 2]
+            mms([(R(bank), R("ID"), R(v, 512 * i, 512 * i + 512)),
+                 (R(bank), R(ct, 128 * h, 128 * h + 128, 1, 96), R("EX", 512 * (i % 3), 512 * (i % 3) + 512, 1, 96))], True)
+            act(R(d, 512 * i, 512 * i + 512), R(bank), AF.Abs)
+
+    def distances(bank, v, mx, mn, cz, cx, ct, d, by_act, order, all_centres):
+        group_sum(bank, v, "Gm", [h for h in (0, 1) if h not in by_act])
+        for q in order:
+            extremes(v, mx, mn, q)
+            if q // 2 not in by_act:
+                centres(mx, mn, cz, q)
+                spread(cz, cx, q)
+                larger(v, cx, d, q)
+            elif (q ^ 1) in order[:order.index(q)]:
+                turned(mx, mn, ct, q // 2)
+                apart(v, ct, d, q // 2, (B3, B4))
+        for h in (0, 1):
+            group_sum(bank, d, "G32" if h in by_act else "G64", [h])
+        for h in by_act:
+            centres(mx, mn, cz, 2 * h, 2)
+            if all_centres:
+                spread(cz, cx, 2 * h)
+                spread(cz, cx, 2 * h + 1)
 
     def larger(v, cx, d, q):
         tt(part(v, q, 16), part(v, q, 16), part(cx, q, 16), OP.max)
         scan(part(d, q), part(cx, q), part(v, q), OP.min, OP.max)
 
     def least(f, at, bank):
-        scan(R(f, at, at + 192), R("mB"), R(bank, 0, 192), OP.add, OP.min)
+        scan(R(f, at, at + 256), R("mB"), R(bank, 0, 256, 1, 96), OP.add, OP.min)
 
     def largest(f, at, bank):
-        scan(R(f, at, at + 192), R("mD"), R(bank, 0, 192), OP.add, OP.max)
+        scan(R(f, at, at + 256), R("mD"), R(bank, 0, 256, 1, 96), OP.add, OP.max)
 
     def rest(o, f, lo, hi, turn=False):
         ends, r = R(f, lo + 15, hi, 16), R("rS" if f == "FS" else "rK", lo // 16, hi // 16)
@@ -379,113 +457,101 @@ def rank_program(g, core, T, topo):
         IC, MR = "IC%d" % t, "MR%d" % t
         last = t == 1
         KI, KR, KE, KB = B0, B1, B2, B3
-        lim = R("lim" if t else "lim0")
-        gather("VI", oI, 144, 192, cp)
-        for q in range(3):
-            gather("VI", oI, 48 * q, 48 * q + 48)
-        for q in range(4):
-            gather("VR", oR, 48 * q, 48 * q + 48)
-        for bank in (KI, KE, KR, KB):
-            row(bank, 192, "one", "krow")
-        group_sum(KI, "VI", "Wm")
-        group_sum(KR, "VR", "Wm")
+        lim = R("lim") if t else -15.5
+
+        def opened(bank, n, rows):
+            mm(R(bank, 0, 256, 1, 96), R("ONE", 0, 96, 1, n), R(rows), True)
+        gather("VI", oI, FLAGS["n1"])
+        gather("VR", oR, FLAGS["n1"])
+        opened(KI, 1, "krow")
+        opened(KR, 1, "krow")
+        opened(KE, 3, "TR")
         ts(R("M16"), R(oI), -2048.0, OP.add)
-        for q in (3, 0, 1, 2):
-            centres("VI", "XI", "NI", "CXI", q)
-            larger("VI", "CXI", "DA", q)
-        group_sum(KI, "DA", "W64")
-        group_sum(KE, "CXI", "Wm")
-        for q in range(4):
-            centres("VR", "XR", "NR", "CXR", q)
-            larger("VR", "CXR", "DR", q)
-        group_sum(KR, "DR", "W64")
-        least("FK1", 0, KI)
-        row(B4, 192, "kap")
-        mm(R(B4, 0, 192), R("I13"), R("M16"))
-        rest(R("VV", 24, 36), "FK1", 0, 192)
-        from_keys(B4, R("VV", 24, 36))
-        clamp(R("S2"), B4)
+        distances(KI, "VI", "XI", "NI", "CZI", "CXI", "CTI", "DA", FLAGS["ai"], FLAGS["oi"], True)
+        group_sum(KE, "CXI", "Gm")
+        distances(KR, "VR", "XR", "NR", "CZR", "CXR", "CTR", "DR", FLAGS["ar"], (0, 1, 2, 3), False)
+        opened(KB, 3, "TR")
+        least("FK", 0, KI)
+        row(B5, 192, "kap")
+        mm(R(B5, 0, 192), R("I13"), R("M16"))
+        rest(Z(4), "FK", 0, 256)
+        from_keys(B5, 4)
+        clamp(R("S2"), B5)
         row(B5, 12, "cm")
         row(B5, 12, "ch", "one", False)
         to_list(B5, "S2", "W8")
         ts(R("rs"), R(B5, 0, 12), R4096, OP.add, R4096, OP.subtract)
         tt(R("SW", 0, 12), R(B5, 0, 12), R("rs"), OP.subtract)
         ts(R("sL"), R("SW", 0, 12), MID, OP.add)
-        act(R("b0"), IND("ow", 4096, "sL"))
+        either(R("b0"), IND("ow", 4096, "sL"))
         cp(R("nL"), IND("nbw", 4096, "sL"))
-        largest("FK1", 192, KI)
-        largest("FK1", 384, KR)
-        rest(R("UU", 24, 36), "FK1", 192, 384)
-        rest(R("kR"), "FK1", 384, 576, True)
-        for i in range(6):
-            gather("V2", "nL", 32 * i, 32 * i + 32)
+        largest("FK", 256, KI)
+        largest("FK", 512, KR)
+        rest(R("UU", 32, 48), "FK", 256, 512)
+        rest(Z(5), "FK", 512, 768, True)
+        gather("V2", "nL", FLAGS["n2"])
         to_list(B5, "b0", "W1", 192, True)
         mm(R(B4, 0, 192), R("BLK"), R("b0"), True)
-        act(R("bf"), R(B4, 0, 192))
+        either(R("bf"), R(B4, 0, 192))
         ts(R("Lc"), R(B5, 0, 12), 16.0, OP.mult)
         ts(R("SW", 12, 24), R(B5, 0, 12), -MID, OP.add)
         cp(R("Lb"), R(B5, 0, 12))
-        act(R("Cb"), IND("CXR", 3072, "Lc"))
+        either(R("Cb"), IND("CZR", 3072, "Lc"))
         for h in (0, 1):
             mm(R(B4, 128 * h, 128 * h + 128, 1, 96), R("Cb", 96 * h, 96 * h + 96), R("ID"), True)
-        act(R("CT", p=96), R(B4, 0, 256, 1, 96))
+        either(R("CT", p=96), R(B4, 0, 256, 1, 96))
         ts(R("n16"), R("nL"), -2048.0, OP.add)
         for c in range(12):
             ts(R("EQ", 208 * c, 192 * c + 192), R("bf", 16 * c, 192), -MID, OP.add, R("SW", 12 + c, 13 + c), OP.is_equal)
         row(B6, 192, "zrow")
-        for c in range(11):
-            mm(R(B6, 16 * c + 16, 192), R("BLK"), R("EQ", 208 * c + 16, 192 * c + 192))
-        for r in range(1, 16):
-            mm(R(B6, r, 192, 16), R("LO", 128 * r, 128 * r + 128), R("EQ", r, 2304, 208))
+        for c0, c1 in ((0, 4), (4, 11)):
+            mms([(R(B6, 16 * c + 16, 192), R("BLK"), R("EQ", 208 * c + 16, 192 * c + 192)) for c in range(c0, c1)])
+        mms([(R(B6, r, 192, 16), R("LO", 128 * r, 128 * r + 128), R("EQ", r, 2304, 208)) for r in range(1, 16)])
         for h in (0, 1):
-            act(R("cnt", 192 * h, 192 * h + 192), R(B6, 0, 192))
+            either(R("cnt", 192 * h, 192 * h + 192), R(B6, 0, 192))
         mm(R(B7, 0, 24), R("IDf"), R("SW"), True)
         to_list(B7, "cnt", "W8", 384)
         tt(R("l1"), R(B7, 0, 24), R("aC"), OP.min)
         ts(R("LS"), R("l1"), MID, OP.add)
-        row(B7, 192, "kap")
-        from_keys(B7, R("kR"))
-        act(R("QR"), R(B7, 0, 192), AF.Square)
-        act(R("QG"), IND("QR", 192, "Lb"))
-        act(R("Mg"), IND(MR, 192, "Lb"))
-        group_sum(KE, "V2", "Wm")
-        for i in range(6):
-            bank = PSUM[4 + i % 2]
-            mm(R(bank), R("ID"), R("V2", 512 * i, 512 * i + 512), True)
-            mm(R(bank), R("CT", 128 * (i // 3), 128 * (i // 3) + 128, 1, 96), R("EX", 512 * (i % 3), 512 * (i % 3) + 512, 1, 96))
-            act(R("DB", 512 * i, 512 * i + 512), R(bank), AF.Abs)
-        group_sum(KB, "DB", "W32")
+        from_keys(B7, 5, True)
+        act(R("QR"), R(B7, 0, 192), AF.Square, R("kc"))
+        either(R("QG"), IND("QR", 192, "Lb"))
+        either(R("Mg"), IND(MR, 192, "Lb"))
+        group_sum(KE, "V2", "Gm")
+        for h in (0, 1):
+            apart("V2", "CT", "DB", h, (B4, B5))
+        group_sum(KB, "DB", "G32")
         for q in range(4):
             larger("V2", "CXI", "D2", q)
-        group_sum(KE, "D2", "W64")
+        group_sum(KE, "D2", "G64")
         if not last:
             act(R("xg"), IND("X", 4096, "sL"), AF.Relu, -16.0)
             cp(IND("X", 4288, "LS"), R("xg"))
         for bank, l in ((B0, "kan"), (B1, "kap")):
             row(bank, 192, l)
             mm(R(bank, 0, 192), R("I13"), R("n16"))
-        row(B4, 192, "kap")
         mm(R(B5, 0, 192), R("IDn"), R("cnt", 0, 192), True)
         row(B6, 192, "cI")
         mm(R(B6, 0, 192), R("IDk"), R("cnt", 0, 192))
         row(B7, 192, "cR")
         mm(R(B7, 0, 192), R("IDk"), R("QG"))
         for i, bank in enumerate((KE, KB)):
-            act(R("FM", 192 * i, 192 * i + 192), R(bank, 0, 192), AF.Sign, lim, -1.0)
-            scan(R("CN", 192 * i, 192 * i + 192), R("m01", 0, 192), R("FM", 192 * i, 192 * i + 192), OP.mult, OP.add)
-            least("FS", 576 * i, bank)
-            largest("FS", 192 + 192 * i, bank)
-            rest(R("VV" if i else "UU", 0, 24), "FS", 384 * i, 384 * i + 384)
-        tt(R("won"), R("CN", 15, 192, 16), R("CN", 207, 384, 16), OP.is_gt)
+            act(R("FM", 256 * i, 256 * i + 256), R(bank, 0, 256, 1, 96), AF.Sign, lim, -1.0)
+            scan(R("CN", 256 * i, 256 * i + 256), R("m01", 0, 256, 1, 96), R("FM", 256 * i, 256 * i + 256), OP.mult, OP.add)
+            least("FS", 768 * i, bank)
+            largest("FS", 256 + 256 * i, bank)
+            rest(R("VV" if i else "UU", 0, 32), "FS", 512 * i, 512 * i + 512)
+        tt(Z(3), R("CN", 15, 256, 16), R("CN", 271, 512, 16), OP.is_gt)
         for i, bank in enumerate((B0, B1, B4)):
-            u, v, s, p, r = (R(n, 12 * i, 12 * i + 12) for n in ("UU", "VV", "SS", "PP", "RR"))
+            u, s, p = (R(n, 16 * i, 16 * i + 16) for n in ("UU", "SS", "PP"))
+            v = R("VV", 16 * i, 16 * i + 16) if i < 2 else Z(4)
             tt(s, u, v, OP.add)
-            tt(p, s, R("won"), OP.mult)
-            tt(r, v, p, OP.subtract)
-            from_keys(bank, r)
+            tt(p, s, Z(3), OP.mult)
+            tt(Z(i), v, p, OP.subtract)
+            from_keys(bank, i, i == 2)
         clamp(R("S0"), B0)
         clamp(R("S1"), B1)
-        act(R("QK"), R(B4, 0, 192), AF.Square)
+        act(R("QK"), R(B4, 0, 192), AF.Square, R("kc"))
         mm(R(B6, 0, 192), R("BK8"), R("S0"))
         mm(R(B6, 0, 192), R("IDk"), R("QK"))
         act(R(IC), R(B6, 0, 192), AF.Relu)
@@ -498,7 +564,7 @@ def rank_program(g, core, T, topo):
         tt(IND(MR, 384, "LS", 12, 24), R("zr"), R("Mg"), OP.max)
         if not last:
             send(MR, [(up2, "inM", "rR")])
-        from_keys(B5, R("won"))
+        from_keys(B5, 3)
         act(R("wf"), R(B5, 0, 192), AF.Relu, acc=R("wc"))
         mm(R(B2, 0, 192), R("BLK"), R("b0"), True)
         mm(R(B2, 0, 192), R("ID"), R("wf"))
@@ -507,10 +573,10 @@ def rank_program(g, core, T, topo):
         tt(IND("ow", 4288, "LS"), R("xa"), R("ya"), OP.subtract)
         if not last:
             act(R("wb"), R("wc"))
-            mm(R(B3, 0, 1), R("ONE"), R("wb"), True)
-            ts(R("wi"), R(B3, 0, 1), 0.0625, OP.mult)
+            mm(R(B3, 0, 1, 1, 96), R("ONE", 0, 96), R("wb"), True)
+            ts(R("wi"), R(B3, 0, 1, 1, 96), 0.0625, OP.mult)
             ts(R("wj"), R("wi"), 63, OP.bitwise_and)
-            ts(R("lim"), R("wj"), 32.0, OP.mult, R("lim0"), OP.add)
+            ts(R("lim"), R("wj"), 32.0, OP.mult, -15.5, OP.add)
 
     def merged(old, new, both, words):
         tt(R(both), R(old, 0, 192), R(new), OP.max)

@@ -6,20 +6,21 @@ OP = AluOpType
 AF = ActivationFunctionType
 F32, BF, I32, U16, F16 = "float32", "bfloat16", "int32", "uint16", "float16"
 SIZE = {F32: 4, I32: 4, BF: 2, U16: 2, F16: 2}
-BIG = float(2 ** 26)
+BIG = float(2 ** 22)
 KILL = float(2 ** 18)
 R1, R32, R4096 = 1.5 * 2 ** 23, 1.5 * 2 ** 28, 1.5 * 2 ** 35
 MID = 2047.5
-CYCLE, WAKE, SLACK, HOP = 0.00087, 0.12, 0.05, 2.5
+CYCLE, WAKE, SLACK, HOP = 0.00087, 0.18, 0.05, 2.0
 ORDER = []
-FLAGS = dict(n1=24, n2=16, ai=(0,), ar=(0,), oi=(0, 1, 2, 3))
+FLAGS = dict(n1=24, n2=32, fi=False, fr=False, lm=1.8, lx=5.0, ls=3.0, mh=2, both=False, split=False, swap=False, bi=False, br=False, b3=True)
+AHEAD = 1.0
 SECOND = 1.0
-URGENT = {}
+TRIES = 4000
 
 OWN_TILES = {
     F32: "ow:4288 IC0:192 IC1:192 MR0:384 MR1:384 inA:192 inB:192 inM:192 inC:192 yo:192 ob:256",
-    BF: "X:4288 VI:3072 VR:3072 V2:3072 XI:3072 NI:3072 XR:3072 NR:3072 CXI:3072 CXR:3072 DA:3072 DR:3072 D2:3072 DB:3072 "
-        "CZI:3072 CZR:3072 m01:768 m512:768 LO:2048 EX:1536 EQ:2304 QR:192",
+    BF: "X:4288 VI:3072 VR:3072 V2:3072 XI:3072 NI:3072 XR:3072 NR:3072 CXI:3072 DA:3072 DR:3072 D2:3072 DB:3072 "
+        "CZI:1536 CZR:1536 on5:512 m01:768 m512:768 LO:2048 EX:1536 EQ:2304 QR:192",
     I32: "nbw:4096 od:256 mi32:192 thi:8",
     U16: "oR0:192 oI0:192",
 }
@@ -28,11 +29,11 @@ POOLS = {
          "xa:192 ya:192 wc:1 lim:1/96",
     BF: "ONE:128 BLK:128 BK8:128 ID:128 I13:128 IDk:128 IDn:128 G64:8 G32:8 Gm:8 W1:144 W8:144 mB:256/96 mD:256/96 "
         "krow:256/1 TR:256/3 thd:3 e3:3/1 kap:128/1 kan:128/1 cm:128/1 ch:128/1 cI:128/1 cR:128/1 one:192/1 zrow:128/1 "
-        "UU:48/96 VV:32/96 SS:48/96 PP:48/96 ZZ:1536/96 ZX:1536/96 b0:192 bf:192 cnt:384 Cb:192 CT:256 QG:192 QK:192 FM:512/96 CN:512/96 "
+        "UU:16/96 VV:64/96 SS:48/96 PP:48/96 ZZ:2048/96 ZX:2048/96 I64:128 I64n:128 IDK:128 c64:128/1 cn1:128/1 QQ:384 b0:192 bf:192 cnt:384 Cb:192 CT:256 QG:192 QK:384 FM:512/96 CN:512/96 "
         "wf:192 wb:1 xg:192 CTI:256 CTR:256",
-    F16: "IDh:128 M16:192 n16:192 S0:192 S1:192 S2:192",
-    I32: "pI:1 pJ:1 wi:1/96 wj:1/96 td:2 mw:192 mv:192 mu:192",
-    U16: "oI1:192 oR1:192 sL:12 nL:192 Lb:12 Lc:12 LS:24",
+    F16: "IDh:128 M16:192 n16:192 S0:384 S1:384 S2:192",
+    I32: "pI:1 pJ:1 wi:1/96 wj:1/96 td:2 mw:192 mv:192 mu:192 a32:96",
+    U16: "oI1:192 oR1:192 sL:12 nL:192 Lb:12 Lc:12 LS:24 aU:96",
 }
 SCRATCH, SHAPE, PLACE = {}, {}, {}
 for _d, _names in OWN_TILES.items():
@@ -53,6 +54,89 @@ for _n in PSUM:
     SCRATCH[_n] = ("psum", [128, 512], F32)
     SHAPE[_n], PLACE[_n] = (128, 512), (_n, 0)
 SEMAPHORES = ["qv", "qa", "qp", "qg"] + ["d%d" % i for i in range(8)] + ["rM", "rA", "rB", "rR", "rC"] + ["l%d" % i for i in range(4)]
+
+
+def arrange(calls, other, span, tries=None):
+    n = len(calls)
+    qs = [c[0] for c in calls]
+    users = [[] for _ in calls]
+    for i, c in enumerate(calls):
+        for d in c[5]:
+            users[d].append(i)
+    gap = [[(d, calls[d][2] - calls[d][1], qs[d] != "x" and not qs[d] == qs[i] == "p") for d in c[5]] for i, c in enumerate(calls)]
+
+    def walk(way):
+        left, ready, free, out = [len(c[5]) for c in calls], [0.0] * n, {q: 0.0 for q in "vapgsx"}, []
+        can = {q: [i for i in range(n) if q in qs[i] and not left[i]] for q in free}
+        while len(out) < n:
+            t, q = min((max(free[q], min(ready[i] for i in lst)), q) for q, lst in can.items() if lst)
+            rank = {j: way[j] - (0.0 if qs[j][0] == q else SECOND) for j in can[q]}
+            time = {j: other[j] if j in other and qs[j][0] != q else calls[j][1] for j in can[q]}
+            i = max((j for j in rank if ready[j] <= t + SLACK), key=rank.get)
+            u = max((j for j in rank if ready[j] <= t + time[i]), key=rank.get)
+            if rank[u] > rank[i] + AHEAD:
+                fit = [j for j in rank if max(ready[j], t) + time[j] <= ready[u] + SLACK]
+                if fit:
+                    i = max(fit, key=rank.get)
+                elif ready[u] - t < t + time[i] - ready[u]:
+                    i = u
+            for e in qs[i]:
+                can[e].remove(i)
+            t = max(t, ready[i])
+            busy, late = (other[i], other[i]) if i in other and qs[i][0] != q else calls[i][1:3]
+            free[q] = t + busy
+            out.append((i, q, busy))
+            for u in users[i]:
+                ready[u] = max(ready[u], t + late + (0.0 if q == "x" or q == qs[u] == "p" else WAKE))
+                left[u] -= 1
+                if not left[u]:
+                    for e in qs[u]:
+                        can[e].append(u)
+        return out
+
+    def length(out):
+        total = 0.0
+        for sign, wake in ((-1, 0.7 * WAKE), (1, 1.3 * WAKE)):
+            end, free = [0.0] * n, {q: 0.0 for q in "vapgsx"}
+            for i, q, busy in out:
+                t = free[q]
+                for d, late, wait in gap[i]:
+                    t = max(t, end[d] + late + (wake if wait else 0.0))
+                end[i] = free[q] = t + busy + sign * span.get(i, 0.0)
+            total += max(e + c[2] - c[1] for e, c in zip(end, calls))
+        return total
+    way = [0.0] * n
+    for i in range(n - 1, -1, -1):
+        way[i] = calls[i][2] + max([way[u] + WAKE for u in users[i]] + [0.0]) - 1e-6 * i
+    alike = {}
+    for i, c in enumerate(calls):
+        alike.setdefault(c[0] + c[3][0], []).append(i)
+    rng = np.random.RandomState(1)
+    out = walk(way)
+    best = length(out)
+    now, o = list(way), out
+    for _ in range(30):
+        tail, nxt = [0.0] * n, {}
+        for i, q, busy in reversed(o):
+            w = max([tail[u] + (0.0 if q == "x" or q == qs[u] == "p" else WAKE) for u in users[i]] + [0.0]) + calls[i][2] - calls[i][1]
+            tail[i] = max(w, tail[nxt[q]] if q in nxt and q != "x" else 0.0) + busy
+            nxt[q] = i
+        now = [0.9 * now[i] + 0.1 * (calls[i][2] + max([tail[u] + WAKE for u in users[i]] + [0.0])) for i in range(n)]
+        o = walk(now)
+        e = length(o)
+        if e < best:
+            way, out, best = now, o, e
+    for _ in range(TRIES if tries is None else tries):
+        new = list(way)
+        j = int(rng.randint(n))
+        step = float(rng.normal()) * 1.5
+        for i in alike[qs[j] + calls[j][3][0]] if rng.rand() < 0.4 else [j]:
+            new[i] += step
+        o = walk(new)
+        e = length(o)
+        if e <= best:
+            way, out, best = new, o, e
+    return [(i, q) for i, q, _ in out], best / 2
 
 
 def rank_program(g, core, T, topo):
@@ -108,7 +192,10 @@ def rank_program(g, core, T, topo):
         calls.append((q, busy, late, (wr + rd)[0], issue, deps))
         return len(calls) - 1
 
-    def emit(q, call, outs, ins, each=1.0):
+    other = {}
+    span = {}
+
+    def emit(q, call, outs, ins, each=1.0, second=None):
         o = outs[0]
         full = [x for x in ins if isinstance(x, tuple) and x[2] > 1] or [o]
         if o[5]:
@@ -118,7 +205,10 @@ def rank_program(g, core, T, topo):
             c = 70 + 1.5 * o[2]
         else:
             c = max(64, o[2] * (0.5 if each == 0.5 and all(x[3] == 2 for x in full + [o]) else max(each, 1.0)))
-        put(q, c * CYCLE, c * CYCLE, outs, ins, call)
+        i = put(q, c * CYCLE, c * CYCLE, outs, ins, call)
+        if second:
+            other[i] = second
+        span[i] = (2.0 * o[2] if o[5] else 0.45 * o[2] if full[0][5] else 0.0) * CYCLE
 
     def tt(o, a, b, op):
         emit("v", lambda: g.vector.tensor_tensor(o[0], a[0], b[0], op), [o], [a, b], 1.0 if a[4] or b[4] else 2.0)
@@ -210,40 +300,12 @@ def rank_program(g, core, T, topo):
             put("x", 0.0, 0.0, [R(land)], [], (rs, m), False, [me])
         return me
 
-    def order():
-        n = len(calls)
-        users = [[] for _ in calls]
-        for i, c in enumerate(calls):
-            for d in c[5]:
-                users[d].append(i)
-        way = [0.0] * n
-        for i in range(n - 1, -1, -1):
-            way[i] = calls[i][2] + max([way[u] + WAKE for u in users[i]] + [0.0])
-        way = [w + URGENT.get(c[0] + "." + c[3][0], 0.0) - 1e-6 * i for i, (w, c) in enumerate(zip(way, calls))]
-        left, ready, free, out = [len(c[5]) for c in calls], [0.0] * n, {q: 0.0 for q in "vapgsx"}, []
-        can = {q: [i for i in range(n) if q in calls[i][0] and not left[i]] for q in free}
-        while len(out) < n:
-            t, q = min((max(free[q], min(ready[i] for i in lst)), q) for q, lst in can.items() if lst)
-            i = max((i for i in can[q] if ready[i] <= t + SLACK), key=lambda i: way[i] - (0.0 if calls[i][0][0] == q else SECOND))
-            for e in calls[i][0]:
-                can[e].remove(i)
-            t = max(t, ready[i])
-            free[q] = t + calls[i][1]
-            out.append((i, q))
-            for u in users[i]:
-                ready[u] = max(ready[u], t + calls[i][2] + (0.0 if q == "x" or q == calls[u][0] == "p" else WAKE))
-                left[u] -= 1
-                if not left[u]:
-                    for e in calls[u][0]:
-                        can[e].append(u)
-        return out
-
     def issue_all():
         count = {q: 0 for q in "vapg"}
         known = {q: {} for q in queue}
         snap, done = {}, {}
         if not ORDER:
-            ORDER.extend(order())
+            ORDER.extend(arrange(calls, other, span)[0])
         for i, q in ORDER:
             qs, _, _, lab, issue, deps = calls[i]
             if len(qs) > 1:
@@ -275,64 +337,76 @@ def rank_program(g, core, T, topo):
     up1, up2 = (rank + 1) % n_ranks, (rank + 2) % n_ranks
     dn1, dn2 = (rank - 1) % n_ranks, (rank - 2) % n_ranks
 
-    dma("s", R("mi32"), hbm("m0"), 2.5)
-    dma("s", R("X", 0, 4096), hbm("x0"), 6.0)
+    def fill(o, c):
+        emit("vg", {"v": lambda: g.vector.memset(o[0], float(c)),
+                    "g": lambda: g.iota(o[0], [[0, o[2]]], c, 0, allow_small_or_imprecise_dtypes=True)}, [o], [], 0.5, 0.13 + 2 * o[2] * CYCLE)
+
+    def lin(o, a, mul, add=0.0):
+        emit("va", {"v": lambda: g.vector.tensor_scalar(o[0], a[0], ap(mul), add, OP.mult, OP.add),
+                    "a": lambda: g.scalar.activation(o[0], a[0], AF.Copy, bias=add, scale=ap(mul))}, [o], [a, mul], 0.5, max(64, o[2]) * CYCLE)
+
+    dma("s", R("mi32"), hbm("m0"), FLAGS["lm"])
+    dma("s", R("X", 0, 4096), hbm("x0"), FLAGS["lx"])
     dma("a", R("od"), hbm("own0"), 2.5)
     ms(R("thi"), 0)
     dma("a", (T.thi[0:128:16, 0:1], [("thi", 0, 8)]), hbm("th"), 8.0)
     cp(R("oR0"), R("mi32"))
-    first = send("oR0", [(up1, "oI0", "rM")], 4.0)
-    ms(R("ONE"), 1.0)
+    send("oR0", [(up1, "oI0", "rM")], FLAGS["ls"])
+    ms(R("on5"), 1.0)
     iota(R("pI"), [[0, 1]], 0, 1, False)
     iota(R("cc"), [[1, 16]])
-    select(R("ID"), R("ONE"), [[-1, 128]], OP.is_equal, 0, 1)
-    select(R("BLK"), R("ONE"), [[-16, 8], [0, 16]], OP.is_ge, 0, 1)
+    select(R("ID"), R("on5", 0, 128), [[-1, 128]], OP.is_equal, 0, 1)
+    select(R("BLK"), R("on5", 0, 128), [[-16, 8], [0, 16]], OP.is_ge, 0, 1)
     select(R("BLK"), R("BLK"), [[16, 8], [0, 16]], OP.is_ge, 15, -1)
     ms(R("m01"), 1.0)
-    ms(R("EX", p=96), -1.0)
     ms(R("m01", 0, 768, 16), 0.0)
-    ms(R("m512"), 0.0)
-    ms(R("m512", 0, 768, 16), 512.0)
-    for lo in range(0, 4288, 768):
-        hi = min(lo + 768, 4288)
-        act(R("ow", lo, hi), R("m512", 0, hi - lo), AF.Copy, 0.0, 0.0)
+    lin(R("m512"), R("m01"), -512.0, 512.0)
+    lin(R("mB"), R("m01", 0, 256, 1, 96), -BIG, BIG)
+    lin(R("mD"), R("m01", 0, 256, 1, 96), BIG + 2.0, -BIG)
+    for lo in range(0, 4288, 512):
+        hi = min(lo + 512, 4288)
+        act(R("ow", lo, hi), R("on5", 0, hi - lo), AF.Copy, 0.0, 0.0)
     iota(R("krow"), [[0, 16], [1, 16]], -15)
     iota(R("kap"), [[0, 8], [-1, 16]], 15)
     iota(R("kan"), [[0, 8], [1, 16]], -15)
+    iota(R("a32"), [[16, 96]], 0, 0, False)
+    cp(R("aU"), R("a32"))
     for i in range(3):
-        select(R("EX", 512 * i, 512 * i + 512, 1, 96), R("EX", 512 * i, 512 * i + 512, 1, 96), [[-1, 32], [0, 16]], OP.is_equal, -32 * i, 1)
+        select(R("EX", 512 * i, 512 * i + 512, 1, 96), R("on5", p=96), [[-1, 32], [0, 16]], OP.is_equal, -32 * i, 1)
     for i in range(4):
-        ms(R("CZI", 768 * i, 768 * i + 768), 0.0)
-        iota(R("CZR", 768 * i, 768 * i + 768), [[0, 768]])
+        fill(R("CZI", 384 * i, 384 * i + 384), 0)
+        fill(R("CZR", 384 * i, 384 * i + 384), 0)
     ts(R("pJ"), R("pI"), 15, OP.bitwise_and)
     cp(R("p15"), R("pJ"))
     ts(R("kc"), R("pJ"), -1.0, OP.mult, 15.0, OP.add)
     ts(R("LTm"), R("cc"), R("p15"), OP.is_gt)
     for name, c in (("W1", 1.0), ("W8", 8192.0)):
-        ms(R(name), 0.0)
-        ts(R(name, 15, 143, 16), R("BLK", 0, 128, 16), c, OP.mult)
+        fill(R(name), 0)
+        lin(R(name, 15, 143, 16), R("BLK", 0, 128, 16), c)
     for name, c in (("G64", 64.0), ("G32", 32.0), ("Gm", -32.0)):
-        ts(R(name), R("BLK", 0, 128, 16), c, OP.mult)
-    for name, c in (("IDh", 511.0 / 1024.0), ("I13", 2.0 ** -13), ("IDk", -KILL), ("IDn", -1.0)):
-        ts(R(name), R("ID"), c, OP.mult)
-    for name, c in (("one", 1.0), ("cm", -2048.0), ("ch", 0.5), ("cI", 163840.0), ("cR", 98304.0), ("zrow", 0.0)):
-        ms(R(name), c)
-    for i in range(2):
-        ms(R("ZZ", 768 * i, 768 * i + 768), 0.0)
+        lin(R(name), R("BLK", 0, 128, 16), c)
+    ts(R("IDh"), R("ID"), 511.0 / 1024.0, OP.mult)
+    for name, c in (("I13", 2.0 ** -13), ("IDk", -KILL), ("IDn", -1.0), ("IDf", 1.0)):
+        lin(R(name), R("ID"), c)
+    lin(R("BK8"), R("BLK"), 8192.0)
+    ms(R("ch"), 0.5)
+    for name, c in (("cm", -2048), ("cI", -131072 if FLAGS["both"] else 163840), ("cR", 65536 if FLAGS["both"] else 98304), ("zrow", 0)):
+        fill(R(name), c)
+    for i in range(8 if FLAGS["both"] else 6):
+        fill(R("ZZ", 256 * i, 256 * i + 256), 0)
+    if FLAGS["both"]:
+        for name, c in (("I64", 64.0), ("I64n", -64.0), ("IDK", KILL)):
+            lin(R(name), R("ID"), c)
+        fill(R("c64"), 64)
+        fill(R("cn1"), -1)
     cp(R("ob"), R("od"))
     dma("s", (T.ow[0:128:16, 0:4096], [("ow", 0, 4096)]), R("ob"), 5.0)
     dma("s", R("nbw"), (T.nb[:], [("ob", 0, 1), ("oR0", 0, 1)]), 10.0)
-    ms(R("mB"), 0.0)
-    ms(R("mB", 0, 256, 16), BIG)
-    ms(R("mD"), 2.0)
-    ms(R("mD", 0, 256, 16), -BIG)
-    ts(R("BK8"), R("BLK"), 8192.0, OP.mult)
     for r in range(1, 16):
-        act(R("LO", 128 * r, 128 * r + 128), R("BLK"), AF.Copy, 0.0, R("LTm", r, r + 1))
-    cp(R("IDf"), R("ID"))
-    ms(R("X", 4096, 4288), 0.0)
-    ms(R("MR0", 192, 384), 0.0)
-    ms(R("MR1", 192, 384), 0.0)
+        lin(R("LO", 128 * r, 128 * r + 128), R("BLK"), R("LTm", r, r + 1))
+    fill(R("X", 4096, 4288), 0)
+    fill(R("MR0", 192, 384), 0)
+    fill(R("MR1", 192, 384), 0)
     cp(R("MR0", 0, 192), R("mi32"))
     iota(R("aC", 0, 12), [[16, 12]], 2049)
     iota(R("aC", 12, 24), [[16, 12]], -1855)
@@ -360,23 +434,25 @@ def rank_program(g, core, T, topo):
         for lo in range(0, 192, n):
             either(R(v, 16 * lo, 16 * (lo + n)), IND("X", 4096, off, lo, lo + n))
 
-    def row(bank, n, l, r="one", start=True):
-        mm(R(bank, 0, n), R(l, 0, 128), R(r, 0, n), start)
+    def row(bank, n, l, start=True):
+        mm(R(bank, 0, n), R(l, 0, 128), R("on5", 0, n, 1, 1), start)
 
-    def group_sum(bank, src, w, halves=(0, 1)):
+    def group_sum(place, src, w, halves=(0, 1)):
         for h in halves:
+            bank, at = place[h] if isinstance(place, list) else (place, 128 * h)
             for k0 in (0, 8):
-                mms([(R(bank, 128 * h + k, 128 * h + 128, 16, 96), R(src, 1536 * h + k, 1536 * h + 1536, 16), R(w)) for k in range(k0, k0 + 8)])
+                mms([(R(bank, at + k, at + 128, 16, 96), R(src, 1536 * h + k, 1536 * h + 1536, 16), R(w)) for k in range(k0, k0 + 8)])
 
-    def Z(i):
-        return R("ZZ", 256 * i, 256 * i + 256, 16)
+    def Z(i, h=None):
+        return R("ZZ", 256 * i, 256 * i + 256, 16) if h is None else R("ZZ", 256 * i + 128 * h, 256 * i + 128 * h + 128, 16)
 
-    def from_keys(bank, i, start=False):
-        scan(R("ZX", 256 * i, 256 * i + 256), R("m01", 0, 256, 1, 96), R("ZZ", 256 * i, 256 * i + 256), OP.mult, OP.add)
-        lst = [(R(bank, 96 * h, 96 * h + 96), R("ZX", 256 * i + 128 * h, 256 * i + 128 * h + 128), R("ID", 0, 96, 1, 96)) for h in (0, 1)]
+    def from_keys(bank, i, start=False, halves=(0, 1)):
+        lo, n = 256 * i + 128 * halves[0], 128 * len(halves)
+        scan(R("ZX", lo, lo + n), R("m01", 0, n, 1, 96), R("ZZ", lo, lo + n), OP.mult, OP.add)
+        lst = [(R(bank, 96 * h, 96 * h + 96), R("ZX", 256 * i + 128 * h, 256 * i + 128 * h + 128), R("ID", 0, 96, 1, 96)) for h in halves]
         if start:
-            mms(lst[:1], True)
-            mms(lst[1:], True)
+            for m in lst:
+                mms([m], True)
         else:
             mms(lst)
 
@@ -394,7 +470,7 @@ def rank_program(g, core, T, topo):
         bank = PSUM[6 + turn[0] % 2]
         o = R(bank, 0, 48 * n)
         mms([(o, R("IDh"), R(m, 768 * q + 15, 768 * (q + n), 16)) for m in (mx, mn)], True)
-        ts(R(cz, 768 * q, 768 * (q + n), 16), R(bank, 0, 48 * n), R1, OP.add, R1, OP.subtract)
+        ts(R(cz, 768 * (q % 2), 768 * (q % 2 + n), 16), R(bank, 0, 48 * n), R1, OP.add, R1, OP.subtract)
 
     def turned(mx, mn, ct, h):
         turn[0] += 1
@@ -402,34 +478,41 @@ def rank_program(g, core, T, topo):
         mms([(o, R(m, 1536 * h + 15, 1536 * h + 1536, 16), R("IDh")) for m in (mx, mn)], True)
         ts(R(ct, 128 * h, 128 * h + 128, 1, 96), o, R1, OP.add, R1, OP.subtract)
 
-    def spread(cz, cx, q):
-        scan(part(cx, q), R("m01"), part(cz, q), OP.mult, OP.add)
+    def spread(cz, cx, q, free=False):
+        o, z = part(cx, q), part(cz, q % 2)
+        if not free:
+            return scan(o, R("m01"), z, OP.mult, OP.add)
+        w = IND(cz, 1536, "aU", 48 * (q % 2), 48 * (q % 2) + 48)
+        emit("va", {"v": lambda: g.vector.tensor_tensor_scan(o[0], R("m01")[0], z[0], 0.0, OP.mult, OP.add),
+                    "a": lambda: g.scalar.activation(o[0], w[0], AF.Copy)}, [o], [R("m01"), z, (0, w[1], 0)], 0.5, (70 + 1.5 * 768) * CYCLE)
 
-    def apart(v, ct, d, h, banks):
+    def apart(v, ct, d, h, banks, first=None):
         for i in range(3 * h, 3 * h + 3):
-            bank = banks[i % 2]
-            mms([(R(bank), R("ID"), R(v, 512 * i, 512 * i + 512)),
-                 (R(bank), R(ct, 128 * h, 128 * h + 128, 1, 96), R("EX", 512 * (i % 3), 512 * (i % 3) + 512, 1, 96))], True)
+            bank = banks[i % len(banks)]
+            lst = [(R(bank), R("IDn"), R(v, 512 * i, 512 * i + 512)),
+                   (R(bank), R(ct, 128 * h, 128 * h + 128, 1, 96), R("EX", 512 * (i % 3), 512 * (i % 3) + 512, 1, 96))]
+            if first:
+                lst += [(R(bank, 0, 512, 16), R("ID"), R(v, 512 * i, 512 * i + 512, 16)), (R(bank, 0, 512, 16), R("IDn"), R(first, 32 * i, 32 * i + 32))]
+            mms(lst, True)
             act(R(d, 512 * i, 512 * i + 512), R(bank), AF.Abs)
 
-    def distances(bank, v, mx, mn, cz, cx, ct, d, by_act, order, all_centres):
-        group_sum(bank, v, "Gm", [h for h in (0, 1) if h not in by_act])
-        for q in order:
+    def distances(bank, v, mx, mn, cz, cx, ct, d, free, both=False):
+        if not both:
+            group_sum(bank, v, "Gm", [1])
+        for q in range(4):
             extremes(v, mx, mn, q)
-            if q // 2 not in by_act:
-                centres(mx, mn, cz, q)
-                spread(cz, cx, q)
-                larger(v, cx, d, q)
-            elif (q ^ 1) in order[:order.index(q)]:
-                turned(mx, mn, ct, q // 2)
-                apart(v, ct, d, q // 2, (B3, B4))
-        for h in (0, 1):
-            group_sum(bank, d, "G32" if h in by_act else "G64", [h])
-        for h in by_act:
-            centres(mx, mn, cz, 2 * h, 2)
-            if all_centres:
-                spread(cz, cx, 2 * h)
-                spread(cz, cx, 2 * h + 1)
+        turned(mx, mn, ct, 0)
+        apart(v, ct, d, 0, (B3, B4))
+        if both:
+            turned(mx, mn, ct, 1)
+            apart(v, ct, d, 1, (B4, B3))
+            return group_sum(bank, d, "G32")
+        for q in (2, 3):
+            centres(mx, mn, cz, q)
+            spread(cz, cx, q, free)
+            larger(v, cx, d, q)
+        group_sum(bank, d, "G32", [0])
+        group_sum(bank, d, "G64", [1])
 
     def larger(v, cx, d, q):
         tt(part(v, q, 16), part(v, q, 16), part(cx, q, 16), OP.max)
@@ -456,21 +539,31 @@ def rank_program(g, core, T, topo):
         oI, oR = "oI%d" % t, "oR%d" % t
         IC, MR = "IC%d" % t, "MR%d" % t
         last = t == 1
-        KI, KR, KE, KB = B0, B1, B2, B3
+        KI, KR, E = B0, B1, (B2, B3)
+        KE, KB = ([(E[0], 0), (E[1], 0)], [(E[0], 128), (E[1], 128)]) if FLAGS["split"] else E
         lim = R("lim") if t else -15.5
 
         def opened(bank, n, rows):
-            mm(R(bank, 0, 256, 1, 96), R("ONE", 0, 96, 1, n), R(rows), True)
+            mm(R(bank, 0, 256, 1, 96), R("on5", 0, 96, 1, n), R(rows), True)
         gather("VI", oI, FLAGS["n1"])
         gather("VR", oR, FLAGS["n1"])
         opened(KI, 1, "krow")
         opened(KR, 1, "krow")
-        opened(KE, 3, "TR")
+        opened(E[0], 3, "TR")
         ts(R("M16"), R(oI), -2048.0, OP.add)
-        distances(KI, "VI", "XI", "NI", "CZI", "CXI", "CTI", "DA", FLAGS["ai"], FLAGS["oi"], True)
-        group_sum(KE, "CXI", "Gm")
-        distances(KR, "VR", "XR", "NR", "CZR", "CXR", "CTR", "DR", FLAGS["ar"], (0, 1, 2, 3), False)
-        opened(KB, 3, "TR")
+        distances(KI, "VI", "XI", "NI", "CZI", "CXI", "CTI", "DA", False, FLAGS["bi"])
+        if not FLAGS["swap"]:
+            centres("XI", "NI", "CZI", 0, 2)
+            for q in (0, 1):
+                spread("CZI", "CXI", q, FLAGS["fi"])
+            group_sum(KE, "CXI", "Gm", [0])
+        elif not FLAGS["bi"]:
+            turned("XI", "NI", "CTI", 1)
+        distances(KR, "VR", "XR", "NR", "CZR", "NR", "CTR", "DR", FLAGS["fr"], FLAGS["br"])
+        centres("XR", "NR", "NR", 0, 4 if FLAGS["br"] else 2)
+        opened(E[1], 3, "TR")
+        if not FLAGS["swap"]:
+            group_sum(KE, "CXI", "Gm", [1])
         least("FK", 0, KI)
         row(B5, 192, "kap")
         mm(R(B5, 0, 192), R("I13"), R("M16"))
@@ -478,7 +571,7 @@ def rank_program(g, core, T, topo):
         from_keys(B5, 4)
         clamp(R("S2"), B5)
         row(B5, 12, "cm")
-        row(B5, 12, "ch", "one", False)
+        row(B5, 12, "ch", False)
         to_list(B5, "S2", "W8")
         ts(R("rs"), R(B5, 0, 12), R4096, OP.add, R4096, OP.subtract)
         tt(R("SW", 0, 12), R(B5, 0, 12), R("rs"), OP.subtract)
@@ -487,7 +580,7 @@ def rank_program(g, core, T, topo):
         cp(R("nL"), IND("nbw", 4096, "sL"))
         largest("FK", 256, KI)
         largest("FK", 512, KR)
-        rest(R("UU", 32, 48), "FK", 256, 512)
+        rest(Z(7) if FLAGS["both"] else R("UU"), "FK", 256, 512, FLAGS["both"])
         rest(Z(5), "FK", 512, 768, True)
         gather("V2", "nL", FLAGS["n2"])
         to_list(B5, "b0", "W1", 192, True)
@@ -496,10 +589,16 @@ def rank_program(g, core, T, topo):
         ts(R("Lc"), R(B5, 0, 12), 16.0, OP.mult)
         ts(R("SW", 12, 24), R(B5, 0, 12), -MID, OP.add)
         cp(R("Lb"), R(B5, 0, 12))
-        either(R("Cb"), IND("CZR", 3072, "Lc"))
-        for h in (0, 1):
-            mm(R(B4, 128 * h, 128 * h + 128, 1, 96), R("Cb", 96 * h, 96 * h + 96), R("ID"), True)
-        either(R("CT", p=96), R(B4, 0, 256, 1, 96))
+        if FLAGS["swap"]:
+            for h, cz in enumerate(("CZI", "CZR")):
+                either(R(cz, 0, 1536, 16), IND("NR", 3072, "Lc", 6 * h, 6 * h + 6))
+                spread(cz, "CXI", 2 * h, FLAGS["fi"])
+                spread(cz, "CXI", 2 * h + 1, FLAGS["fi"])
+        else:
+            either(R("Cb"), IND("NR", 3072, "Lc"))
+            for h in (0, 1):
+                mm(R(B4, 128 * h, 128 * h + 128, 1, 96), R("Cb", 96 * h, 96 * h + 96), R("ID"), True)
+            either(R("CT", p=96), R(B4, 0, 256, 1, 96))
         ts(R("n16"), R("nL"), -2048.0, OP.add)
         for c in range(12):
             ts(R("EQ", 208 * c, 192 * c + 192), R("bf", 16 * c, 192), -MID, OP.add, R("SW", 12 + c, 13 + c), OP.is_equal)
@@ -515,18 +614,34 @@ def rank_program(g, core, T, topo):
         ts(R("LS"), R("l1"), MID, OP.add)
         from_keys(B7, 5, True)
         act(R("QR"), R(B7, 0, 192), AF.Square, R("kc"))
+        if FLAGS["both"]:
+            from_keys(B7, 7, True)
+            for h in (0, 1):
+                mm(R(B7, 192 + 96 * h, 288 + 96 * h), R("ZX", 1024 + 128 * h, 1152 + 128 * h), R("ID", 0, 96, 1, 96), True)
+            act(R("QQ"), R(B7, 0, 384), AF.Square, R("kc"))
         either(R("QG"), IND("QR", 192, "Lb"))
         either(R("Mg"), IND(MR, 192, "Lb"))
-        group_sum(KE, "V2", "Gm")
-        for h in (0, 1):
-            apart("V2", "CT", "DB", h, (B4, B5))
-        group_sum(KB, "DB", "G32")
-        for q in range(4):
-            larger("V2", "CXI", "D2", q)
-        group_sum(KE, "D2", "G64")
+        if FLAGS["swap"]:
+            group_sum(KB, "V2", "Gm")
+            group_sum(KB, "CXI", "Gm")
+            apart("V2", "CTI", "D2", 0, (B4, B5, B0))
+            apart("V2", "CTI", "D2", 1, (B4, B5, B0))
+            for q in range(4):
+                larger("V2", "CXI", "DB", q)
+            group_sum(KB, "DB", "G64")
+        else:
+            group_sum(KE, "V2", "Gm")
+            for h in (0, 1):
+                apart("V2", "CT", "DB", h, (B4, B5, B0) if FLAGS["b3"] else (B4, B5))
+            group_sum(KB, "DB", "G32")
+            for q in range(4):
+                larger("V2", "CXI", "D2", q)
+        group_sum(KE, "D2", "G32" if FLAGS["swap"] else "G64")
         if not last:
             act(R("xg"), IND("X", 4096, "sL"), AF.Relu, -16.0)
             cp(IND("X", 4288, "LS"), R("xg"))
+        if FLAGS["both"]:
+            return finish(t, lim, E)
         for bank, l in ((B0, "kan"), (B1, "kap")):
             row(bank, 192, l)
             mm(R(bank, 0, 192), R("I13"), R("n16"))
@@ -535,36 +650,54 @@ def rank_program(g, core, T, topo):
         mm(R(B6, 0, 192), R("IDk"), R("cnt", 0, 192))
         row(B7, 192, "cR")
         mm(R(B7, 0, 192), R("IDk"), R("QG"))
-        for i, bank in enumerate((KE, KB)):
-            act(R("FM", 256 * i, 256 * i + 256), R(bank, 0, 256, 1, 96), AF.Sign, lim, -1.0)
-            scan(R("CN", 256 * i, 256 * i + 256), R("m01", 0, 256, 1, 96), R("FM", 256 * i, 256 * i + 256), OP.mult, OP.add)
-            least("FS", 768 * i, bank)
-            largest("FS", 256 + 256 * i, bank)
-            rest(R("VV" if i else "UU", 0, 32), "FS", 512 * i, 512 * i + 512)
-        tt(Z(3), R("CN", 15, 256, 16), R("CN", 271, 512, 16), OP.is_gt)
-        for i, bank in enumerate((B0, B1, B4)):
-            u, s, p = (R(n, 16 * i, 16 * i + 16) for n in ("UU", "SS", "PP"))
-            v = R("VV", 16 * i, 16 * i + 16) if i < 2 else Z(4)
-            tt(s, u, v, OP.add)
-            tt(p, s, Z(3), OP.mult)
-            tt(Z(i), v, p, OP.subtract)
-            from_keys(bank, i, i == 2)
-        clamp(R("S0"), B0)
-        clamp(R("S1"), B1)
-        act(R("QK"), R(B4, 0, 192), AF.Square, R("kc"))
-        mm(R(B6, 0, 192), R("BK8"), R("S0"))
-        mm(R(B6, 0, 192), R("IDk"), R("QK"))
+        tt(R("SS", 32, 48), R("UU"), Z(4), OP.add)
+        if not FLAGS["split"]:
+            for i in (0, 1):
+                act(R("FM", 256 * i, 256 * i + 256), R(E[i], 0, 256, 1, 96), AF.Sign, lim, -1.0)
+                scan(R("CN", 256 * i, 256 * i + 256), R("m01", 0, 256, 1, 96), R("FM", 256 * i, 256 * i + 256), OP.mult, OP.add)
+                least("FS", 768 * i, E[i])
+                largest("FS", 256 + 256 * i, E[i])
+                rest(R("VV", 32 * i, 32 * i + 32), "FS", 512 * i, 512 * i + 512)
+            tt(Z(3), R("CN", 15, 256, 16), R("CN", 271, 512, 16), OP.is_gt)
+            tt(R("SS", 0, 32), R("VV", 0, 32), R("VV", 32, 64), OP.add)
+            for i, bank in enumerate((B0, B1, B4)):
+                s, p = (R(n, 16 * i, 16 * i + 16) for n in ("SS", "PP"))
+                tt(p, s, Z(3), OP.mult)
+                tt(Z(i), R("VV", 32 + 16 * i, 48 + 16 * i) if i < 2 else Z(4), p, OP.subtract)
+                from_keys(bank, i, i == 2)
+            from_keys(B5, 3)
+        for h in (0, 1) if FLAGS["split"] else ():
+            act(R("FM", 256 * h, 256 * h + 256), R(E[h], 0, 256, 1, 96), AF.Sign, lim, -1.0)
+            scan(R("CN", 256 * h, 256 * h + 256), R("m01", 0, 256, 1, 96), R("FM", 256 * h, 256 * h + 256), OP.mult, OP.add)
+            least("FS", 512 * h, E[h])
+            largest("FS", 512 * h + 256, E[h])
+            rest(R("VV", 32 * h, 32 * h + 32), "FS", 512 * h, 512 * h + 512)
+            best_i, best_r, worst_i, worst_r = (R("VV", 32 * h + 8 * i, 32 * h + 8 * i + 8) for i in range(4))
+            won = Z(3, h)
+            tt(won, R("CN", 256 * h + 15, 256 * h + 128, 16), R("CN", 256 * h + 143, 256 * h + 256, 16), OP.is_gt)
+            for i, (bank, u, v) in enumerate(((B0, best_i, worst_r), (B1, worst_i, best_r), (B4, None, Z(4, h)))):
+                s, p = (R(n, 16 * i + 8 * h, 16 * i + 8 * h + 8) for n in ("SS", "PP"))
+                if u:
+                    tt(s, u, v, OP.add)
+                tt(p, s, won, OP.mult)
+                tt(Z(i, h), v, p, OP.subtract)
+                from_keys(bank, i, i == 2, [h])
+            from_keys(B5, 3, False, [h])
+        clamp(R("S0", 0, 192), B0)
+        clamp(R("S1", 0, 192), B1)
+        act(R("QK", 0, 192), R(B4, 0, 192), AF.Square, R("kc"))
+        mm(R(B6, 0, 192), R("BK8"), R("S0", 0, 192))
+        mm(R(B6, 0, 192), R("IDk"), R("QK", 0, 192))
         act(R(IC), R(B6, 0, 192), AF.Relu)
         if not last:
             send(IC, [(dn1, "inA", "rA"), (up1, "inB", "rB")])
         else:
             send(IC, [(dn2, "inC", "rC")])
-        mm(R(B7, 0, 192), R("BK8"), R("S1"))
+        mm(R(B7, 0, 192), R("BK8"), R("S1", 0, 192))
         act(R("zr"), R(B7, 0, 192), AF.Relu)
         tt(IND(MR, 384, "LS", 12, 24), R("zr"), R("Mg"), OP.max)
         if not last:
             send(MR, [(up2, "inM", "rR")])
-        from_keys(B5, 3)
         act(R("wf"), R(B5, 0, 192), AF.Relu, acc=R("wc"))
         mm(R(B2, 0, 192), R("BLK"), R("b0"), True)
         mm(R(B2, 0, 192), R("ID"), R("wf"))
@@ -573,24 +706,88 @@ def rank_program(g, core, T, topo):
         tt(IND("ow", 4288, "LS"), R("xa"), R("ya"), OP.subtract)
         if not last:
             act(R("wb"), R("wc"))
-            mm(R(B3, 0, 1, 1, 96), R("ONE", 0, 96), R("wb"), True)
+            mm(R(B3, 0, 1, 1, 96), R("on5", 0, 96), R("wb"), True)
             ts(R("wi"), R(B3, 0, 1, 1, 96), 0.0625, OP.mult)
             ts(R("wj"), R("wi"), 63, OP.bitwise_and)
             ts(R("lim"), R("wj"), 32.0, OP.mult, -15.5, OP.add)
 
-    def merged(old, new, both, words):
-        tt(R(both), R(old, 0, 192), R(new), OP.max)
-        ts(R(words), R(both), 4095, OP.bitwise_and)
+    def finish(t, lim, E):
+        IC, MR = "IC%d" % t, "MR%d" % t
+        last = t == 1
 
+        def turn_to(bank, at, i, w):
+            mms([(R(bank, at + 96 * h, at + 96 * h + 96), R("ZX", 256 * i + 128 * h, 256 * i + 128 * h + 128), R(w, 0, 96, 1, 96)) for h in (0, 1)])
+
+        def repeat(i, n):
+            scan(R("ZX", 256 * i, 256 * (i + n)), R("m01", 0, 256 * n, 1, 96), R("ZZ", 256 * i, 256 * (i + n)), OP.mult, OP.add)
+        for bank in (B0, B1):
+            row(bank, 384, "kap")
+            mms([(R(bank, at, at + 192), R("I13"), R("n16")) for at in (0, 192)] + [(R(bank, 0, 192), R("c64"), R("on5", 0, 192, 1, 1))])
+        mm(R(B4, 0, 384), R("IDn"), R("QQ"), True)
+        mm(R(B4, 0, 192), R("cn1"), R("on5", 0, 192, 1, 1))
+        mm(R(B5, 0, 192), R("IDn"), R("cnt", 0, 192), True)
+        row(B6, 192, "cI")
+        mm(R(B6, 0, 192), R("IDk"), R("cnt", 0, 192))
+        row(B7, 192, "cR")
+        mm(R(B7, 0, 192), R("IDk"), R("QG"))
+        for i in (0, 1):
+            act(R("FM", 256 * i, 256 * i + 256), R(E[i], 0, 256, 1, 96), AF.Sign, lim, -1.0)
+            scan(R("CN", 256 * i, 256 * i + 256), R("m01", 0, 256, 1, 96), R("FM", 256 * i, 256 * i + 256), OP.mult, OP.add)
+            least("FS", 512 * i, E[i])
+            largest("FS", 512 * i + 256, E[i])
+            rest(R("ZZ", 512 * i, 512 * i + 512, 16), "FS", 512 * i, 512 * i + 512)
+            repeat(2 * i, 2)
+            turn_to((B0, B1)[i], 192 * i, 2 * i, "ID")
+            turn_to((B1, B0)[i], 192 * i, 2 * i + 1, "IDn")
+        tt(Z(6), R("CN", 15, 256, 16), R("CN", 271, 512, 16), OP.is_gt)
+        repeat(6, 1)
+        for bank in (B0, B1):
+            turn_to(bank, 0, 6, "I64n")
+            turn_to(bank, 192, 6, "I64")
+        turn_to(B4, 0, 6, "ID")
+        turn_to(B4, 192, 6, "IDn")
+        turn_to(B5, 0, 6, "ID")
+        ts(R("S0"), R(B0, 0, 384), -0.25, OP.max, 0.25, OP.min)
+        ts(R("S1"), R(B1, 0, 384), -0.25, OP.max, 0.25, OP.min)
+        act(R("QK"), R(B4, 0, 384), AF.Relu, 1.0)
+        mms([(R(B6, 0, 192), R("BK8"), R("S0", at, at + 192)) for at in (0, 192)])
+        mms([(R(B6, 0, 192), R("IDK"), R("QK", at, at + 192)) for at in (0, 192)])
+        act(R(IC), R(B6, 0, 192), AF.Relu)
+        if not last:
+            send(IC, [(dn1, "inA", "rA"), (up1, "inB", "rB")])
+        else:
+            send(IC, [(dn2, "inC", "rC")])
+        mms([(R(B7, 0, 192), R("BK8"), R("S1", at, at + 192)) for at in (0, 192)])
+        act(R("zr"), R(B7, 0, 192), AF.Relu)
+        tt(IND(MR, 384, "LS", 12, 24), R("zr"), R("Mg"), OP.max)
+        if not last:
+            send(MR, [(up2, "inM", "rR")])
+        act(R("wf"), R(B5, 0, 192), AF.Relu, acc=R("wc"))
+        mm(R(B2, 0, 192), R("BLK"), R("b0"), True)
+        mm(R(B2, 0, 192), R("ID"), R("wf"))
+        act(R("xa"), R(B2, 0, 192), AF.Copy, 0.0, R("e0"))
+        act(R("ya"), R(B2, 0, 192), AF.Relu, R("eB"), R("e192"))
+        tt(IND("ow", 4288, "LS"), R("xa"), R("ya"), OP.subtract)
+        if not last:
+            act(R("wb"), R("wc"))
+            mm(R(B3, 0, 1, 1, 96), R("on5", 0, 96), R("wb"), True)
+            ts(R("wi"), R(B3, 0, 1, 1, 96), 0.0625, OP.mult)
+            ts(R("wj"), R("wi"), 63, OP.bitwise_and)
+            ts(R("lim"), R("wj"), 32.0, OP.mult, -15.5, OP.add)
+
+    def merged(old, new, both, words, out, n):
+        for lo in range(0, 192, n):
+            tt(R(both, lo, lo + n), R(old, lo, lo + n), R(new, lo, lo + n), OP.max)
+            ts(R(words, lo, lo + n), R(both, lo, lo + n), 4095, OP.bitwise_and)
+            cp(R(out, lo, lo + n), R(words, lo, lo + n))
+
+    constants = [len(calls)]
     play(0)
-    merged("MR0", "inA", "mv", "mi32")
-    cp(R("oR1"), R("mi32"))
+    merged("inM", "inB", "mu", "mw", "oI1", 192 // FLAGS["mh"])
+    merged("MR0", "inA", "mv", "mi32", "oR1", 192 // FLAGS["mh"])
     cp(R("MR1", 0, 192), R("mi32"))
-    merged("inM", "inB", "mu", "mw")
-    cp(R("oI1"), R("mw"))
     play(1)
-    merged("MR1", "inC", "mv", "mi32")
-    cp(R("yo"), R("mi32"))
+    merged("MR1", "inC", "mv", "mi32", "yo", 96)
     stores = [dma("a", hbm("yown"), (T.ow[0:128:16, 0:4096], [("ow", 0, 4096)]), 2.5), dma("s", hbm("ym"), R("yo"), 2.5)]
     count = issue_all()
     for q in count:

@@ -8,32 +8,30 @@ F32, BF, I32, U16, F16 = "float32", "bfloat16", "int32", "uint16", "float16"
 SIZE = {F32: 4, I32: 4, BF: 2, U16: 2, F16: 2}
 BIG = float(2 ** 22)
 KILL = float(2 ** 18)
-R1, R32, R4096 = 1.5 * 2 ** 23, 1.5 * 2 ** 28, 1.5 * 2 ** 35
+R1, R32 = 1.5 * 2 ** 23, 1.5 * 2 ** 28
 MID = 2047.5
 CYCLE, WAKE, SLACK, HOP = 0.00087, 0.18, 0.05, 2.0
-ORDER = []
-FLAGS = dict(n1=24, n2=32, fi=False, fr=False, lm=1.8, lx=5.0, ls=3.0, mh=2, both=False, split=False, swap=False, bi=False, br=False, b3=True)
-AHEAD = 1.0
-SECOND = 1.0
+AHEAD, SECOND = 1.0, 1.6
 TRIES = 4000
+ORDER = []
 
 OWN_TILES = {
     F32: "ow:4288 IC0:192 IC1:192 MR0:384 MR1:384 inA:192 inB:192 inM:192 inC:192 yo:192 ob:256",
-    BF: "X:4288 VI:3072 VR:3072 V2:3072 XI:3072 NI:3072 XR:3072 NR:3072 CXI:3072 DA:3072 DR:3072 D2:3072 DB:3072 "
-        "CZI:1536 CZR:1536 on5:512 m01:768 m512:768 LO:2048 EX:1536 EQ:2304 QR:192",
+    BF: "X:4288 VI:3072 VR:3072 V2:3072 XI:3072 NI:3072 XR:3072 NR:3072 CX:3072 DA:3072 DR:3072 D2:3072 DB:3072 "
+        "CZ:1536 on5:512 m01:768 m512:768 LO:2048 EX:1536 EQ:2304 QR:192 CR:192",
     I32: "nbw:4096 od:256 mi32:192 thi:8",
     U16: "oR0:192 oI0:192",
 }
 POOLS = {
-    F32: "p15:1 kc:1 e0:1 e192:1 eB:1 cc:16 aC:24 LTm:16 IDf:128 FS:1024/96 FK:768/96 rS:64/96 rK:48/96 rs:12 SW:24 l1:24 Mg:192 zr:192 "
+    F32: "p15:1 kc:1 e0:1 e192:1 eB:1 aC:24 IDf:128 FS:1024/96 FK:768/96 FB:256/96 rS:64/96 rK:48/96 SW:24 l1:24 Mg:192 zr:192 "
          "xa:192 ya:192 wc:1 lim:1/96",
-    BF: "ONE:128 BLK:128 BK8:128 ID:128 I13:128 IDk:128 IDn:128 G64:8 G32:8 Gm:8 W1:144 W8:144 mB:256/96 mD:256/96 "
-        "krow:256/1 TR:256/3 thd:3 e3:3/1 kap:128/1 kan:128/1 cm:128/1 ch:128/1 cI:128/1 cR:128/1 one:192/1 zrow:128/1 "
-        "UU:16/96 VV:64/96 SS:48/96 PP:48/96 ZZ:2048/96 ZX:2048/96 I64:128 I64n:128 IDK:128 c64:128/1 cn1:128/1 QQ:384 b0:192 bf:192 cnt:384 Cb:192 CT:256 QG:192 QK:384 FM:512/96 CN:512/96 "
-        "wf:192 wb:1 xg:192 CTI:256 CTR:256",
-    F16: "IDh:128 M16:192 n16:192 S0:384 S1:384 S2:192",
+    BF: "BLK:128 BK8:128 ID:128 I13:128 IDk:128 IDn:128 G64:8 G32:8 Gm:8 W1:144 W8:144 mB:256/96 mD:256/96 "
+        "krow:256/1 TR:256/3 thd:3 e3:3/1 kap:128/1 kan:128/1 cI:128/1 cR:128/1 zrow:128/1 "
+        "VV:96/96 SS:48/96 PP:48/96 ZZ:1280/96 ZX:1280/96 OH:256/96 b0:192 bf:192 cnt:384 Cb:96 QG:192 QK:192 FM:512/96 CN:512/96 "
+        "wf:192 wb:1 xg:192 CTI:128/96 CTR:128/96 CTB:128/96",
+    F16: "IDh:128 M16:192 n16:192 S0:192 S1:192 S2:192",
     I32: "pI:1 pJ:1 wi:1/96 wj:1/96 td:2 mw:192 mv:192 mu:192 a32:96",
-    U16: "oI1:192 oR1:192 sL:12 nL:192 Lb:12 Lc:12 LS:24 aU:96",
+    U16: "oI1:192 oR1:192 sL:12 nL:192 Lb:12 LS:24 aU:96",
 }
 SCRATCH, SHAPE, PLACE = {}, {}, {}
 for _d, _names in OWN_TILES.items():
@@ -53,10 +51,10 @@ PSUM = ["b%d_" % _i for _i in range(8)]
 for _n in PSUM:
     SCRATCH[_n] = ("psum", [128, 512], F32)
     SHAPE[_n], PLACE[_n] = (128, 512), (_n, 0)
-SEMAPHORES = ["qv", "qa", "qp", "qg"] + ["d%d" % i for i in range(8)] + ["rM", "rA", "rB", "rR", "rC"] + ["l%d" % i for i in range(4)]
+SEMAPHORES = ["qv", "qa", "qp", "qg"] + ["d%d" % i for i in range(8)] + ["rM", "rN", "rA", "rB", "rR", "rC"] + ["l%d" % i for i in range(5)]
 
 
-def arrange(calls, other, span, tries=None):
+def arrange(calls, other, span):
     n = len(calls)
     qs = [c[0] for c in calls]
     users = [[] for _ in calls]
@@ -70,7 +68,7 @@ def arrange(calls, other, span, tries=None):
         can = {q: [i for i in range(n) if q in qs[i] and not left[i]] for q in free}
         while len(out) < n:
             t, q = min((max(free[q], min(ready[i] for i in lst)), q) for q, lst in can.items() if lst)
-            rank = {j: way[j] - (0.0 if qs[j][0] == q else SECOND) for j in can[q]}
+            rank = {j: way[j] - (0.0 if qs[j][0] == q else SECOND) if j else 1e9 for j in can[q]}
             time = {j: other[j] if j in other and qs[j][0] != q else calls[j][1] for j in can[q]}
             i = max((j for j in rank if ready[j] <= t + SLACK), key=rank.get)
             u = max((j for j in rank if ready[j] <= t + time[i]), key=rank.get)
@@ -108,10 +106,6 @@ def arrange(calls, other, span, tries=None):
     way = [0.0] * n
     for i in range(n - 1, -1, -1):
         way[i] = calls[i][2] + max([way[u] + WAKE for u in users[i]] + [0.0]) - 1e-6 * i
-    alike = {}
-    for i, c in enumerate(calls):
-        alike.setdefault(c[0] + c[3][0], []).append(i)
-    rng = np.random.RandomState(1)
     out = walk(way)
     best = length(out)
     now, o = list(way), out
@@ -126,17 +120,29 @@ def arrange(calls, other, span, tries=None):
         e = length(o)
         if e < best:
             way, out, best = now, o, e
-    for _ in range(TRIES if tries is None else tries):
+    alike, twin, names = {}, {}, {}
+    for i, c in enumerate(calls):
+        alike.setdefault(c[0] + c[3][0], []).append(i)
+        names.setdefault((c[0], c[3][0].rstrip("01"), c[3][1]), []).append(i)
+    for lst in names.values():
+        if len(lst) % 2 == 0:
+            for a, b in zip(lst[:len(lst) // 2], lst[len(lst) // 2:]):
+                twin[a], twin[b] = b, a
+    rng = np.random.RandomState(1)
+    top = (best, out)
+    for _ in range(TRIES):
         new = list(way)
-        j = int(rng.randint(n))
-        step = float(rng.normal()) * 1.5
-        for i in alike[qs[j] + calls[j][3][0]] if rng.rand() < 0.4 else [j]:
-            new[i] += step
+        for _ in range(1 + int(rng.rand() < 0.4)):
+            j = 2 + int(rng.randint(n - 2))
+            step, x = float(rng.normal()) * (calls[j][3][0] != "oR0"), rng.rand()
+            for i in alike[qs[j] + calls[j][3][0]] if x < 0.3 else [j, twin[j]] if j in twin and x < 0.7 else [j]:
+                new[i] += step
         o = walk(new)
         e = length(o)
-        if e <= best:
-            way, out, best = new, o, e
-    return [(i, q) for i, q, _ in out], best / 2
+        if e <= best + 0.02 * rng.rand():
+            way, best = new, e
+            top = min(top, (e, o))
+    return [(i, q) for i, q, _ in top[1]], top[0] / 2
 
 
 def rank_program(g, core, T, topo):
@@ -146,7 +152,6 @@ def rank_program(g, core, T, topo):
     n_ranks = len(T.cores)
     S = T.sem
     queue = {"v": g.vector, "a": g.scalar, "p": g.tensor, "g": g, "s": g.sync}
-    ndma = [0]
     B0, B1, B2, B3, B4, B5, B6, B7 = PSUM
 
     def R(name, lo=0, hi=None, step=1, p=None):
@@ -157,9 +162,16 @@ def rank_program(g, core, T, topo):
         ap = T[buf][0:p, at + lo:at + hi:step] if step > 1 else T[buf][0:p, at + lo:at + hi]
         return (ap, [(name, lo, hi)], -(-(hi - lo) // step), SIZE[SCRATCH[buf][2]], name in PSUM, False)
 
+    def back(name, n):
+        buf, at = PLACE[name]
+        return (T[buf][0:SHAPE[name][0], at + n - 1:at - 1:-1],) + R(name, 0, n)[1:]
+
     def IND(win, n, off, c0=0, c1=12):
         buf, at = PLACE[off]
         return (T[win][:, 0:n].indirect(T[buf][:, at + c0:at + c1]), [(win, 0, n), (off, c0, c1)], 16 * (c1 - c0), 4, False, True)
+
+    def hbm(name):
+        return (T[name][:], [(name, 0, 1)])
 
     def spans(refs):
         return [s for r in refs if isinstance(r, tuple) for s in r[1]]
@@ -170,30 +182,29 @@ def rank_program(g, core, T, topo):
     calls = []
     seen = {}
     group = {}
+    other = {}
+    span = {}
 
-    def put(q, busy, late, outs, ins, issue, adds=False, after=()):
+    def put(q, busy, late, outs, ins, issue, loose=False, after=()):
         rd, wr = spans(ins), spans(outs)
         deps = set(after)
         for lst, w in ((rd, False), (wr, True)):
             for name, lo, hi in lst:
                 for e in seen.get(name, ()):
                     if name in PSUM and (q != e[1] or q in ("p", "av")):
-                        hit = not (adds and e[5])
+                        hit = not (loose and e[5])
                     else:
-                        hit = (w or e[0]) and e[3] < hi and lo < e[4]
+                        hit = (w or e[0]) and e[3] < hi and lo < e[4] and not (w and loose and e[5])
                     if hit:
                         deps.add(e[2])
         for lst, w in ((rd, False), (wr, True)):
             for name, lo, hi in lst:
                 old = seen.setdefault(name, [])
-                if w and not adds:
+                if w and not loose:
                     old[:] = [e for e in old if not (lo <= e[3] and e[4] <= hi) and name not in PSUM]
-                old.append([w, q, len(calls), lo, hi, adds])
+                old.append([w, q, len(calls), lo, hi, loose])
         calls.append((q, busy, late, (wr + rd)[0], issue, deps))
         return len(calls) - 1
-
-    other = {}
-    span = {}
 
     def emit(q, call, outs, ins, each=1.0, second=None):
         o = outs[0]
@@ -234,6 +245,17 @@ def rank_program(g, core, T, topo):
         else:
             emit("a", lambda: g.scalar.activation(o[0], a[0], func, bias=ap(bias), scale=ap(scale), accum_out=acc[0]), [o, acc], [a, bias, scale])
 
+    def either(o, a):
+        emit("av", {"a": lambda: g.scalar.activation(o[0], a[0], AF.Copy), "v": lambda: g.vector.tensor_copy(o[0], a[0])}, [o], [a])
+
+    def fill(o, c):
+        emit("vg", {"v": lambda: g.vector.memset(o[0], float(c)),
+                    "g": lambda: g.iota(o[0], [[0, o[2]]], c, 0, allow_small_or_imprecise_dtypes=True)}, [o], [], 0.5, 0.13 + 2 * o[2] * CYCLE)
+
+    def lin(o, a, mul, add=0.0):
+        emit("va", {"v": lambda: g.vector.tensor_scalar(o[0], a[0], mul, add, OP.mult, OP.add),
+                    "a": lambda: g.scalar.activation(o[0], a[0], AF.Copy, bias=add, scale=mul)}, [o], [a], 0.5, max(64, o[2]) * CYCLE)
+
     def mms(lst, start=False):
         bank = lst[0][0][1][0][0]
         if start:
@@ -257,48 +279,46 @@ def rank_program(g, core, T, topo):
         c = 0.13 + 2 * o[2] * CYCLE
         put("g", c, c, [o], [], lambda: g.iota(o[0], pat, base, cm, **kw))
 
-    def select(o, a, pat, op, base, cm):
+    def select(o, a, pat, op, base, cm, loose=False):
         c = 0.17 + 2 * o[2] * CYCLE
-        put("g", c, c, [o], [a], lambda: g.affine_select(o[0], a[0], pat, op, 0.0, base, cm))
+        put("g", c, c, [o], [a], lambda: g.affine_select(o[0], a[0], pat, op, 0.0, base, cm), loose)
 
-    def dma(q, a, b, late, after=()):
-        sem = "d%d" % ndma[0]
-        ndma[0] += 1
+    dmas, sent = [], []
+
+    def dma(q, a, b, late):
+        sem = "d%d" % len(dmas)
+        dmas.append(sem)
 
         def issue():
             queue[q].dma_start(a[0], b[0]).then_inc(S[sem], 16)
             return (sem, 16)
-        put(q, 0.05, late, [a], [b], issue, False, after)
+        put(q, 0.05, late, [a], [b], issue)
         return sem
 
-    def hbm(name):
-        return (T[name][:], [(name, 0, 1)])
-
-    sent = []
-
-    def send(src, outs, late=HOP):
+    def send(src, outs, late, half=None):
         ls = "l%d" % len(sent)
+        lo, hi = (0, 192) if half is None else (96 * half, 96 * half + 96)
         tr = []
         for i, (d, land, rs) in enumerate(outs):
             dst = T.cores[d]
             rid, pid, _ = topo.addr(dst)
             es = topo.engines(core, dst)
-            m = len(es) // len(outs)
+            m = len(es) // (len(outs) if half is None else 2)
+            i += half or 0
             tr.append((rid, pid, sum(1 << e for e in es[i * m:(i + 1) * m]), land, rs))
         sent.append((ls, m * len(outs)))
 
         def issue():
             if len(tr) == 1:
                 rid, pid, mask, land, rs = tr[0]
-                g.remote_dma(T[land][:], T[src][:, 0:192], S[rs], S[ls], pid, rid, mask)
+                g.remote_dma(T[land][:, lo:hi], T[src][:, lo:hi], S[rs], S[ls], pid, rid, mask)
             else:
                 g.remote_dma_fused([RemoteDMATransfer(dst_ids=[DstId(rid=rid, pnc=pid)], dma_engine_mask=mask, remote_sem=S[rs],
-                                                      src=T[src][:, 0:192], dst=T[land][:]) for rid, pid, mask, land, rs in tr], local_sem=S[ls])
+                                                      src=T[src][:, lo:hi], dst=T[land][:, lo:hi]) for rid, pid, mask, land, rs in tr], local_sem=S[ls])
             return (ls, m * len(outs))
-        me = put("g", 0.3, late, [], [R(src, 0, 192)], issue)
+        me = put("g", 0.3, late, [], [R(src, lo, hi)], issue)
         for d, land, rs in outs:
-            put("x", 0.0, 0.0, [R(land)], [], (rs, m), False, [me])
-        return me
+            put("x", 0.0, 0.0, [R(land, lo, hi)], [], (rs, m), False, [me])
 
     def issue_all():
         count = {q: 0 for q in "vapg"}
@@ -337,24 +357,16 @@ def rank_program(g, core, T, topo):
     up1, up2 = (rank + 1) % n_ranks, (rank + 2) % n_ranks
     dn1, dn2 = (rank - 1) % n_ranks, (rank - 2) % n_ranks
 
-    def fill(o, c):
-        emit("vg", {"v": lambda: g.vector.memset(o[0], float(c)),
-                    "g": lambda: g.iota(o[0], [[0, o[2]]], c, 0, allow_small_or_imprecise_dtypes=True)}, [o], [], 0.5, 0.13 + 2 * o[2] * CYCLE)
-
-    def lin(o, a, mul, add=0.0):
-        emit("va", {"v": lambda: g.vector.tensor_scalar(o[0], a[0], ap(mul), add, OP.mult, OP.add),
-                    "a": lambda: g.scalar.activation(o[0], a[0], AF.Copy, bias=add, scale=ap(mul))}, [o], [a, mul], 0.5, max(64, o[2]) * CYCLE)
-
-    dma("s", R("mi32"), hbm("m0"), FLAGS["lm"])
-    dma("s", R("X", 0, 4096), hbm("x0"), FLAGS["lx"])
+    dma("s", R("mi32"), hbm("m0"), 1.8)
+    dma("s", R("X", 0, 4096), hbm("x0"), 5.0)
     dma("a", R("od"), hbm("own0"), 2.5)
     ms(R("thi"), 0)
     dma("a", (T.thi[0:128:16, 0:1], [("thi", 0, 8)]), hbm("th"), 8.0)
-    cp(R("oR0"), R("mi32"))
-    send("oR0", [(up1, "oI0", "rM")], FLAGS["ls"])
+    for h, rs in enumerate(("rM", "rN")):
+        cp(R("oR0", 96 * h, 96 * h + 96), R("mi32", 96 * h, 96 * h + 96))
+        send("oR0", [(up1, "oI0", rs)], 3.0, h)
     ms(R("on5"), 1.0)
     iota(R("pI"), [[0, 1]], 0, 1, False)
-    iota(R("cc"), [[1, 16]])
     select(R("ID"), R("on5", 0, 128), [[-1, 128]], OP.is_equal, 0, 1)
     select(R("BLK"), R("on5", 0, 128), [[-16, 8], [0, 16]], OP.is_ge, 0, 1)
     select(R("BLK"), R("BLK"), [[16, 8], [0, 16]], OP.is_ge, 15, -1)
@@ -374,12 +386,10 @@ def rank_program(g, core, T, topo):
     for i in range(3):
         select(R("EX", 512 * i, 512 * i + 512, 1, 96), R("on5", p=96), [[-1, 32], [0, 16]], OP.is_equal, -32 * i, 1)
     for i in range(4):
-        fill(R("CZI", 384 * i, 384 * i + 384), 0)
-        fill(R("CZR", 384 * i, 384 * i + 384), 0)
+        fill(R("CZ", 384 * i, 384 * i + 384), 0)
     ts(R("pJ"), R("pI"), 15, OP.bitwise_and)
     cp(R("p15"), R("pJ"))
     ts(R("kc"), R("pJ"), -1.0, OP.mult, 15.0, OP.add)
-    ts(R("LTm"), R("cc"), R("p15"), OP.is_gt)
     for name, c in (("W1", 1.0), ("W8", 8192.0)):
         fill(R(name), 0)
         lin(R(name, 15, 143, 16), R("BLK", 0, 128, 16), c)
@@ -389,21 +399,15 @@ def rank_program(g, core, T, topo):
     for name, c in (("I13", 2.0 ** -13), ("IDk", -KILL), ("IDn", -1.0), ("IDf", 1.0)):
         lin(R(name), R("ID"), c)
     lin(R("BK8"), R("BLK"), 8192.0)
-    ms(R("ch"), 0.5)
-    for name, c in (("cm", -2048), ("cI", -131072 if FLAGS["both"] else 163840), ("cR", 65536 if FLAGS["both"] else 98304), ("zrow", 0)):
+    for name, c in (("cI", 2 ** 17 + 32768), ("cR", 2 ** 16 + 32768), ("zrow", 0)):
         fill(R(name), c)
-    for i in range(8 if FLAGS["both"] else 6):
+    for i in range(5):
         fill(R("ZZ", 256 * i, 256 * i + 256), 0)
-    if FLAGS["both"]:
-        for name, c in (("I64", 64.0), ("I64n", -64.0), ("IDK", KILL)):
-            lin(R(name), R("ID"), c)
-        fill(R("c64"), 64)
-        fill(R("cn1"), -1)
     cp(R("ob"), R("od"))
     dma("s", (T.ow[0:128:16, 0:4096], [("ow", 0, 4096)]), R("ob"), 5.0)
     dma("s", R("nbw"), (T.nb[:], [("ob", 0, 1), ("oR0", 0, 1)]), 10.0)
     for r in range(1, 16):
-        lin(R("LO", 128 * r, 128 * r + 128), R("BLK"), R("LTm", r, r + 1))
+        select(R("LO", 128 * r, 128 * r + 128), R("BLK"), [[16, 8], [0, 16]], OP.is_ge, r - 1, -1)
     fill(R("X", 4096, 4288), 0)
     fill(R("MR0", 192, 384), 0)
     fill(R("MR1", 192, 384), 0)
@@ -422,101 +426,80 @@ def rank_program(g, core, T, topo):
     ts(R("e3"), R("e3"), 0.0, OP.max)
     mms([(R(B5, 0, 128, 1, 3), R("thd"), R("BLK")), (R(B5, 0, 128, 1, 3), R("e3"), R("krow", 0, 128))], True)
     for h in (0, 1):
-        cp(R("TR", 128 * h, 128 * h + 128), R(B5, 0, 128, 1, 3))
+        act(R("TR", 128 * h, 128 * h + 128), R(B5, 0, 128, 1, 3))
 
     def part(name, q, step=1):
         return R(name, 768 * q, 768 * q + 768, step)
-
-    def either(o, a):
-        emit("av", {"a": lambda: g.scalar.activation(o[0], a[0], AF.Copy), "v": lambda: g.vector.tensor_copy(o[0], a[0])}, [o], [a])
 
     def gather(v, off, n):
         for lo in range(0, 192, n):
             either(R(v, 16 * lo, 16 * (lo + n)), IND("X", 4096, off, lo, lo + n))
 
-    def row(bank, n, l, start=True):
-        mm(R(bank, 0, n), R(l, 0, 128), R("on5", 0, n, 1, 1), start)
+    def row(bank, l):
+        mm(R(bank, 0, 192), R(l), R("on5", 0, 192, 1, 1), True)
 
-    def group_sum(place, src, w, halves=(0, 1)):
-        for h in halves:
-            bank, at = place[h] if isinstance(place, list) else (place, 128 * h)
-            for k0 in (0, 8):
-                mms([(R(bank, at + k, at + 128, 16, 96), R(src, 1536 * h + k, 1536 * h + 1536, 16), R(w)) for k in range(k0, k0 + 8)])
+    def opened(bank, n, rows):
+        mm(R(bank, 0, 256, 1, 96), R("on5", 0, 96, 1, n), R(rows), True)
 
-    def Z(i, h=None):
-        return R("ZZ", 256 * i, 256 * i + 256, 16) if h is None else R("ZZ", 256 * i + 128 * h, 256 * i + 128 * h + 128, 16)
+    def group_sum(bank, src, w, h, same=False):
+        for k0 in (0, 8):
+            mms([(R(bank, 128 * h + k, 128 * h + 128, 16, 96), R(src, 1536 * h + (0 if same else k), 1536 * h + 1536, 16), R(w))
+                 for k in range(k0, k0 + 8)])
 
-    def from_keys(bank, i, start=False, halves=(0, 1)):
-        lo, n = 256 * i + 128 * halves[0], 128 * len(halves)
-        scan(R("ZX", lo, lo + n), R("m01", 0, n, 1, 96), R("ZZ", lo, lo + n), OP.mult, OP.add)
-        lst = [(R(bank, 96 * h, 96 * h + 96), R("ZX", 256 * i + 128 * h, 256 * i + 128 * h + 128), R("ID", 0, 96, 1, 96)) for h in halves]
+    def Z(i):
+        return R("ZZ", 256 * i, 256 * i + 256, 16)
+
+    def turn_over(bank, src, at, start):
+        lst = [(R(bank, 96 * h, 96 * h + 96), R(src, at + 128 * h, at + 128 * h + 128), R("ID", 0, 96, 1, 96)) for h in (0, 1)]
         if start:
             for m in lst:
                 mms([m], True)
         else:
             mms(lst)
 
-    def to_list(bank, src, w, n=192, start=False):
+    def from_keys(bank, i, start=False):
+        scan(R("ZX", 256 * i, 256 * i + 256), R("m01", 0, 256, 1, 96), R("ZZ", 256 * i, 256 * i + 256), OP.mult, OP.add)
+        turn_over(bank, "ZX", 256 * i, start)
+
+    def to_list(bank, src, w, n=192, start=True):
         mms([(R(bank, 0, n // 16), R(w, 15 - j, 143 - j), R(src, j, n, 16)) for j in range(16)], start)
 
     turn = [0]
 
-    def extremes(v, mx, mn, q):
-        scan(part(mx, q), R("m01"), part(v, q), OP.mult, OP.max)
-        scan(part(mn, q), R("m512"), part(v, q), OP.add, OP.min)
-
-    def centres(mx, mn, cz, q, n=1):
+    def centres(mx, mn, q, n, out):
         turn[0] += 1
-        bank = PSUM[6 + turn[0] % 2]
-        o = R(bank, 0, 48 * n)
+        o = R(PSUM[6 + turn[0] % 2], 0, 48 * n)
         mms([(o, R("IDh"), R(m, 768 * q + 15, 768 * (q + n), 16)) for m in (mx, mn)], True)
-        ts(R(cz, 768 * (q % 2), 768 * (q % 2 + n), 16), R(bank, 0, 48 * n), R1, OP.add, R1, OP.subtract)
+        ts(out, o, R1, OP.add, R1, OP.subtract)
 
-    def turned(mx, mn, ct, h):
-        turn[0] += 1
-        o = R(PSUM[6 + turn[0] % 2], 0, 128, 1, 96)
-        mms([(o, R(m, 1536 * h + 15, 1536 * h + 1536, 16), R("IDh")) for m in (mx, mn)], True)
-        ts(R(ct, 128 * h, 128 * h + 128, 1, 96), o, R1, OP.add, R1, OP.subtract)
-
-    def spread(cz, cx, q, free=False):
-        o, z = part(cx, q), part(cz, q % 2)
+    def spread(q, free=False):
+        o, z = part("CX", q), part("CZ", q % 2)
         if not free:
             return scan(o, R("m01"), z, OP.mult, OP.add)
-        w = IND(cz, 1536, "aU", 48 * (q % 2), 48 * (q % 2) + 48)
+        w = IND("CZ", 1536, "aU", 48 * (q % 2), 48 * (q % 2) + 48)
         emit("va", {"v": lambda: g.vector.tensor_tensor_scan(o[0], R("m01")[0], z[0], 0.0, OP.mult, OP.add),
                     "a": lambda: g.scalar.activation(o[0], w[0], AF.Copy)}, [o], [R("m01"), z, (0, w[1], 0)], 0.5, (70 + 1.5 * 768) * CYCLE)
 
-    def apart(v, ct, d, h, banks, first=None):
-        for i in range(3 * h, 3 * h + 3):
-            bank = banks[i % len(banks)]
-            lst = [(R(bank), R("IDn"), R(v, 512 * i, 512 * i + 512)),
-                   (R(bank), R(ct, 128 * h, 128 * h + 128, 1, 96), R("EX", 512 * (i % 3), 512 * (i % 3) + 512, 1, 96))]
-            if first:
-                lst += [(R(bank, 0, 512, 16), R("ID"), R(v, 512 * i, 512 * i + 512, 16)), (R(bank, 0, 512, 16), R("IDn"), R(first, 32 * i, 32 * i + 32))]
-            mms(lst, True)
-            act(R(d, 512 * i, 512 * i + 512), R(bank), AF.Abs)
-
-    def distances(bank, v, mx, mn, cz, cx, ct, d, free, both=False):
-        if not both:
-            group_sum(bank, v, "Gm", [1])
-        for q in range(4):
-            extremes(v, mx, mn, q)
-        turned(mx, mn, ct, 0)
-        apart(v, ct, d, 0, (B3, B4))
-        if both:
-            turned(mx, mn, ct, 1)
-            apart(v, ct, d, 1, (B4, B3))
-            return group_sum(bank, d, "G32")
-        for q in (2, 3):
-            centres(mx, mn, cz, q)
-            spread(cz, cx, q, free)
-            larger(v, cx, d, q)
-        group_sum(bank, d, "G32", [0])
-        group_sum(bank, d, "G64", [1])
+    def apart(v, ct, d, h, banks):
+        for i in range(3):
+            cols = (1536 * h + 512 * i, 1536 * h + 512 * i + 512)
+            mms([(R(banks[i]), R("IDn"), R(v, *cols)), (R(banks[i]), R(ct), R("EX", 512 * i, 512 * i + 512, 1, 96))], True)
+            act(R(d, *cols), R(banks[i]), AF.Abs)
 
     def larger(v, cx, d, q):
         tt(part(v, q, 16), part(v, q, 16), part(cx, q, 16), OP.max)
         scan(part(d, q), part(cx, q), part(v, q), OP.min, OP.max)
+
+    def first_half(bank, v, mx, mn, ct, d):
+        group_sum(bank, v, "Gm", 1)
+        for q in range(4):
+            scan(part(mx, q), R("m01"), part(v, q), OP.mult, OP.max)
+            scan(part(mn, q), R("m512"), part(v, q), OP.add, OP.min)
+        turn[0] += 1
+        o = R(PSUM[6 + turn[0] % 2], 0, 128, 1, 96)
+        mms([(o, R(m, 15, 1536, 16), R("IDh")) for m in (mx, mn)], True)
+        ts(R(ct), o, R1, OP.add, R1, OP.subtract)
+        apart(v, ct, d, 0, (B3, B4, B2))
 
     def least(f, at, bank):
         scan(R(f, at, at + 256), R("mB"), R(bank, 0, 256, 1, 96), OP.add, OP.min)
@@ -524,244 +507,137 @@ def rank_program(g, core, T, topo):
     def largest(f, at, bank):
         scan(R(f, at, at + 256), R("mD"), R(bank, 0, 256, 1, 96), OP.add, OP.max)
 
-    def rest(o, f, lo, hi, turn=False):
+    def rest(o, f, lo, hi, turned=False):
         ends, r = R(f, lo + 15, hi, 16), R("rS" if f == "FS" else "rK", lo // 16, hi // 16)
         ts(r, ends, R32, OP.add, R32, OP.subtract)
-        if turn:
+        if turned:
             tt(o, r, ends, OP.subtract)
         else:
             tt(o, ends, r, OP.subtract)
-
-    def clamp(o, bank):
-        ts(o, R(bank, 0, 192), -0.25, OP.max, 0.25, OP.min)
 
     def play(t):
         oI, oR = "oI%d" % t, "oR%d" % t
         IC, MR = "IC%d" % t, "MR%d" % t
         last = t == 1
-        KI, KR, E = B0, B1, (B2, B3)
-        KE, KB = ([(E[0], 0), (E[1], 0)], [(E[0], 128), (E[1], 128)]) if FLAGS["split"] else E
-        lim = R("lim") if t else -15.5
-
-        def opened(bank, n, rows):
-            mm(R(bank, 0, 256, 1, 96), R("on5", 0, 96, 1, n), R(rows), True)
-        gather("VI", oI, FLAGS["n1"])
-        gather("VR", oR, FLAGS["n1"])
+        KI, KR, KE, KB = B0, B1, B2, B3
+        gather("VI", oI, 24)
+        gather("VR", oR, 24)
         opened(KI, 1, "krow")
         opened(KR, 1, "krow")
-        opened(E[0], 3, "TR")
         ts(R("M16"), R(oI), -2048.0, OP.add)
-        distances(KI, "VI", "XI", "NI", "CZI", "CXI", "CTI", "DA", False, FLAGS["bi"])
-        if not FLAGS["swap"]:
-            centres("XI", "NI", "CZI", 0, 2)
-            for q in (0, 1):
-                spread("CZI", "CXI", q, FLAGS["fi"])
-            group_sum(KE, "CXI", "Gm", [0])
-        elif not FLAGS["bi"]:
-            turned("XI", "NI", "CTI", 1)
-        distances(KR, "VR", "XR", "NR", "CZR", "NR", "CTR", "DR", FLAGS["fr"], FLAGS["br"])
-        centres("XR", "NR", "NR", 0, 4 if FLAGS["br"] else 2)
-        opened(E[1], 3, "TR")
-        if not FLAGS["swap"]:
-            group_sum(KE, "CXI", "Gm", [1])
+        first_half(KI, "VI", "XI", "NI", "CTI", "DA")
+        for q in (2, 3):
+            centres("XI", "NI", q, 1, part("CZ", q % 2, 16))
+            spread(q)
+            larger("VI", "CX", "DA", q)
+        group_sum(KI, "DA", "G32", 0)
+        group_sum(KI, "DA", "G64", 1)
+        first_half(KR, "VR", "XR", "NR", "CTR", "DR")
+        centres("XR", "NR", 2, 2, R("CR", 96, 192))
+        for k in range(16):
+            select(R("NR", 1536 + k, 3072, 16), R("CR", 96, 192), [[0, 96]], OP.is_ge, 0, 0, True)
+        for q in (2, 3):
+            larger("VR", "NR", "DR", q)
+        group_sum(KR, "DR", "G32", 0)
+        group_sum(KR, "DR", "G64", 1)
+        centres("XR", "NR", 0, 2, R("CR", 0, 96))
+        opened(KE, 3, "TR")
+        opened(KB, 3, "TR")
+        group_sum(KE, "CX", "Gm", 1)
         least("FK", 0, KI)
-        row(B5, 192, "kap")
-        mm(R(B5, 0, 192), R("I13"), R("M16"))
-        rest(Z(4), "FK", 0, 256)
-        from_keys(B5, 4)
-        clamp(R("S2"), B5)
-        row(B5, 12, "cm")
-        row(B5, 12, "ch", False)
-        to_list(B5, "S2", "W8")
-        ts(R("rs"), R(B5, 0, 12), R4096, OP.add, R4096, OP.subtract)
-        tt(R("SW", 0, 12), R(B5, 0, 12), R("rs"), OP.subtract)
-        ts(R("sL"), R("SW", 0, 12), MID, OP.add)
+        scan(back("FB", 256), R("mB"), back("FK", 256), OP.add, OP.min)
+        tt(R("OH"), R(KI, 0, 256, 1, 96), R("FB"), OP.is_equal)
+        turn_over(B5, "OH", 0, True)
+        tt(R("S2"), R(B5, 0, 192), R("M16"), OP.mult)
+        to_list(B5, "S2", "W1")
+        ts(R("sL"), R(B5, 0, 12), 2048.0, OP.add)
+        ts(R("SW", 0, 12), R(B5, 0, 12), 2048.0 - MID, OP.add)
+        rest(R("VV", 80, 96), "FK", 0, 256)
         either(R("b0"), IND("ow", 4096, "sL"))
         cp(R("nL"), IND("nbw", 4096, "sL"))
         largest("FK", 256, KI)
         largest("FK", 512, KR)
-        rest(Z(7) if FLAGS["both"] else R("UU"), "FK", 256, 512, FLAGS["both"])
-        rest(Z(5), "FK", 512, 768, True)
-        gather("V2", "nL", FLAGS["n2"])
-        to_list(B5, "b0", "W1", 192, True)
+        rest(R("VV", 32, 48), "FK", 256, 512)
+        rest(Z(4), "FK", 512, 768, True)
+        gather("V2", "nL", 32)
+        to_list(B5, "b0", "W1")
         mm(R(B4, 0, 192), R("BLK"), R("b0"), True)
         either(R("bf"), R(B4, 0, 192))
-        ts(R("Lc"), R(B5, 0, 12), 16.0, OP.mult)
         ts(R("SW", 12, 24), R(B5, 0, 12), -MID, OP.add)
         cp(R("Lb"), R(B5, 0, 12))
-        if FLAGS["swap"]:
-            for h, cz in enumerate(("CZI", "CZR")):
-                either(R(cz, 0, 1536, 16), IND("NR", 3072, "Lc", 6 * h, 6 * h + 6))
-                spread(cz, "CXI", 2 * h, FLAGS["fi"])
-                spread(cz, "CXI", 2 * h + 1, FLAGS["fi"])
-        else:
-            either(R("Cb"), IND("NR", 3072, "Lc"))
-            for h in (0, 1):
-                mm(R(B4, 128 * h, 128 * h + 128, 1, 96), R("Cb", 96 * h, 96 * h + 96), R("ID"), True)
-            either(R("CT", p=96), R(B4, 0, 256, 1, 96))
+        either(R("Cb"), IND("CR", 192, "Lb", 6, 12))
+        mm(R(B7, 0, 128, 1, 96), R("Cb"), R("ID"), True)
+        either(R("CTB"), R(B7, 0, 128, 1, 96))
+        either(R("CZ", 0, 1536, 16), IND("CR", 192, "Lb", 0, 6))
+        group_sum(KB, "CZ", "Gm", 0, True)
+        for q in (0, 1):
+            spread(q, True)
         ts(R("n16"), R("nL"), -2048.0, OP.add)
         for c in range(12):
             ts(R("EQ", 208 * c, 192 * c + 192), R("bf", 16 * c, 192), -MID, OP.add, R("SW", 12 + c, 13 + c), OP.is_equal)
-        row(B6, 192, "zrow")
+        row(B6, "zrow")
         for c0, c1 in ((0, 4), (4, 11)):
             mms([(R(B6, 16 * c + 16, 192), R("BLK"), R("EQ", 208 * c + 16, 192 * c + 192)) for c in range(c0, c1)])
         mms([(R(B6, r, 192, 16), R("LO", 128 * r, 128 * r + 128), R("EQ", r, 2304, 208)) for r in range(1, 16)])
         for h in (0, 1):
             either(R("cnt", 192 * h, 192 * h + 192), R(B6, 0, 192))
         mm(R(B7, 0, 24), R("IDf"), R("SW"), True)
-        to_list(B7, "cnt", "W8", 384)
+        to_list(B7, "cnt", "W8", 384, False)
         tt(R("l1"), R(B7, 0, 24), R("aC"), OP.min)
         ts(R("LS"), R("l1"), MID, OP.add)
-        from_keys(B7, 5, True)
+        from_keys(B7, 4, True)
         act(R("QR"), R(B7, 0, 192), AF.Square, R("kc"))
-        if FLAGS["both"]:
-            from_keys(B7, 7, True)
-            for h in (0, 1):
-                mm(R(B7, 192 + 96 * h, 288 + 96 * h), R("ZX", 1024 + 128 * h, 1152 + 128 * h), R("ID", 0, 96, 1, 96), True)
-            act(R("QQ"), R(B7, 0, 384), AF.Square, R("kc"))
         either(R("QG"), IND("QR", 192, "Lb"))
         either(R("Mg"), IND(MR, 192, "Lb"))
-        if FLAGS["swap"]:
-            group_sum(KB, "V2", "Gm")
-            group_sum(KB, "CXI", "Gm")
-            apart("V2", "CTI", "D2", 0, (B4, B5, B0))
-            apart("V2", "CTI", "D2", 1, (B4, B5, B0))
-            for q in range(4):
-                larger("V2", "CXI", "DB", q)
-            group_sum(KB, "DB", "G64")
-        else:
-            group_sum(KE, "V2", "Gm")
-            for h in (0, 1):
-                apart("V2", "CT", "DB", h, (B4, B5, B0) if FLAGS["b3"] else (B4, B5))
-            group_sum(KB, "DB", "G32")
-            for q in range(4):
-                larger("V2", "CXI", "D2", q)
-        group_sum(KE, "D2", "G32" if FLAGS["swap"] else "G64")
+        group_sum(KB, "V2", "Gm", 0)
+        group_sum(KE, "V2", "Gm", 1)
+        apart("V2", "CTI", "D2", 0, (B4, B5, B0))
+        apart("V2", "CTB", "DB", 1, (B4, B5, B0))
+        for q in range(4):
+            larger("V2", "CX", "D2" if q > 1 else "DB", q)
+        group_sum(KE, "D2", "G32", 0)
+        group_sum(KB, "DB", "G64", 0)
+        group_sum(KE, "D2", "G64", 1)
+        group_sum(KB, "DB", "G32", 1)
         if not last:
             act(R("xg"), IND("X", 4096, "sL"), AF.Relu, -16.0)
             cp(IND("X", 4288, "LS"), R("xg"))
-        if FLAGS["both"]:
-            return finish(t, lim, E)
         for bank, l in ((B0, "kan"), (B1, "kap")):
-            row(bank, 192, l)
+            row(bank, l)
             mm(R(bank, 0, 192), R("I13"), R("n16"))
         mm(R(B5, 0, 192), R("IDn"), R("cnt", 0, 192), True)
-        row(B6, 192, "cI")
+        row(B6, "cI")
         mm(R(B6, 0, 192), R("IDk"), R("cnt", 0, 192))
-        row(B7, 192, "cR")
+        row(B7, "cR")
         mm(R(B7, 0, 192), R("IDk"), R("QG"))
-        tt(R("SS", 32, 48), R("UU"), Z(4), OP.add)
-        if not FLAGS["split"]:
-            for i in (0, 1):
-                act(R("FM", 256 * i, 256 * i + 256), R(E[i], 0, 256, 1, 96), AF.Sign, lim, -1.0)
-                scan(R("CN", 256 * i, 256 * i + 256), R("m01", 0, 256, 1, 96), R("FM", 256 * i, 256 * i + 256), OP.mult, OP.add)
-                least("FS", 768 * i, E[i])
-                largest("FS", 256 + 256 * i, E[i])
-                rest(R("VV", 32 * i, 32 * i + 32), "FS", 512 * i, 512 * i + 512)
-            tt(Z(3), R("CN", 15, 256, 16), R("CN", 271, 512, 16), OP.is_gt)
-            tt(R("SS", 0, 32), R("VV", 0, 32), R("VV", 32, 64), OP.add)
-            for i, bank in enumerate((B0, B1, B4)):
-                s, p = (R(n, 16 * i, 16 * i + 16) for n in ("SS", "PP"))
-                tt(p, s, Z(3), OP.mult)
-                tt(Z(i), R("VV", 32 + 16 * i, 48 + 16 * i) if i < 2 else Z(4), p, OP.subtract)
-                from_keys(bank, i, i == 2)
-            from_keys(B5, 3)
-        for h in (0, 1) if FLAGS["split"] else ():
-            act(R("FM", 256 * h, 256 * h + 256), R(E[h], 0, 256, 1, 96), AF.Sign, lim, -1.0)
-            scan(R("CN", 256 * h, 256 * h + 256), R("m01", 0, 256, 1, 96), R("FM", 256 * h, 256 * h + 256), OP.mult, OP.add)
-            least("FS", 512 * h, E[h])
-            largest("FS", 512 * h + 256, E[h])
-            rest(R("VV", 32 * h, 32 * h + 32), "FS", 512 * h, 512 * h + 512)
-            best_i, best_r, worst_i, worst_r = (R("VV", 32 * h + 8 * i, 32 * h + 8 * i + 8) for i in range(4))
-            won = Z(3, h)
-            tt(won, R("CN", 256 * h + 15, 256 * h + 128, 16), R("CN", 256 * h + 143, 256 * h + 256, 16), OP.is_gt)
-            for i, (bank, u, v) in enumerate(((B0, best_i, worst_r), (B1, worst_i, best_r), (B4, None, Z(4, h)))):
-                s, p = (R(n, 16 * i + 8 * h, 16 * i + 8 * h + 8) for n in ("SS", "PP"))
-                if u:
-                    tt(s, u, v, OP.add)
-                tt(p, s, won, OP.mult)
-                tt(Z(i, h), v, p, OP.subtract)
-                from_keys(bank, i, i == 2, [h])
-            from_keys(B5, 3, False, [h])
-        clamp(R("S0", 0, 192), B0)
-        clamp(R("S1", 0, 192), B1)
-        act(R("QK", 0, 192), R(B4, 0, 192), AF.Square, R("kc"))
-        mm(R(B6, 0, 192), R("BK8"), R("S0", 0, 192))
-        mm(R(B6, 0, 192), R("IDk"), R("QK", 0, 192))
-        act(R(IC), R(B6, 0, 192), AF.Relu)
-        if not last:
-            send(IC, [(dn1, "inA", "rA"), (up1, "inB", "rB")])
-        else:
-            send(IC, [(dn2, "inC", "rC")])
-        mm(R(B7, 0, 192), R("BK8"), R("S1", 0, 192))
-        act(R("zr"), R(B7, 0, 192), AF.Relu)
-        tt(IND(MR, 384, "LS", 12, 24), R("zr"), R("Mg"), OP.max)
-        if not last:
-            send(MR, [(up2, "inM", "rR")])
-        act(R("wf"), R(B5, 0, 192), AF.Relu, acc=R("wc"))
-        mm(R(B2, 0, 192), R("BLK"), R("b0"), True)
-        mm(R(B2, 0, 192), R("ID"), R("wf"))
-        act(R("xa"), R(B2, 0, 192), AF.Copy, 0.0, R("e0"))
-        act(R("ya"), R(B2, 0, 192), AF.Relu, R("eB"), R("e192"))
-        tt(IND("ow", 4288, "LS"), R("xa"), R("ya"), OP.subtract)
-        if not last:
-            act(R("wb"), R("wc"))
-            mm(R(B3, 0, 1, 1, 96), R("on5", 0, 96), R("wb"), True)
-            ts(R("wi"), R(B3, 0, 1, 1, 96), 0.0625, OP.mult)
-            ts(R("wj"), R("wi"), 63, OP.bitwise_and)
-            ts(R("lim"), R("wj"), 32.0, OP.mult, -15.5, OP.add)
-
-    def finish(t, lim, E):
-        IC, MR = "IC%d" % t, "MR%d" % t
-        last = t == 1
-
-        def turn_to(bank, at, i, w):
-            mms([(R(bank, at + 96 * h, at + 96 * h + 96), R("ZX", 256 * i + 128 * h, 256 * i + 128 * h + 128), R(w, 0, 96, 1, 96)) for h in (0, 1)])
-
-        def repeat(i, n):
-            scan(R("ZX", 256 * i, 256 * (i + n)), R("m01", 0, 256 * n, 1, 96), R("ZZ", 256 * i, 256 * (i + n)), OP.mult, OP.add)
-        for bank in (B0, B1):
-            row(bank, 384, "kap")
-            mms([(R(bank, at, at + 192), R("I13"), R("n16")) for at in (0, 192)] + [(R(bank, 0, 192), R("c64"), R("on5", 0, 192, 1, 1))])
-        mm(R(B4, 0, 384), R("IDn"), R("QQ"), True)
-        mm(R(B4, 0, 192), R("cn1"), R("on5", 0, 192, 1, 1))
-        mm(R(B5, 0, 192), R("IDn"), R("cnt", 0, 192), True)
-        row(B6, 192, "cI")
-        mm(R(B6, 0, 192), R("IDk"), R("cnt", 0, 192))
-        row(B7, 192, "cR")
-        mm(R(B7, 0, 192), R("IDk"), R("QG"))
-        for i in (0, 1):
-            act(R("FM", 256 * i, 256 * i + 256), R(E[i], 0, 256, 1, 96), AF.Sign, lim, -1.0)
+        for i, bank in enumerate((KE, KB)):
+            act(R("FM", 256 * i, 256 * i + 256), R(bank, 0, 256, 1, 96), AF.Sign, R("lim") if t else -15.5, -1.0)
             scan(R("CN", 256 * i, 256 * i + 256), R("m01", 0, 256, 1, 96), R("FM", 256 * i, 256 * i + 256), OP.mult, OP.add)
-            least("FS", 512 * i, E[i])
-            largest("FS", 512 * i + 256, E[i])
-            rest(R("ZZ", 512 * i, 512 * i + 512, 16), "FS", 512 * i, 512 * i + 512)
-            repeat(2 * i, 2)
-            turn_to((B0, B1)[i], 192 * i, 2 * i, "ID")
-            turn_to((B1, B0)[i], 192 * i, 2 * i + 1, "IDn")
-        tt(Z(6), R("CN", 15, 256, 16), R("CN", 271, 512, 16), OP.is_gt)
-        repeat(6, 1)
-        for bank in (B0, B1):
-            turn_to(bank, 0, 6, "I64n")
-            turn_to(bank, 192, 6, "I64")
-        turn_to(B4, 0, 6, "ID")
-        turn_to(B4, 192, 6, "IDn")
-        turn_to(B5, 0, 6, "ID")
-        ts(R("S0"), R(B0, 0, 384), -0.25, OP.max, 0.25, OP.min)
-        ts(R("S1"), R(B1, 0, 384), -0.25, OP.max, 0.25, OP.min)
-        act(R("QK"), R(B4, 0, 384), AF.Relu, 1.0)
-        mms([(R(B6, 0, 192), R("BK8"), R("S0", at, at + 192)) for at in (0, 192)])
-        mms([(R(B6, 0, 192), R("IDK"), R("QK", at, at + 192)) for at in (0, 192)])
+            least("FS", 768 * i, bank)
+            largest("FS", 256 + 256 * i, bank)
+            rest(R("VV", 48 * i, 48 * i + 32), "FS", 512 * i, 512 * i + 512)
+        tt(Z(3), R("CN", 15, 256, 16), R("CN", 271, 512, 16), OP.is_gt)
+        tt(R("SS"), R("VV", 0, 48), R("VV", 48, 96), OP.add)
+        for i in range(3):
+            tt(R("PP", 16 * i, 16 * i + 16), R("SS", 16 * i, 16 * i + 16), Z(3), OP.mult)
+        tt(R("ZZ", 0, 768, 16), R("VV", 48, 96), R("PP"), OP.subtract)
+        for i, bank in enumerate((B0, B1, B4, B5)):
+            from_keys(bank, i, i == 2)
+        for s, bank in (("S0", B0), ("S1", B1)):
+            ts(R(s), R(bank, 0, 192), -0.25, OP.max, 0.25, OP.min)
+        act(R("QK"), R(B4, 0, 192), AF.Square, R("kc"))
+        mm(R(B6, 0, 192), R("BK8"), R("S0"))
+        mm(R(B6, 0, 192), R("IDk"), R("QK"))
         act(R(IC), R(B6, 0, 192), AF.Relu)
         if not last:
-            send(IC, [(dn1, "inA", "rA"), (up1, "inB", "rB")])
+            send(IC, [(dn1, "inA", "rA"), (up1, "inB", "rB")], HOP)
         else:
-            send(IC, [(dn2, "inC", "rC")])
-        mms([(R(B7, 0, 192), R("BK8"), R("S1", at, at + 192)) for at in (0, 192)])
+            send(IC, [(dn2, "inC", "rC")], 0.8 * HOP)
+        mm(R(B7, 0, 192), R("BK8"), R("S1"))
         act(R("zr"), R(B7, 0, 192), AF.Relu)
         tt(IND(MR, 384, "LS", 12, 24), R("zr"), R("Mg"), OP.max)
         if not last:
-            send(MR, [(up2, "inM", "rR")])
+            send(MR, [(up2, "inM", "rR")], 0.8 * HOP)
         act(R("wf"), R(B5, 0, 192), AF.Relu, acc=R("wc"))
         mm(R(B2, 0, 192), R("BLK"), R("b0"), True)
         mm(R(B2, 0, 192), R("ID"), R("wf"))
@@ -775,19 +651,18 @@ def rank_program(g, core, T, topo):
             ts(R("wj"), R("wi"), 63, OP.bitwise_and)
             ts(R("lim"), R("wj"), 32.0, OP.mult, -15.5, OP.add)
 
-    def merged(old, new, both, words, out, n):
-        for lo in range(0, 192, n):
-            tt(R(both, lo, lo + n), R(old, lo, lo + n), R(new, lo, lo + n), OP.max)
-            ts(R(words, lo, lo + n), R(both, lo, lo + n), 4095, OP.bitwise_and)
-            cp(R(out, lo, lo + n), R(words, lo, lo + n))
+    def merged(old, new, both, words, out):
+        for lo in (0, 96):
+            tt(R(both, lo, lo + 96), R(old, lo, lo + 96), R(new, lo, lo + 96), OP.max)
+            ts(R(words, lo, lo + 96), R(both, lo, lo + 96), 4095, OP.bitwise_and)
+            cp(R(out, lo, lo + 96), R(words, lo, lo + 96))
 
-    constants = [len(calls)]
     play(0)
-    merged("inM", "inB", "mu", "mw", "oI1", 192 // FLAGS["mh"])
-    merged("MR0", "inA", "mv", "mi32", "oR1", 192 // FLAGS["mh"])
+    merged("inM", "inB", "mu", "mw", "oI1")
+    merged("MR0", "inA", "mv", "mi32", "oR1")
     cp(R("MR1", 0, 192), R("mi32"))
     play(1)
-    merged("MR1", "inC", "mv", "mi32", "yo", 96)
+    merged("MR1", "inC", "mv", "mi32", "yo")
     stores = [dma("a", hbm("yown"), (T.ow[0:128:16, 0:4096], [("ow", 0, 4096)]), 2.5), dma("s", hbm("ym"), R("yo"), 2.5)]
     count = issue_all()
     for q in count:

@@ -7,33 +7,47 @@ AF = ActivationFunctionType
 F32, BF, I32, U16, F16 = "float32", "bfloat16", "int32", "uint16", "float16"
 SIZE = {F32: 4, I32: 4, BF: 2, U16: 2, F16: 2}
 BIG = float(2 ** 22)
-KILL = float(2 ** 18)
 R1, R32 = 1.5 * 2 ** 23, 1.5 * 2 ** 28
 MID = 2047.5
-CYCLE, WAKE, SLACK, HOP = 0.00087, 0.18, 0.05, 2.0
-AHEAD, SECOND = 1.0, 1.6
-TRIES = 4000
-ORDER = []
+KP = 102
+ALL = slice(None)
+CYCLE, WAKE, HOP = 0.00087, 0.18, 2.0
+TRIES = 90000
+FAR, WARM = 0.75, 0.012
+ROUND = {
+    "v": "[BKn [ID4 [P4 [mv*2 [mi32*2 [mu*2 [mw*2 [oI*2 VA*3 XB NB XB NB VA XB NB XB NB VA XA CTI VA XA*5 NR XR*2 NR CA XR DI*2 XR DI*2 NR*2 M16 "
+         "(aC FK CT0 (CN FB XR OH NR*2 XR S2 XR*2 NR*2 sL nL FK SW CS rK bf VN pb VN Lb Cb VN SW CTB VN*3 EQ R16 DJ EQ CB EQ DK DJ DK*2 EQ DJ*2 VV DK n16 "
+         "FS VR FS DS rS pc DS VV CN l1 SS ZZ LS DS PP DS ZZ ZX*3 FR S0 FB S1 pi OR LI X MR wi ow wj lim",
+    "a": "VR VB*4 VR*3 (TR*2 DA*3 VR*2 DR*3 b0 CR V2*3 D2*3 DB CB DB*2 xg FM cnt FM IV QK wf IC zr wb WR ya xa",
+    "p": "KI CTI DA*4 CA DA*2 KI*10 CT0 DR*4 OH DR*2 sL KR*2 CR KR bf Fa*2 Fb KR*2 D2*4 CTB D2*2 DB*2 CB DB*4 EQ Fb Fa Fb Fa*3 Fb*2 Fa*9 EQ*4 "
+         "KR*2 LS JI*2 KK NI WR*2 NR JR*2 WN KR*2 JI KK JR WN NI*3 NR OW WR WS",
+    "g": "[cN [oR*2 CX (ZZ*2 IC MR (IV",
+}
+ORDER, BANK = [], {}
 
 OWN_TILES = {
-    F32: "ow:4288 IC0:192 IC1:192 MR0:384 MR1:384 inA:192 inB:192 inM:192 inC:192 yo:192 ob:256",
-    BF: "X:4288 VI:3072 VR:3072 V2:3072 XI:3072 NI:3072 XR:3072 NR:3072 CX:3072 DA:3072 DR:3072 D2:3072 DB:3072 "
-        "CZ:1536 on5:512 m01:768 m512:768 LO:2048 EX:1536 EQ:2304 QR:192 CR:192",
+    F32: "ow:4288 IC0:192 IC1:192 MR0:192 inA:192 inB:192 inM:192 inC:192 yo:192 ob:256 CR:192 zr:208 IV0:384 IV1:384 aT:192",
+    BF: "X:4288 VB:1536 XB:1536 NB:1536 VR:3168 XR:3072 NR:3072 CX:1536 V2:1536 DA:1632 DR:1632 DS:1632 D2:1632 DB:1632 "
+        "on5:512 m01:384 m512:384 EX:1536",
+    F16: "VA:1632 VN:1632 XA:816 NA:816 DI:1632 DJ:1632 DK:1632",
     I32: "nbw:4096 od:256 mi32:192 thi:8",
     U16: "oR0:192 oI0:192",
 }
+BOXES = {"EQ": ([12, 192], BF), "FM": ([2, 256], BF), "VV": ([2, 48], BF)}
 POOLS = {
-    F32: "p15:1 kc:1 e0:1 e192:1 eB:1 aC:24 IDf:128 FS:1024/96 FK:768/96 FB:256/96 rS:64/96 rK:48/96 SW:24 l1:24 Mg:192 zr:192 "
-         "xa:192 ya:192 wc:1 lim:1/96",
-    BF: "BLK:128 BK8:128 ID:128 I13:128 IDk:128 IDn:128 G64:8 G32:8 Gm:8 W1:144 W8:144 mB:256/96 mD:256/96 "
-        "krow:256/1 TR:256/3 thd:3 e3:3/1 kap:128/1 kan:128/1 cI:128/1 cR:128/1 zrow:128/1 "
-        "VV:96/96 SS:48/96 PP:48/96 ZZ:1280/96 ZX:1280/96 OH:256/96 b0:192 bf:192 cnt:384 Cb:96 QG:192 QK:192 FM:512/96 CN:512/96 "
-        "wf:192 wb:1 xg:192 CTI:128/96 CTR:128/96 CTB:128/96",
-    F16: "IDh:128 M16:192 n16:192 S0:192 S1:192 S2:192",
-    I32: "pI:1 pJ:1 wi:1/96 wj:1/96 td:2 mw:192 mv:192 mu:192 a32:96",
-    U16: "oI1:192 oR1:192 sL:12 nL:192 Lb:12 LS:24 aU:96",
+    F32: "p15:1 p16:1 kc:1 cB:1 cS:1 aC:24 IDf:128 FS:1024/102 FK:512/102 FR:256/102 FB:256/102 rS:64/102 rK:32/102 SW:24 l1:24 "
+         "xa:192 ya:192 WR:192 wc:1 lim:1/102",
+    BF: "BLK:128 BK8:128 BKm:128 ID:128 IDn:128 IDh:128 ID8:128 IDw:128 G64:8 G32:8 Gm:16 W1:144 MK:192 pb:256 pi:192 "
+        "mB:256/102 mD:256/102 mE:256/102 krow:256/1 kneg:256/1 TR:256/3 thd:3 cI:128/1 cR:128/1 cW:128/1 cE:128/1 cq:128/1 cN:128/1 BKn:128 ID4:128 P4:96/102 half:192/1 h0:192/1 h1:192/1 BKh:128 "
+        "lev:256 levA:102/1 SS:48/102 PP:48/102 ZZ:1024/102 ZX:768/102 OH:256/102 OR:256/102 b0:192 bf:192 cnt:192 Cb:192 QK:192 P0:96/102 "
+        "wf:192 wb:1 xg:192 CS:96",
+    F16: "IDg:128 pc:192 R16:192 M16:192 n16:192 S0:192 S1:192 S2:192 CA:204 CB:204 CTI:128/96 CTB:128/96 CT0:128/96 CN:272/102",
+    I32: "pI:1 pJ:1 wi:1/102 wj:1/102 td:2 mw:192 mv:192 mu:192 MR1:192",
+    U16: "oI1:192 oR1:192 sL:12 nL:192 Lb:12 LS:24 LI:12",
 }
 SCRATCH, SHAPE, PLACE = {}, {}, {}
+for _n, (_w, _d) in BOXES.items():
+    SCRATCH[_n] = ("sbuf", [128] + _w, _d)
 for _d, _names in OWN_TILES.items():
     for _n in _names.split():
         _n, _w = _n.split(":")
@@ -50,121 +64,189 @@ for _d, _names in POOLS.items():
 PSUM = ["b%d_" % _i for _i in range(8)]
 for _n in PSUM:
     SCRATCH[_n] = ("psum", [128, 512], F32)
-    SHAPE[_n], PLACE[_n] = (128, 512), (_n, 0)
 SEMAPHORES = ["qv", "qa", "qp", "qg"] + ["d%d" % i for i in range(8)] + ["rM", "rN", "rA", "rB", "rR", "rC"] + ["l%d" % i for i in range(5)]
 
 
-def arrange(calls, other, span):
+def arrange(calls, other, span, use, marks):
     n = len(calls)
     qs = [c[0] for c in calls]
+    name = [c[3][0].split("@")[0] for c in calls]
     users = [[] for _ in calls]
     for i, c in enumerate(calls):
         for d in c[5]:
             users[d].append(i)
-    gap = [[(d, calls[d][2] - calls[d][1], qs[d] != "x" and not qs[d] == qs[i] == "p") for d in c[5]] for i, c in enumerate(calls)]
+    held = {}
+    for i, u in use.items():
+        held.setdefault(u, []).append(i)
+    opens = {lst[0]: u for u, lst in held.items()}
+    readers = {u: [d for d in lst if qs[d] != "p"] for u, lst in held.items()}
+    short, long = 0.7 * WAKE, 1.3 * WAKE
+    gap = [[(d, calls[d][2] - calls[d][1] + short * w, calls[d][2] - calls[d][1] + long * w)
+            for d in c[5] for w in [qs[d] != "x" and not qs[d] == qs[i] == "p"]] for i, c in enumerate(calls)]
+    busy = [{q: (x - span.get(i, 0.0), x + span.get(i, 0.0)) for q in qs[i] for x in [c[1] if q == qs[i][0] else other.get(i, c[1])]} for i, c in enumerate(calls)]
+    blank = ([0.0] * (n + 1), [0.0] * (n + 1), [n] * n, [n] * n, {}, {},
+             [(dict.fromkeys("vapgsx", n), [(0.0, b, "") for b in range(len(PSUM))], {u: len(lst) for u, lst in held.items()})])
 
-    def walk(way):
-        left, ready, free, out = [len(c[5]) for c in calls], [0.0] * n, {q: 0.0 for q in "vapgsx"}, []
-        can = {q: [i for i in range(n) if q in qs[i] and not left[i]] for q in free}
-        while len(out) < n:
-            t, q = min((max(free[q], min(ready[i] for i in lst)), q) for q, lst in can.items() if lst)
-            rank = {j: way[j] - (0.0 if qs[j][0] == q else SECOND) if j else 1e9 for j in can[q]}
-            time = {j: other[j] if j in other and qs[j][0] != q else calls[j][1] for j in can[q]}
-            i = max((j for j in rank if ready[j] <= t + SLACK), key=rank.get)
-            u = max((j for j in rank if ready[j] <= t + time[i]), key=rank.get)
-            if rank[u] > rank[i] + AHEAD:
-                fit = [j for j in rank if max(ready[j], t) + time[j] <= ready[u] + SLACK]
-                if fit:
-                    i = max(fit, key=rank.get)
-                elif ready[u] - t < t + time[i] - ready[u]:
-                    i = u
-            for e in qs[i]:
-                can[e].remove(i)
-            t = max(t, ready[i])
-            busy, late = (other[i], other[i]) if i in other and qs[i][0] != q else calls[i][1:3]
-            free[q] = t + busy
-            out.append((i, q, busy))
-            for u in users[i]:
-                ready[u] = max(ready[u], t + late + (0.0 if q == "x" or q == qs[u] == "p" else WAKE))
-                left[u] -= 1
-                if not left[u]:
-                    for e in qs[u]:
-                        can[e].append(u)
-        return out
+    def length(seq, eng, lo=0, known=blank):
+        ends, endl, whys, whyl, at, after = [x.copy() for x in known[:6]]
+        stops = known[6][:lo // 32 + 1]
+        last, banks, rest = [x.copy() for x in stops[-1]]
+        for x in range(lo // 32 * 32, n):
+            if x % 32 == 0 and x > lo:
+                stops.append((last.copy(), banks.copy(), rest.copy()))
+            i = seq[x]
+            q = eng[i]
+            ws = wl = last[q]
+            s, l = ends[ws], endl[wl]
+            for d, a, b in gap[i]:
+                if ends[d] + a > s:
+                    s, ws = ends[d] + a, d
+                if endl[d] + b > l:
+                    l, wl = endl[d] + b, d
+            if i in opens:
+                if not banks:
+                    return 1e9, None, None
+                banks.sort()
+                _, at[opens[i]], was = banks.pop(0)
+                after[i] = readers.get(was, ())
+                for d in after[i]:
+                    if ends[d] + short > s:
+                        s, ws = ends[d] + short, d
+                    if endl[d] + long > l:
+                        l, wl = endl[d] + long, d
+            a, b = busy[i][q]
+            ends[i], endl[i], whys[i], whyl[i], last[q] = s + a, l + b, ws, wl, i
+            if i in use:
+                rest[use[i]] -= 1
+                if not rest[use[i]]:
+                    banks.append((ends[i], at[use[i]], use[i]))
+        total, steps = 0.0, []
+        for end, why in ((ends, whys), (endl, whyl)):
+            e, i = max((end[i] + calls[i][2] - calls[i][1], i) for i in range(n - 2, n))
+            total += e
+            while why[i] < n:
+                steps.append((i, why[i]))
+                i = why[i]
+        return total, steps, (ends, endl, whys, whyl, at, after, stops)
 
-    def length(out):
-        total = 0.0
-        for sign, wake in ((-1, 0.7 * WAKE), (1, 1.3 * WAKE)):
-            end, free = [0.0] * n, {q: 0.0 for q in "vapgsx"}
-            for i, q, busy in out:
-                t = free[q]
-                for d, late, wait in gap[i]:
-                    t = max(t, end[d] + late + (wake if wait else 0.0))
-                end[i] = free[q] = t + busy + sign * span.get(i, 0.0)
-            total += max(e + c[2] - c[1] for e, c in zip(end, calls))
-        return total
-    way = [0.0] * n
-    for i in range(n - 1, -1, -1):
-        way[i] = calls[i][2] + max([way[u] + WAKE for u in users[i]] + [0.0]) - 1e-6 * i
-    out = walk(way)
-    best = length(out)
-    now, o = list(way), out
-    for _ in range(30):
-        tail, nxt = [0.0] * n, {}
-        for i, q, busy in reversed(o):
-            w = max([tail[u] + (0.0 if q == "x" or q == qs[u] == "p" else WAKE) for u in users[i]] + [0.0]) + calls[i][2] - calls[i][1]
-            tail[i] = max(w, tail[nxt[q]] if q in nxt and q != "x" else 0.0) + busy
-            nxt[q] = i
-        now = [0.9 * now[i] + 0.1 * (calls[i][2] + max([tail[u] + WAKE for u in users[i]] + [0.0])) for i in range(n)]
-        o = walk(now)
-        e = length(o)
-        if e < best:
-            way, out, best = now, o, e
-    alike, twin, names = {}, {}, {}
-    for i, c in enumerate(calls):
-        alike.setdefault(c[0] + c[3][0], []).append(i)
-        names.setdefault((c[0], c[3][0].rstrip("01"), c[3][1]), []).append(i)
-    for lst in names.values():
-        if len(lst) % 2 == 0:
-            for a, b in zip(lst[:len(lst) // 2], lst[len(lst) // 2:]):
-                twin[a], twin[b] = b, a
-    rng = np.random.RandomState(1)
-    top = (best, out)
-    for _ in range(TRIES):
-        new = list(way)
-        for _ in range(1 + int(rng.rand() < 0.4)):
-            j = 2 + int(rng.randint(n - 2))
-            step, x = float(rng.normal()) * (calls[j][3][0] != "oR0"), rng.rand()
-            for i in alike[qs[j] + calls[j][3][0]] if x < 0.3 else [j, twin[j]] if j in twin and x < 0.7 else [j]:
-                new[i] += step
-        o = walk(new)
-        e = length(o)
-        if e <= best + 0.02 * rng.rand():
-            way, best = new, e
-            top = min(top, (e, o))
-    return [(i, q) for i, q, _ in top[1]], top[0] / 2
+    eng, lists, taken = [q[0] for q in qs], {q: [i for i in range(marks[0]) if qs[i][0] == q] for q in "vapgsx"}, set(range(marks[0]))
+    for lo, mid, hi in ((marks[0], marks[0], marks[1]), (marks[1], marks[2], marks[3])):
+        for q, text in ROUND.items():
+            for word in text.split():
+                word, _, k = word.partition("*")
+                a, b = (lo, mid) if word[0] == "[" else (mid, hi if word[0] != "(" or lo == mid else mid)
+                fit = [i for i in range(a, b) if i not in taken and q in qs[i] and word.lstrip("[(") in (name[i], name[i][:-1])]
+                for i in sorted(fit, key=lambda i: len(qs[i]))[:int(k or 1)]:
+                    taken.add(i)
+                    lists[q].append(i)
+                    eng[i] = q
+    for i in range(n):
+        if i not in taken:
+            lists[eng[i]].append(i)
+    seq, end, free, left, count = [], {}, dict.fromkeys(lists, 0.0), {u: len(lst) for u, lst in held.items()}, len(PSUM)
+    while len(seq) < n:
+        t, i = min((max([free[q]] + [end[d] + WAKE for d in calls[lst[0]][5]]), lst[0]) for q, lst in lists.items()
+                   if lst and all(d in end for d in calls[lst[0]][5]) and (count or lst[0] not in opens))
+        lists[eng[i]].pop(0)
+        free[eng[i]], end[i] = t + calls[i][1], t + calls[i][2]
+        seq.append(i)
+        if i in use:
+            left[use[i]] -= 1
+            count += (not left[use[i]]) - (i in opens)
+    best, steps, known = length(seq, eng)
+    top = (best, seq, eng, known)
+    both = [i for i in range(marks[0], n) if len(qs[i]) > 1]
+    pos = {i: x for x, i in enumerate(seq)}
+    rng = np.random.RandomState(5)
+    for it in range(TRIES):
+        new, turn, r = seq, None, rng.rand()
+        if r < 0.75:
+            x = int(rng.randint(len(steps)))
+            i, j = steps[x]
+            early = rng.rand() < 0.5
+            while rng.rand() < FAR:
+                x += 1 if early else -1
+                if not 0 <= x < len(steps) or eng[steps[x][early]] != eng[i if early else j] or steps[x][not early] != (j if early else i):
+                    break
+                i, j = (i, steps[x][1]) if early else (steps[x][0], j)
+            if j < marks[0]:
+                continue
+            if len(qs[j]) > 1 and (j in calls[i][5] or rng.rand() < 0.3):
+                turn = j
+            elif len(qs[i]) > 1 and rng.rand() < 0.3:
+                turn = i
+            else:
+                lo, hi = pos[j], pos[i] if early or rng.rand() < 0.5 else min(n - 1, pos[i] + int(rng.exponential(10)))
+                piece, moved = seq[lo:hi + 1], {i if early else j}
+                for k in piece[::-1] if early else piece:
+                    if k in moved:
+                        moved.update(calls[k][5] if early else users[k])
+                if i in moved and j in moved:
+                    continue
+                new = seq[:lo] + [k for k in piece if (k in moved) == early] + [k for k in piece if (k in moved) != early] + seq[hi + 1:]
+        elif r < 0.82:
+            turn = both[int(rng.randint(len(both)))]
+        else:
+            i = int(rng.randint(marks[0], n))
+            lo, hi = max([pos[d] for d in calls[i][5]] + [1]) + 1, min([pos[d] for d in users[i]] + [n]) - 1
+            new = seq[:pos[i]] + seq[pos[i] + 1:]
+            x = int(min(hi, max(lo, pos[i] + rng.normal() * (100 if rng.rand() < 0.3 else 20))))
+            new.insert(x, i)
+            lo = min(x, pos[i])
+        on = eng
+        if turn is not None:
+            on, lo = eng[:turn] + [qs[turn].replace(eng[turn], "")] + eng[turn + 1:], pos[turn]
+        e, s, k = length(new, on, lo, known)
+        if e <= best + (0.002 + WARM * (1 - it / TRIES)) * rng.exponential():
+            seq, eng, best, steps, known = new, on, e, s, k
+            if e < top[0]:
+                top = (e, seq, eng, known)
+            if it % 16 == 0:
+                new = [seq[x] for x in sorted(range(n), key=lambda x: (k[0][seq[x]] - busy[seq[x]][eng[seq[x]]][0], x))]
+                e, s, k = length(new, eng)
+                if e <= best:
+                    seq, best, steps, known = new, e, s, k
+            pos = {i: x for x, i in enumerate(seq)}
+    best, seq, eng, known = top
+    return [(i, eng[i], known[5].get(i, ())) for i in seq], known[4], best / 2
 
 
 def rank_program(g, core, T, topo):
     rank = T.rank_of(core)
     if rank is None:
         return
+    if not ORDER:
+        program(g, core, rank, T, topo)
+    program(g, core, rank, T, topo)
+
+
+def program(g, core, rank, T, topo):
     n_ranks = len(T.cores)
     S = T.sem
     queue = {"v": g.vector, "a": g.scalar, "p": g.tensor, "g": g, "s": g.sync}
-    B0, B1, B2, B3, B4, B5, B6, B7 = PSUM
+    uses = []
+
+    def bank_for(what):
+        uses.append(what)
+        return "%s@%d" % (what, len(uses))
 
     def R(name, lo=0, hi=None, step=1, p=None):
-        shape = SHAPE[name]
+        shape = SHAPE.get(name, (128, 512))
         hi = shape[1] if hi is None else hi
         p = shape[0] if p is None else p
-        buf, at = PLACE[name]
+        buf, at = PLACE.get(name) or (PSUM[BANK.get(name, 0)], 0)
         ap = T[buf][0:p, at + lo:at + hi:step] if step > 1 else T[buf][0:p, at + lo:at + hi]
-        return (ap, [(name, lo, hi)], -(-(hi - lo) // step), SIZE[SCRATCH[buf][2]], name in PSUM, False)
+        return (ap, [(name, lo, hi)], -(-(hi - lo) // step), SIZE[SCRATCH[buf][2]], "@" in name, False)
 
-    def back(name, n):
+    def back(name, lo, hi, step=1):
         buf, at = PLACE[name]
-        return (T[buf][0:SHAPE[name][0], at + n - 1:at - 1:-1],) + R(name, 0, n)[1:]
+        return (T[buf][0:SHAPE[name][0], at + hi - 1:at + lo - 1:-step],) + R(name, lo, hi, step)[1:]
+
+    def BX(name, *at, p=128):
+        shape, d = BOXES[name]
+        cols = np.sort(np.arange(shape[0] * shape[1]).reshape(shape)[at].reshape(-1))
+        cut = [0] + [int(i) + 1 for i in np.nonzero(np.diff(cols) > 16)[0]] + [len(cols)]
+        return (T[name][(slice(0, p),) + at], [(name, int(cols[a]), int(cols[b - 1]) + 1) for a, b in zip(cut, cut[1:])], len(cols), SIZE[d], False, False)
 
     def IND(win, n, off, c0=0, c1=12):
         buf, at = PLACE[off]
@@ -183,15 +265,19 @@ def rank_program(g, core, T, topo):
     seen = {}
     group = {}
     other = {}
+    bundle = []
+    use = {}
     span = {}
 
     def put(q, busy, late, outs, ins, issue, loose=False, after=()):
+        if bundle:
+            return bundle[0].append((q, busy, outs, ins, issue))
         rd, wr = spans(ins), spans(outs)
         deps = set(after)
         for lst, w in ((rd, False), (wr, True)):
             for name, lo, hi in lst:
                 for e in seen.get(name, ()):
-                    if name in PSUM and (q != e[1] or q in ("p", "av")):
+                    if "@" in name and (q != e[1] or q == "p" or len(q) > 1):
                         hit = not (loose and e[5])
                     else:
                         hit = (w or e[0]) and e[3] < hi and lo < e[4] and not (w and loose and e[5])
@@ -201,10 +287,22 @@ def rank_program(g, core, T, topo):
             for name, lo, hi in lst:
                 old = seen.setdefault(name, [])
                 if w and not loose:
-                    old[:] = [e for e in old if not (lo <= e[3] and e[4] <= hi) and name not in PSUM]
+                    old[:] = [e for e in old if not (lo <= e[3] and e[4] <= hi) and "@" not in name]
                 old.append([w, q, len(calls), lo, hi, loose])
-        calls.append((q, busy, late, (wr + rd)[0], issue, deps))
+                if "@" in name:
+                    use[len(calls)] = name
+        calls.append((q, busy, late, (wr + rd)[0], issue, sorted(deps)))
         return len(calls) - 1
+
+    def together(f, items, n):
+        items = list(items)
+        for lo in range(0, len(items), n):
+            bundle.append([])
+            for x in items[lo:lo + n]:
+                f(x)
+            lst = bundle.pop()
+            c = sum(e[1] for e in lst)
+            put(lst[0][0], c, c, [o for e in lst for o in e[2]], [a for e in lst for a in e[3]], lambda lst=lst: [e[4]() for e in lst])
 
     def emit(q, call, outs, ins, each=1.0, second=None):
         o = outs[0]
@@ -236,11 +334,13 @@ def rank_program(g, core, T, topo):
     def ms(o, c):
         emit("v", lambda: g.vector.memset(o[0], c), [o], [], 0.5)
 
-    def scan(o, d0, d1, op0, op1):
-        emit("v", lambda: g.vector.tensor_tensor_scan(o[0], d0[0], d1[0], 0.0, op0, op1), [o], [d0, d1], 0.5)
+    def scan(o, d0, d1, op0, op1, first=0.0):
+        emit("v", lambda: g.vector.tensor_tensor_scan(o[0], d0[0], d1[0], first, op0, op1), [o], [d0, d1], 0.5)
 
     def act(o, a, func=AF.Copy, bias=0.0, scale=1.0, acc=None):
-        if acc is None:
+        if o[5]:
+            emit("a", lambda: g.scalar.activation(o[0], a[0], func), [o], [a])
+        elif acc is None:
             emit("a", lambda: g.scalar.activation(o[0], a[0], func, bias=ap(bias), scale=ap(scale)), [o], [a, bias, scale])
         else:
             emit("a", lambda: g.scalar.activation(o[0], a[0], func, bias=ap(bias), scale=ap(scale), accum_out=acc[0]), [o, acc], [a, bias, scale])
@@ -249,12 +349,14 @@ def rank_program(g, core, T, topo):
         emit("av", {"a": lambda: g.scalar.activation(o[0], a[0], AF.Copy), "v": lambda: g.vector.tensor_copy(o[0], a[0])}, [o], [a])
 
     def fill(o, c):
-        emit("vg", {"v": lambda: g.vector.memset(o[0], float(c)),
-                    "g": lambda: g.iota(o[0], [[0, o[2]]], c, 0, allow_small_or_imprecise_dtypes=True)}, [o], [], 0.5, 0.13 + 2 * o[2] * CYCLE)
+        t = 0.13 + 2 * o[2] * CYCLE
+        other[put("gv", t, t, [o], [], {"g": lambda: g.iota(o[0], [[0, o[2]]], c, 0, allow_small_or_imprecise_dtypes=True),
+                                        "v": lambda: g.vector.memset(o[0], float(c))})] = max(64, o[2] * o[3] / 4) * CYCLE
 
     def lin(o, a, mul, add=0.0):
         emit("va", {"v": lambda: g.vector.tensor_scalar(o[0], a[0], mul, add, OP.mult, OP.add),
-                    "a": lambda: g.scalar.activation(o[0], a[0], AF.Copy, bias=add, scale=mul)}, [o], [a], 0.5, max(64, o[2]) * CYCLE)
+                    "a": lambda: g.scalar.activation(o[0], a[0], AF.Copy, bias=add, scale=mul)}, [o], [a], 0.5,
+             None if a[5] else max(64, o[2]) * CYCLE)
 
     def mms(lst, start=False):
         bank = lst[0][0][1][0][0]
@@ -285,14 +387,15 @@ def rank_program(g, core, T, topo):
 
     dmas, sent = [], []
 
-    def dma(q, a, b, late):
+    def dma(q, late, *pairs):
         sem = "d%d" % len(dmas)
         dmas.append(sem)
 
         def issue():
-            queue[q].dma_start(a[0], b[0]).then_inc(S[sem], 16)
-            return (sem, 16)
-        put(q, 0.05, late, [a], [b], issue)
+            for a, b in pairs:
+                queue[q].dma_start(a[0], b[0]).then_inc(S[sem], 16)
+            return (sem, 16 * len(pairs))
+        put(q, 0.05 * len(pairs), late, [a for a, b in pairs], [b for a, b in pairs], issue)
         return sem
 
     def send(src, outs, late, half=None):
@@ -316,17 +419,16 @@ def rank_program(g, core, T, topo):
                 g.remote_dma_fused([RemoteDMATransfer(dst_ids=[DstId(rid=rid, pnc=pid)], dma_engine_mask=mask, remote_sem=S[rs],
                                                       src=T[src][:, lo:hi], dst=T[land][:, lo:hi]) for rid, pid, mask, land, rs in tr], local_sem=S[ls])
             return (ls, m * len(outs))
-        me = put("g", 0.3, late, [], [R(src, lo, hi)], issue)
+        busy = 0.4 if half is None else 0.9
+        me = put("g", busy, busy, [], [R(src, lo, hi)], issue)
         for d, land, rs in outs:
-            put("x", 0.0, 0.0, [R(land, lo, hi)], [], (rs, m), False, [me])
+            put("x", 0.0, late - busy, [R(land, lo, hi)], [], (rs, m), False, [me])
 
     def issue_all():
         count = {q: 0 for q in "vapg"}
         known = {q: {} for q in queue}
         snap, done = {}, {}
-        if not ORDER:
-            ORDER.extend(arrange(calls, other, span)[0])
-        for i, q in ORDER:
+        for i, q, after in ORDER:
             qs, _, _, lab, issue, deps = calls[i]
             if len(qs) > 1:
                 issue = issue[q]
@@ -334,7 +436,7 @@ def rank_program(g, core, T, topo):
                 done[i] = issue
                 continue
             want = {}
-            for d in deps:
+            for d in list(deps) + list(after):
                 if not q == calls[d][0] == "p":
                     sem, val = done[d]
                     want[sem] = max(want.get(sem, 0), val)
@@ -347,8 +449,9 @@ def rank_program(g, core, T, topo):
                     k[sem] = val
             r = issue()
             if not isinstance(r, tuple):
-                count[q] += 1
-                r.then_inc(S["q" + q], 1)
+                for ins in r if isinstance(r, list) else [r]:
+                    count[q] += 1
+                    ins.then_inc(S["q" + q], 1)
                 r = ("q" + q, count[q])
             done[i] = r
             snap[r] = dict(k)
@@ -357,317 +460,371 @@ def rank_program(g, core, T, topo):
     up1, up2 = (rank + 1) % n_ranks, (rank + 2) % n_ranks
     dn1, dn2 = (rank - 1) % n_ranks, (rank - 2) % n_ranks
 
-    dma("s", R("mi32"), hbm("m0"), 1.8)
-    dma("s", R("X", 0, 4096), hbm("x0"), 5.0)
-    dma("a", R("od"), hbm("own0"), 2.5)
+    dma("s", 1.8, (R("mi32"), hbm("m0")))
+    dma("s", 4.4, (R("X", 0, 4096), hbm("x0")))
     ms(R("thi"), 0)
-    dma("a", (T.thi[0:128:16, 0:1], [("thi", 0, 8)]), hbm("th"), 8.0)
-    for h, rs in enumerate(("rM", "rN")):
-        cp(R("oR0", 96 * h, 96 * h + 96), R("mi32", 96 * h, 96 * h + 96))
-        send("oR0", [(up1, "oI0", rs)], 3.0, h)
+    dma("a", 2.0, ((T.thi[0:128:16, 0:1], [("thi", 0, 8)]), hbm("th")))
     ms(R("on5"), 1.0)
     iota(R("pI"), [[0, 1]], 0, 1, False)
+    iota(R("lev"), [[-256, 16], [0, 16]], 1792)
     select(R("ID"), R("on5", 0, 128), [[-1, 128]], OP.is_equal, 0, 1)
     select(R("BLK"), R("on5", 0, 128), [[-16, 8], [0, 16]], OP.is_ge, 0, 1)
     select(R("BLK"), R("BLK"), [[16, 8], [0, 16]], OP.is_ge, 15, -1)
     ms(R("m01"), 1.0)
-    ms(R("m01", 0, 768, 16), 0.0)
-    lin(R("m512"), R("m01"), -512.0, 512.0)
-    lin(R("mB"), R("m01", 0, 256, 1, 96), -BIG, BIG)
-    lin(R("mD"), R("m01", 0, 256, 1, 96), BIG + 2.0, -BIG)
-    for lo in range(0, 4288, 512):
-        hi = min(lo + 512, 4288)
-        act(R("ow", lo, hi), R("on5", 0, hi - lo), AF.Copy, 0.0, 0.0)
-    iota(R("krow"), [[0, 16], [1, 16]], -15)
-    iota(R("kap"), [[0, 8], [-1, 16]], 15)
-    iota(R("kan"), [[0, 8], [1, 16]], -15)
-    iota(R("a32"), [[16, 96]], 0, 0, False)
-    cp(R("aU"), R("a32"))
-    for i in range(3):
-        select(R("EX", 512 * i, 512 * i + 512, 1, 96), R("on5", p=96), [[-1, 32], [0, 16]], OP.is_equal, -32 * i, 1)
-    for i in range(4):
-        fill(R("CZ", 384 * i, 384 * i + 384), 0)
+    together(lambda lo: ms(R("VA", lo, lo + 16), 2048.0), range(0, 1632, 272), 6)
+    ms(R("XA", 0, 816, 136), 0.0)
+    ms(R("NA", 7, 816, 136), 0.0)
+    ms(R("cq"), -0.25)
+    ms(R("m01", 0, 384, 16), 0.0)
     ts(R("pJ"), R("pI"), 15, OP.bitwise_and)
+    ms(R("W1"), 0.0)
+    lin(R("m512"), R("m01"), -512.0, 512.0)
     cp(R("p15"), R("pJ"))
-    ts(R("kc"), R("pJ"), -1.0, OP.mult, 15.0, OP.add)
-    for name, c in (("W1", 1.0), ("W8", 8192.0)):
-        fill(R(name), 0)
-        lin(R(name, 15, 143, 16), R("BLK", 0, 128, 16), c)
-    for name, c in (("G64", 64.0), ("G32", 32.0), ("Gm", -32.0)):
-        lin(R(name), R("BLK", 0, 128, 16), c)
-    ts(R("IDh"), R("ID"), 511.0 / 1024.0, OP.mult)
-    for name, c in (("I13", 2.0 ** -13), ("IDk", -KILL), ("IDn", -1.0), ("IDf", 1.0)):
-        lin(R(name), R("ID"), c)
-    lin(R("BK8"), R("BLK"), 8192.0)
-    for name, c in (("cI", 2 ** 17 + 32768), ("cR", 2 ** 16 + 32768), ("zrow", 0)):
-        fill(R(name), c)
-    for i in range(5):
-        fill(R("ZZ", 256 * i, 256 * i + 256), 0)
-    cp(R("ob"), R("od"))
-    dma("s", (T.ow[0:128:16, 0:4096], [("ow", 0, 4096)]), R("ob"), 5.0)
-    dma("s", R("nbw"), (T.nb[:], [("ob", 0, 1), ("oR0", 0, 1)]), 10.0)
-    for r in range(1, 16):
-        select(R("LO", 128 * r, 128 * r + 128), R("BLK"), [[16, 8], [0, 16]], OP.is_ge, r - 1, -1)
-    fill(R("X", 4096, 4288), 0)
-    fill(R("MR0", 192, 384), 0)
-    fill(R("MR1", 192, 384), 0)
-    cp(R("MR0", 0, 192), R("mi32"))
-    iota(R("aC", 0, 12), [[16, 12]], 2049)
-    iota(R("aC", 12, 24), [[16, 12]], -1855)
-    ts(R("aC"), R("aC"), R("p15"), OP.add, -0.5, OP.add)
-    for name, c in (("e0", 1.0), ("e192", 192.0), ("eB", -192.0 * 191.0)):
-        ts(R(name), R("p15"), 0.0, OP.is_equal, c, OP.mult)
+    ts(R("p16"), R("pJ"), 1.0, OP.add)
+    lin(R("mB"), R("m01", 0, 256, 1, KP), -BIG, BIG)
+    scan(R("pb"), R("m01", 0, 256), R("m01", 0, 256), OP.mult, OP.add)
+    lin(R("mD"), R("m01", 0, 256, 1, KP), BIG + 2.0, -BIG)
+    put("a", 1.5, 1.5, [R("IV0")], [R("on5")], lambda: g.scalar.activation(T.IV0[:, 0:192], T.on5[:, 0:192], AF.Silu, scale=256.0))
+    for lo in range(0, 3584, 512):
+        act(R("ow", lo, lo + 512), R("on5"), AF.Copy, 0.0, 0.0)
+    for h, rs in enumerate(("rM", "rN")):
+        cp(R("oR0", 96 * h, 96 * h + 96), R("mi32", 96 * h, 96 * h + 96))
+        send("oR0", [(up1, "oI0", rs)], 2.8 - 0.4 * h, h)
+    behind = [("X", 0, 1)]
+    dma("s", 2.0, (R("od"), (T.own0[:], behind)))
+    dma("s", 4.5, (R("nbw", 0, 2048), (T.nb[:, 0:2048], behind)))
+    lin(R("mE"), R("m01", 0, 256, 1, KP), BIG, -BIG)
+    lin(R("krow"), R("pb", p=1), 1.0, -15.0)
+    lin(R("kneg"), R("pb", p=1), -1.0, 15.0)
+    ms(R("cE"), -2.5)
+    ts(R("kc"), R("pJ"), -1024.0, OP.mult, 1024.0 * (8192 + 15), OP.add)
+    ts(R("cB"), R("p15"), 15.0, OP.is_lt, 256.0, OP.mult)
+    ts(R("IDg"), R("ID"), 511.0 / 1024.0, OP.mult)
+    lin(R("IDh"), R("ID"), 0.5)
+    ts(R("cS"), R("cB"), 8192.0, OP.mult, MID + 8192.0, OP.add)
+    for name, lo, c in (("G64", 0, 64.0), ("G32", 0, 32.0), ("Gm", 0, -32.0), ("Gm", 8, -32.0)):
+        lin(R(name, lo, lo + 8), R("BLK", 0, 128, 16), c)
+    lin(R("W1", 15, 143, 16), R("BLK", 0, 128, 16), 1.0)
+    iota(R("aC", 0, 12), [[16, 12]], 4096)
+    iota(R("aC", 12, 24), [[16, 12]], 192)
+    ts(R("pc"), R("pb", 0, 192), R("p15"), OP.is_equal, 1024.0, OP.mult)
+    ts(R("pi"), R("pb", 0, 192), R("p16"), OP.is_equal, -0.25, OP.mult)
+    lin(R("h0"), R("m01", 0, 192, 1, 1), 0.5)
+    lin(R("h1"), R("m01", 0, 192, 1, 1), -1.0, 1.0)
+    scan(R("MK"), R("pi"), R("pc"), OP.mult, OP.add)
+    scan(R("half"), R("h0"), R("h1"), OP.mult, OP.add)
     ts(R("td", 0, 1), R("thi", 0, 1), 6, OP.arith_shift_right)
     ts(R("td", 1, 2), R("thi", 0, 1), 63, OP.bitwise_and)
     ms(R("thd", 0, 1), 0.0)
     ts(R("thd", 1, 2), R("td", 0, 1), -2048.0, OP.mult)
     ts(R("thd", 2, 3), R("td", 1, 2), -32.0, OP.mult)
-    iota(R("e3"), [[-1, 3]], 1)
-    ts(R("e3"), R("e3"), 0.0, OP.max)
-    mms([(R(B5, 0, 128, 1, 3), R("thd"), R("BLK")), (R(B5, 0, 128, 1, 3), R("e3"), R("krow", 0, 128))], True)
-    for h in (0, 1):
-        act(R("TR", 128 * h, 128 * h + 128), R(B5, 0, 128, 1, 3))
+    for name, c in (("IDn", -1.0), ("IDf", 1.0), ("ID8", 8192.0), ("IDw", -2.0 ** 17)):
+        lin(R(name), R("ID"), c)
+    o = R(bank_for("BKh"), 0, 1)
+    mm(o, R("half", 0, 128), R("on5", 0, 1, 1, 1), True)
+    lin(R("BK8"), R("BLK"), 8192.0)
+    lin(R("BKm"), R("BLK"), -32.0)
+    ts(R("BKh"), R("BLK"), o, OP.mult)
+    rows = R(bank_for("TR"), 0, 128, 1, 3)
+    mms([(rows, R("thd"), R("BLK")), (rows, R("h1", 0, 3), R("krow", 0, 128))], True)
+    fill(R("ow", 3584), 0)
+    for i in range(3):
+        select(R("EX", 512 * i, 512 * i + 512, 1, 96), R("on5", p=96), [[-1, 32], [0, 16]], OP.is_equal, -32 * i, 1)
+        if not i:
+            select(R("ob"), R("od"), [[0, 256]], OP.is_ge, 0, 0)
+            dma("s", 6.0, ((T.ow[0:128:16, 0:4096], [("ow", 0, 4096)]), R("ob")), (R("nbw", 2048), (T.nb[:, 2048:4096], [])))
+    fill(R("DA", 1536), 0)
+    select(R("P0"), R("on5", 0, 96, 1, KP), [[-17, 6], [-1, 16]], OP.is_equal, -1, 1)
+    iota(R("levA"), [[0, 6], [-256, 17]], 2048)
+    together(lambda lo: iota(R("VN", lo, lo + 16), [[0, 16]], 2048), range(0, 1632, 272), 6)
+    for v in ("VR", "DR", "D2", "DB", "DS"):
+        fill(R(v, SHAPE[v][1] - 96), 0)
+    iota(R("aT"), [[1, 192]], 64)
+    for name, c in (("cI", 2 ** 18 + 32768), ("cR", 2 ** 16 + 32768), ("cW", 2 ** 17 + 2048)):
+        fill(R(name), c)
+    for o in (R("zr", 192), R("X", 4096)):
+        fill(o, 0)
 
-    def part(name, q, step=1):
-        return R(name, 768 * q, 768 * q + 768, step)
+    def by_block(v, off):
+        for b in range(6):
+            tt(R(v, 272 * b + 16, 272 * b + 272), IND("X", 4096, off, 16 * b, 16 * b + 16), R("lev"), OP.add)
 
-    def gather(v, off, n):
-        for lo in range(0, 192, n):
-            either(R(v, 16 * lo, 16 * (lo + n)), IND("X", 4096, off, lo, lo + n))
+    def gather(v, off, lo, hi, n, at=96):
+        for a in range(lo, hi, n):
+            either(R(v, 16 * (a - at), 16 * (a - at + n)), IND("X", 4096, off, a, a + n))
+
+    def extremes(v, mx, mn, n):
+        for lo in range(0, 384 * n, 384):
+            scan(R(mx, lo, lo + 384), R("m01"), R(v, lo, lo + 384), OP.mult, OP.max)
+            scan(R(mn, lo, lo + 384), R("m512"), R(v, lo, lo + 384), OP.add, OP.min)
+
+    def on_levels(lo):
+        hi = lo + 256
+        scan(back("XA", lo // 2, hi // 2), back("VA", lo, hi, 2), back("VA", lo, hi - 1, 2), OP.max, OP.max, -4096.0)
+        scan(R("NA", lo // 2, hi // 2), R("VA", lo, hi, 2), R("VA", lo + 1, hi, 2), OP.min, OP.min, 4096.0)
 
     def row(bank, l):
-        mm(R(bank, 0, 192), R(l), R("on5", 0, 192, 1, 1), True)
+        mm(R(bank, 0, 192), R(l, 0, 128), R("on5", 0, 192, 1, 1), True)
 
     def opened(bank, n, rows):
-        mm(R(bank, 0, 256, 1, 96), R("on5", 0, 96, 1, n), R(rows), True)
+        mm(R(bank, 0, 256, 1, KP), R("on5", 0, KP, 1, n), R(rows), True)
 
-    def group_sum(bank, src, w, h, same=False):
-        for k0 in (0, 8):
-            mms([(R(bank, 128 * h + k, 128 * h + 128, 16, 96), R(src, 1536 * h + (0 if same else k), 1536 * h + 1536, 16), R(w))
-                 for k in range(k0, k0 + 8)])
+    def group_sum(bank, at, src, w, n=4):
+        ks = [k // 2 + 8 * (k % 2) for k in range(16)]
+        for k0 in range(0, 16, n):
+            mms([(R(bank, at + k, at + 16 * w[2], 16, KP), src(k), w) for k in ks[k0:k0 + n]])
+
+    def rows_of(d):
+        return lambda k: R(d, 204 * (k % 8) + k // 8, 204 * (k % 8) + 204, 2)
+
+    def plain(d, at=0):
+        return lambda k: R(d, at + k, at + 1632, 16)
 
     def Z(i):
         return R("ZZ", 256 * i, 256 * i + 256, 16)
 
     def turn_over(bank, src, at, start):
-        lst = [(R(bank, 96 * h, 96 * h + 96), R(src, at + 128 * h, at + 128 * h + 128), R("ID", 0, 96, 1, 96)) for h in (0, 1)]
-        if start:
-            for m in lst:
-                mms([m], True)
-        else:
-            mms(lst)
+        mms([(R(bank, 0, 96), R(src, at, at + 128), R("P0")), (R(bank, 96, 192), R(src, at + 128, at + 256, 1, 96), R("ID", 0, 96, 1, 96))], start)
 
-    def from_keys(bank, i, start=False):
-        scan(R("ZX", 256 * i, 256 * i + 256), R("m01", 0, 256, 1, 96), R("ZZ", 256 * i, 256 * i + 256), OP.mult, OP.add)
-        turn_over(bank, "ZX", 256 * i, start)
+    def from_keys(bank, i):
+        scan(R("ZX", 256 * i, 256 * i + 256), R("m01", 0, 256, 1, KP), R("ZZ", 256 * i, 256 * i + 256), OP.mult, OP.add)
+        turn_over(bank, "ZX", 256 * i, False)
 
-    def to_list(bank, src, w, n=192, start=True):
-        mms([(R(bank, 0, n // 16), R(w, 15 - j, 143 - j), R(src, j, n, 16)) for j in range(16)], start)
+    def picked(out, src):
+        scan(R(out, 0, 192), R("MK"), R(src, 0, 192), OP.add, OP.min)
+        return R(out, 15, 192, 16)
 
-    turn = [0]
+    def turned_centres(mx, mn, ct):
+        o = R(bank_for(ct), 0, 128, 1, 96)
+        mms([(o, R(m, 15, 1536, 16), R("IDg")) for m in (mx, mn)], True)
+        lin(R(ct), o, 1.0, 1024.0)
 
-    def centres(mx, mn, q, n, out):
-        turn[0] += 1
-        o = R(PSUM[6 + turn[0] % 2], 0, 48 * n)
-        mms([(o, R("IDh"), R(m, 768 * q + 15, 768 * (q + n), 16)) for m in (mx, mn)], True)
-        ts(out, o, R1, OP.add, R1, OP.subtract)
+    def apart(v, ct, d):
+        for lo in (0, 512, 1024):
+            o = R(bank_for(d))
+            two = [(o, R("IDn"), R(v, lo, lo + 512)), (o, R(ct), R("EX", lo, lo + 512, 1, 96))]
+            mm(*two[d == "D2"], True)
+            mm(*two[d != "D2"])
+            act(R(d, lo, lo + 512), o, AF.Abs, -1024.0)
 
-    def spread(q, free=False):
-        o, z = part("CX", q), part("CZ", q % 2)
-        if not free:
-            return scan(o, R("m01"), z, OP.mult, OP.add)
-        w = IND("CZ", 1536, "aU", 48 * (q % 2), 48 * (q % 2) + 48)
-        emit("va", {"v": lambda: g.vector.tensor_tensor_scan(o[0], R("m01")[0], z[0], 0.0, OP.mult, OP.add),
-                    "a": lambda: g.scalar.activation(o[0], w[0], AF.Copy)}, [o], [R("m01"), z, (0, w[1], 0)], 0.5, (70 + 1.5 * 768) * CYCLE)
+    def larger(v, c, d):
+        together(lambda k: scan(R(d, 204 * k, 204 * k + 204), R(c), R(v, k, 1632, 8), OP.min, OP.max), range(8), 2)
 
-    def apart(v, ct, d, h, banks):
-        for i in range(3):
-            cols = (1536 * h + 512 * i, 1536 * h + 512 * i + 512)
-            mms([(R(banks[i]), R("IDn"), R(v, *cols)), (R(banks[i]), R(ct), R("EX", 512 * i, 512 * i + 512, 1, 96))], True)
-            act(R(d, *cols), R(banks[i]), AF.Abs)
+    def least(f, at, bank, lo=0, n=256):
+        scan(R(f, at, at + n), R("mB", 0, n), R(bank, lo, lo + n, 1, KP), OP.add, OP.min)
 
-    def larger(v, cx, d, q):
-        tt(part(v, q, 16), part(v, q, 16), part(cx, q, 16), OP.max)
-        scan(part(d, q), part(cx, q), part(v, q), OP.min, OP.max)
+    def largest(f, at, bank, lo=0, n=256):
+        scan(R(f, at, at + n), R("mD", 0, n), R(bank, lo, lo + n, 1, KP), OP.add, OP.max)
 
-    def first_half(bank, v, mx, mn, ct, d):
-        group_sum(bank, v, "Gm", 1)
-        for q in range(4):
-            scan(part(mx, q), R("m01"), part(v, q), OP.mult, OP.max)
-            scan(part(mn, q), R("m512"), part(v, q), OP.add, OP.min)
-        turn[0] += 1
-        o = R(PSUM[6 + turn[0] % 2], 0, 128, 1, 96)
-        mms([(o, R(m, 15, 1536, 16), R("IDh")) for m in (mx, mn)], True)
-        ts(R(ct), o, R1, OP.add, R1, OP.subtract)
-        apart(v, ct, d, 0, (B3, B4, B2))
-
-    def least(f, at, bank):
-        scan(R(f, at, at + 256), R("mB"), R(bank, 0, 256, 1, 96), OP.add, OP.min)
-
-    def largest(f, at, bank):
-        scan(R(f, at, at + 256), R("mD"), R(bank, 0, 256, 1, 96), OP.add, OP.max)
-
-    def rest(o, f, lo, hi, turned=False):
-        ends, r = R(f, lo + 15, hi, 16), R("rS" if f == "FS" else "rK", lo // 16, hi // 16)
-        ts(r, ends, R32, OP.add, R32, OP.subtract)
-        if turned:
-            tt(o, r, ends, OP.subtract)
-        else:
-            tt(o, ends, r, OP.subtract)
+    def rest(o, f, r):
+        ends = R(f, 15, None, 16)
+        ts(R(r), ends, R32, OP.add, R32, OP.subtract)
+        tt(o, ends, R(r), OP.subtract)
 
     def play(t):
         oI, oR = "oI%d" % t, "oR%d" % t
-        IC, MR = "IC%d" % t, "MR%d" % t
+        IC, MR, IV = "IC%d" % t, "MR%d" % t, "IV%d" % t
         last = t == 1
-        KI, KR, KE, KB = B0, B1, B2, B3
-        gather("VI", oI, 24)
-        gather("VR", oR, 24)
+        KI, KR, F0, F1 = [bank_for(b) for b in ("KI", "KR", "Fa", "Fb")]
+        by_block("VA", oI)
+        gather("VB", oI, 96, 192, 24)
+        for lo, hi, n in ((0, 96, 24), (96, 192, 48)):
+            gather("VR", oR, lo, hi, n, 0)
         opened(KI, 1, "krow")
-        opened(KR, 1, "krow")
         ts(R("M16"), R(oI), -2048.0, OP.add)
-        first_half(KI, "VI", "XI", "NI", "CTI", "DA")
-        for q in (2, 3):
-            centres("XI", "NI", q, 1, part("CZ", q % 2, 16))
-            spread(q)
-            larger("VI", "CX", "DA", q)
-        group_sum(KI, "DA", "G32", 0)
-        group_sum(KI, "DA", "G64", 1)
-        first_half(KR, "VR", "XR", "NR", "CTR", "DR")
-        centres("XR", "NR", 2, 2, R("CR", 96, 192))
-        for k in range(16):
-            select(R("NR", 1536 + k, 3072, 16), R("CR", 96, 192), [[0, 96]], OP.is_ge, 0, 0, True)
-        for q in (2, 3):
-            larger("VR", "NR", "DR", q)
-        group_sum(KR, "DR", "G32", 0)
-        group_sum(KR, "DR", "G64", 1)
-        centres("XR", "NR", 0, 2, R("CR", 0, 96))
-        opened(KE, 3, "TR")
-        opened(KB, 3, "TR")
-        group_sum(KE, "CX", "Gm", 1)
-        least("FK", 0, KI)
-        scan(back("FB", 256), R("mB"), back("FK", 256), OP.add, OP.min)
-        tt(R("OH"), R(KI, 0, 256, 1, 96), R("FB"), OP.is_equal)
-        turn_over(B5, "OH", 0, True)
-        tt(R("S2"), R(B5, 0, 192), R("M16"), OP.mult)
-        to_list(B5, "S2", "W1")
-        ts(R("sL"), R(B5, 0, 12), 2048.0, OP.add)
-        ts(R("SW", 0, 12), R(B5, 0, 12), 2048.0 - MID, OP.add)
-        rest(R("VV", 80, 96), "FK", 0, 256)
+        group_sum(KI, 0, plain("VA"), R("Gm", 0, 8))
+        together(on_levels, range(16, 1632, 272), 1)
+        extremes("VB", "XB", "NB", 4)
+        b = bank_for("CA")
+        mms([(R(b, 0, 204), R("cq"), R("on5", 0, 204, 1, 1))]
+            + [(R(b, i, 204, 2), R("IDh"), m) for m in (R("XA", 0, 816, 8), R("NA", 7, 816, 8)) for i in (0, 1)], True)
+        ts(R("CA"), R(b, 0, 204), R1, OP.add, R1, OP.subtract)
+        turned_centres("XB", "NB", "CTI")
+        larger("VA", "CA", "DI")
+        apart("VB", "CTI", "DA")
+        group_sum(KI, 0, rows_of("DI"), R("G64"))
+        group_sum(KI, 128, plain("DA"), R("G32"), 8)
+        extremes("VR", "XR", "NR", 8)
+        o = R(bank_for("CR"), 0, 192)
+        mms([(o, R("IDg"), R(m, 15, 3072, 16)) for m in ("XR", "NR")], True)
+        lin(R("CR"), o, 1.0, R1)
+        turned_centres("XR", "NR", "CT0")
+        opened(KR, 1, "kneg")
+        lin(R("CS"), R("CR", 96, 192), 1.0, -R1)
+        together(lambda k: select(R("CX", k, 1536, 16), R("CS"), [[0, 96]], OP.is_ge, 0, 0), range(16), 16)
+        group_sum(KR, 128, plain("VR", 1536), R("Gm", 0, 8))
+        opened(F0, 3, "TR")
+        opened(F1, 3, "TR")
+        mm(R(F0, 0, 128, 1, KP), R("CA", 0, 204, 2), R("BKm"))
+        least("FK", 256, KI)
+        scan(back("FB", 0, 256), R("mB"), back("FK", 256, 512), OP.add, OP.min)
+        tt(R("OH"), R(KI, 0, 256, 1, KP), R("FB"), OP.is_equal)
+        b = bank_for("OH")
+        turn_over(b, "OH", 0, True)
+        tt(R("S2"), R(b, 0, 192), R("M16"), OP.mult)
+        o = R(bank_for("sL"), 0, 12)
+        mms([(o, R("W1", 15 - j, 143 - j), R("S2", j, 192, 16)) for j in range(16)], True)
+        ts(R("sL"), o, 2048.0, OP.add)
+        ts(R("SW", 0, 12), o, 2048.0 - MID, OP.add)
         either(R("b0"), IND("ow", 4096, "sL"))
         cp(R("nL"), IND("nbw", 4096, "sL"))
-        largest("FK", 256, KI)
-        largest("FK", 512, KR)
-        rest(R("VV", 32, 48), "FK", 256, 512)
-        rest(Z(4), "FK", 512, 768, True)
-        gather("V2", "nL", 32)
-        to_list(B5, "b0", "W1")
-        mm(R(B4, 0, 192), R("BLK"), R("b0"), True)
-        either(R("bf"), R(B4, 0, 192))
-        ts(R("SW", 12, 24), R(B5, 0, 12), -MID, OP.add)
-        cp(R("Lb"), R(B5, 0, 12))
-        either(R("Cb"), IND("CR", 192, "Lb", 6, 12))
-        mm(R(B7, 0, 128, 1, 96), R("Cb"), R("ID"), True)
-        either(R("CTB"), R(B7, 0, 128, 1, 96))
-        either(R("CZ", 0, 1536, 16), IND("CR", 192, "Lb", 0, 6))
-        group_sum(KB, "CZ", "Gm", 0, True)
-        for q in (0, 1):
-            spread(q, True)
-        ts(R("n16"), R("nL"), -2048.0, OP.add)
-        for c in range(12):
-            ts(R("EQ", 208 * c, 192 * c + 192), R("bf", 16 * c, 192), -MID, OP.add, R("SW", 12 + c, 13 + c), OP.is_equal)
-        row(B6, "zrow")
-        for c0, c1 in ((0, 4), (4, 11)):
-            mms([(R(B6, 16 * c + 16, 192), R("BLK"), R("EQ", 208 * c + 16, 192 * c + 192)) for c in range(c0, c1)])
-        mms([(R(B6, r, 192, 16), R("LO", 128 * r, 128 * r + 128), R("EQ", r, 2304, 208)) for r in range(1, 16)])
-        for h in (0, 1):
-            either(R("cnt", 192 * h, 192 * h + 192), R(B6, 0, 192))
-        mm(R(B7, 0, 24), R("IDf"), R("SW"), True)
-        to_list(B7, "cnt", "W8", 384, False)
-        tt(R("l1"), R(B7, 0, 24), R("aC"), OP.min)
-        ts(R("LS"), R("l1"), MID, OP.add)
-        from_keys(B7, 4, True)
-        act(R("QR"), R(B7, 0, 192), AF.Square, R("kc"))
-        either(R("QG"), IND("QR", 192, "Lb"))
-        either(R("Mg"), IND(MR, 192, "Lb"))
-        group_sum(KB, "V2", "Gm", 0)
-        group_sum(KE, "V2", "Gm", 1)
-        apart("V2", "CTI", "D2", 0, (B4, B5, B0))
-        apart("V2", "CTB", "DB", 1, (B4, B5, B0))
-        for q in range(4):
-            larger("V2", "CX", "D2" if q > 1 else "DB", q)
-        group_sum(KE, "D2", "G32", 0)
-        group_sum(KB, "DB", "G64", 0)
-        group_sum(KE, "D2", "G64", 1)
-        group_sum(KB, "DB", "G32", 1)
+        largest("FK", 0, KI)
+        rest(BX("VV", ALL, slice(32, 48), p=KP), "FK", "rK")
+        by_block("VN", "nL")
+        gather("V2", "nL", 96, 192, 32)
+        o = R(bank_for("bf"), 0, 192)
+        mm(o, R("BLK"), R("b0"), True)
+        either(R("bf"), o)
+        ends = picked("pb", "bf")
+        ts(R("SW", 12, 24), ends, R("cB"), OP.add, -MID, OP.add)
+        ts(R("Lb"), ends, R("cB"), OP.add)
+        lin(R("Cb"), IND("CR", 192, "Lb"), 1.0, -R1)
+        o = R(bank_for("CTB"), 0, 128, 1, 96)
+        mm(o, R("Cb", 96, 192), R("ID"), True)
+        lin(R("CTB"), o, 1.0, 1024.0)
+        b = bank_for("CB")
+        mms([(R(b, 0, KP), R("on5", 0, 128, 1, 1), R("levA"))]
+            + [(R(b, 17 * j + 1, 17 * j + 17), R("ID"), R("Cb", 16 * j, 16 * j + 16)) for j in range(6)], True)
+        for i in (0, 1):
+            either(R("CB", i, 204, 2), R(b, 0, KP))
+        mm(R(F0, 128, 256, 1, KP), R("CB", 0, 204, 2), R("BKm"))
+        ts(R("n16"), R("nL"), -2048.0, OP.add, 2.0 ** -13, OP.mult)
+        together(lambda c: ts(BX("EQ", c, slice(0, 192 - 16 * c)), R("bf", 16 * c, 192), -MID, OP.add, R("SW", 12 + c, 13 + c), OP.is_equal), range(12), 3)
+        b = bank_for("EQ")
+        mm(R(b, 0, 192), R("cE"), R("half"), True)
+        for c0, c1 in ((0, 3), (3, 6), (6, 11)):
+            mms([(R(b, 16 * c + 16, 192), R("BK8"), BX("EQ", c, slice(16, 192 - 16 * c))) for c in range(c0, c1)])
+        mm(R(b, 0, 192), R("BKh"), BX("EQ", ALL, slice(0, 16)))
+        act(R("cnt"), R(b, 0, 192), AF.Sign)
+        ends = picked("pc", "cnt")
+        b = bank_for("LS")
+        mms([(R(b, 0, 24), R("IDf"), R("SW"))] + [(R(b, lo, lo + 12), R("ID8"), ends) for lo in (0, 12)], True)
+        tt(R("l1"), R(b, 0, 24), R("aC"), OP.min)
+        ts(R("LS"), R("l1"), R("cS"), OP.add)
+        act(IND(IV, 384, "LS", 12, 24), R("aT"), AF.Silu)
+        ts(R("LI"), picked("pi", IV), R("cB"), OP.add, -63.75, OP.add)
+        group_sum(F0, 0, plain("VN"), R("Gm"))
+        apart("V2", "CTI", "D2")
+        apart("V2", "CTB", "DB")
+        larger("VN", "CA", "DJ")
+        larger("VN", "CB", "DK")
+        group_sum(F0, 0, rows_of("DJ"), R("G64"))
+        group_sum(F0, 128, rows_of("DK"), R("G64"))
+        group_sum(F1, 0, plain("D2"), R("G32"), 8)
+        group_sum(F1, 128, plain("DB"), R("G32"), 8)
+        apart("VR", "CT0", "DR")
+        first = R("VR", 1536, 3072, 16)
+        tt(first, first, R("CX", 0, 1536, 16), OP.max)
+        for lo in range(0, 1536, 384):
+            scan(R("DS", lo, lo + 384), R("CX", lo, lo + 384), R("VR", 1536 + lo, 1920 + lo), OP.min, OP.max)
+        group_sum(KR, 0, plain("DR"), R("G32"), 8)
+        group_sum(KR, 128, plain("DS"), R("G64"), 8)
         if not last:
             act(R("xg"), IND("X", 4096, "sL"), AF.Relu, -16.0)
             cp(IND("X", 4288, "LS"), R("xg"))
-        for bank, l in ((B0, "kan"), (B1, "kap")):
+        JI, JR, KK, WN, NI, NR, OW, WS = [bank_for(b) for b in ("JI", "JR", "KK", "WN", "NI", "NR", "OW", "WS")]
+        for bank, l in ((JI, "krow"), (JR, "kneg")):
             row(bank, l)
-            mm(R(bank, 0, 192), R("I13"), R("n16"))
-        mm(R(B5, 0, 192), R("IDn"), R("cnt", 0, 192), True)
-        row(B6, "cI")
-        mm(R(B6, 0, 192), R("IDk"), R("cnt", 0, 192))
-        row(B7, "cR")
-        mm(R(B7, 0, 192), R("IDk"), R("QG"))
-        for i, bank in enumerate((KE, KB)):
-            act(R("FM", 256 * i, 256 * i + 256), R(bank, 0, 256, 1, 96), AF.Sign, R("lim") if t else -15.5, -1.0)
-            scan(R("CN", 256 * i, 256 * i + 256), R("m01", 0, 256, 1, 96), R("FM", 256 * i, 256 * i + 256), OP.mult, OP.add)
-            least("FS", 768 * i, bank)
-            largest("FS", 256 + 256 * i, bank)
-            rest(R("VV", 48 * i, 48 * i + 32), "FS", 512 * i, 512 * i + 512)
-        tt(Z(3), R("CN", 15, 256, 16), R("CN", 271, 512, 16), OP.is_gt)
-        tt(R("SS"), R("VV", 0, 48), R("VV", 48, 96), OP.add)
-        for i in range(3):
-            tt(R("PP", 16 * i, 16 * i + 16), R("SS", 16 * i, 16 * i + 16), Z(3), OP.mult)
-        tt(R("ZZ", 0, 768, 16), R("VV", 48, 96), R("PP"), OP.subtract)
-        for i, bank in enumerate((B0, B1, B4, B5)):
-            from_keys(bank, i, i == 2)
-        for s, bank in (("S0", B0), ("S1", B1)):
+            mm(R(bank, 0, 192), R("ID"), R("n16"))
+        mm(R(WN, 0, 192), R("IDn"), R("cnt"), True)
+        mm(R(KK, 0, 192), R("ID8"), R("cnt"), True)
+        row(NI, "cN" if last else "cI")
+        for h, bank in ((1, F1), (0, F0)):
+            for turn in (h, 1 - h):
+                if turn:
+                    act(BX("FM", ALL, slice(128 * h, 128 * h + 128), p=KP), R(bank, 0, 256, 1, KP), AF.Sign, R("lim") if t else -15.5, -1.0)
+                else:
+                    together(lambda side: (least("FS", 768 * side + 128 * h, bank, 128 * side, 128),
+                                           largest("FS", 256 + 256 * side + 128 * h, bank, 128 * side, 128)), (0, 1), 2)
+        scan(R("CN", 16, 272), BX("FM", 0, p=KP), BX("FM", 1, p=KP), OP.add, OP.subtract)
+        rest(BX("VV", ALL, slice(0, 32), p=KP), "FS", "rS")
+        tt(Z(3), R("CN", 31, 272, 16), R("CN", 15, 256, 16), OP.is_gt)
+        tt(R("SS"), BX("VV", 0, p=KP), BX("VV", 1, p=KP), OP.add)
+        together(lambda lo: tt(R("PP", lo, lo + 16), R("SS", lo, lo + 16), Z(3), OP.mult), (0, 16, 32), 3)
+        tt(R("ZZ", 0, 768, 16), BX("VV", 1, p=KP), R("PP"), OP.subtract)
+        for i, bank in enumerate((JI, JR, KK)):
+            from_keys(bank, i)
+        turn_over(WN, "ZZ", 768, False)
+        for s, bank in (("S0", JI), ("S1", JR)):
             ts(R(s), R(bank, 0, 192), -0.25, OP.max, 0.25, OP.min)
-        act(R("QK"), R(B4, 0, 192), AF.Square, R("kc"))
-        mm(R(B6, 0, 192), R("BK8"), R("S0"))
-        mm(R(B6, 0, 192), R("IDk"), R("QK"))
-        act(R(IC), R(B6, 0, 192), AF.Relu)
+        act(R("QK"), R(KK, 0, 192), AF.Square, R("kc"), 1024.0)
         if not last:
+            mm(R(NI, 0, 192), R("BK8"), R("S0"))
+            mm(R(NI, 0, 192), R("IDn"), R("QK"))
+            act(R(IC), R(NI, 0, 192), AF.Relu)
             send(IC, [(dn1, "inA", "rA"), (up1, "inB", "rB")], HOP)
         else:
+            mms([(R(NI, 0, 96), R("ZX", 0, 128), R("P4")), (R(NI, 96, 192), R("ZX", 128, 256, 1, 96), R("ID4", 0, 96, 1, 96))])
+            mm(R(NI, 0, 192), R("BKn"), R("S0"))
+            mm(R(NI, 0, 192), R("ID"), R("QK"))
+            either(R(IC), R(NI, 0, 192))
             send(IC, [(dn2, "inC", "rC")], 0.8 * HOP)
-        mm(R(B7, 0, 192), R("BK8"), R("S1"))
-        act(R("zr"), R(B7, 0, 192), AF.Relu)
-        tt(IND(MR, 384, "LS", 12, 24), R("zr"), R("Mg"), OP.max)
+        scan(R("FR"), R("mE"), R(KR, 0, 256, 1, KP), OP.add, OP.max)
+        scan(back("FB", 0, 256), R("mE"), back("FR", 0, 256), OP.add, OP.max)
+        tt(R("OR"), R(KR, 0, 256, 1, KP), R("FB"), OP.is_equal)
+        b = bank_for("WR")
+        ts(R("R16"), R(oR), -2048.0, OP.add)
+        row(b, "cW")
+        mm(R(b, 0, 192), R("ID"), R("R16"))
+        mms([(R(b, 96 * h, 96 * h + 96), R("OR", 128 * h, 128 * h + 128, 1, 96), R("IDw", 0, 96, 1, 96)) for h in (0, 1)])
+        either(R("WR"), R(b, 0, 192))
+        row(NR, "cR")
+        mm(R(NR, 0, 192), R("BK8"), R("S1"))
+        either(R("zr", 0, 192), R(NR, 0, 192))
+        tt(R(MR), IND("zr", 208, "LI"), R("WR"), OP.max)
         if not last:
             send(MR, [(up2, "inM", "rR")], 0.8 * HOP)
-        act(R("wf"), R(B5, 0, 192), AF.Relu, acc=R("wc"))
-        mm(R(B2, 0, 192), R("BLK"), R("b0"), True)
-        mm(R(B2, 0, 192), R("ID"), R("wf"))
-        act(R("xa"), R(B2, 0, 192), AF.Copy, 0.0, R("e0"))
-        act(R("ya"), R(B2, 0, 192), AF.Relu, R("eB"), R("e192"))
+        act(R("wf"), R(WN, 0, 192), AF.Relu, -1.0, acc=R("wc"))
+        mms([(R(OW, 0, 192), R("ID"), R("b0")), (R(OW, 0, 192), R("ID"), R("wf"))], True)
+        act(R("xa"), R(OW, 0, 192))
+        act(R("ya"), R(OW, 0, 192), AF.Relu, -192.0 * 191.0, 192.0)
         tt(IND("ow", 4288, "LS"), R("xa"), R("ya"), OP.subtract)
         if not last:
             act(R("wb"), R("wc"))
-            mm(R(B3, 0, 1, 1, 96), R("on5", 0, 96), R("wb"), True)
-            ts(R("wi"), R(B3, 0, 1, 1, 96), 0.0625, OP.mult)
+            mm(R(WS, 0, 1, 1, KP), R("on5", 0, KP), R("wb"), True)
+            cp(R("wi"), R(WS, 0, 1, 1, KP))
             ts(R("wj"), R("wi"), 63, OP.bitwise_and)
             ts(R("lim"), R("wj"), 32.0, OP.mult, -15.5, OP.add)
 
-    def merged(old, new, both, words, out):
-        for lo in (0, 96):
+    def merged(old, new, both, words, out, halves):
+        for lo in halves:
             tt(R(both, lo, lo + 96), R(old, lo, lo + 96), R(new, lo, lo + 96), OP.max)
             ts(R(words, lo, lo + 96), R(both, lo, lo + 96), 4095, OP.bitwise_and)
-            cp(R(out, lo, lo + 96), R(words, lo, lo + 96))
+            o, a = R(out, lo, lo + 96), R(words, lo, lo + 96)
+            emit("vg", {"v": lambda o=o, a=a: g.vector.tensor_copy(o[0], a[0]),
+                        "g": lambda o=o, a=a: g.affine_select(o[0], a[0], [[0, 96]], OP.is_ge, 0.0, 0, 0)}, [o], [a], 1.0, 0.17 + 192 * CYCLE)
 
+    marks = [len(calls)]
+    ts(R("aC"), R("aC"), R("p15"), OP.add, R("cS"), OP.subtract)
+    ms(R("CN", 0, 16), 0.0)
+    for h in (0, 1):
+        either(R("TR", 128 * h, 128 * h + 128), rows)
+    for o, c in ((R("ZZ", 0, 512), 0), (R("ZZ", 512), 0), (R("IV1", 0, 192), 256)):
+        fill(o, c)
     play(0)
-    merged("inM", "inB", "mu", "mw", "oI1")
-    merged("MR0", "inA", "mv", "mi32", "oR1")
-    cp(R("MR1", 0, 192), R("mi32"))
+    marks.append(len(calls))
+    fill(R("cN"), -32768)
+    for name, of, c in (("BKn", "BLK", -8192.0), ("ID4", "ID", 4096.0), ("P4", "P0", 4096.0)):
+        lin(R(name), R(of), c)
+    merged("inM", "inB", "mu", "mw", "oI1", (96, 0))
+    merged("MR0", "inA", "mv", "mi32", "oR1", (0, 96))
+    marks.append(len(calls))
     play(1)
-    merged("MR1", "inC", "mv", "mi32", "yo")
-    stores = [dma("a", hbm("yown"), (T.ow[0:128:16, 0:4096], [("ow", 0, 4096)]), 2.5), dma("s", hbm("ym"), R("yo"), 2.5)]
+    marks.append(len(calls))
+    ts(R("mw"), R("MR1"), 4095, OP.bitwise_and)
+    for lo in (96, 0):
+        tt(R("inA", lo, lo + 96), R("mw", lo, lo + 96), R("inC", lo, lo + 96), OP.min)
+        act(R("yo", lo, lo + 96), R("inA", lo, lo + 96), AF.Abs)
+    stores = [dma("a", 2.5, (hbm("yown"), (T.ow[0:128:16, 0:4096], [("ow", 0, 4096)]))), dma("s", 2.5, (hbm("ym"), R("yo")))]
+    if not ORDER:
+        order, place, _ = arrange(calls, other, span, use, marks)
+        ORDER.extend(order)
+        BANK.update(place)
+        return
     count = issue_all()
     for q in count:
         g.wait_ge(S["q" + q], count[q])
     for sem, val in sent:
         g.wait_ge(S[sem], val)
-    g.wait_ge(S[stores[0]], 16)
-    g.sync.wait_ge(S[stores[1]], 16)
+    for sem in stores:
+        g.sync.wait_ge(S[sem], 16)

import numpy as np
from concourse.bass import DstId, RemoteDMATransfer
from concourse.mybir import AluOpType, ActivationFunctionType

OP = AluOpType
AF = ActivationFunctionType
F32, BF, I32, U16, F16 = "float32", "bfloat16", "int32", "uint16", "float16"
SIZE = {F32: 4, I32: 4, BF: 2, U16: 2, F16: 2}
BIG = float(2 ** 22)
R1, R32 = 1.5 * 2 ** 23, 1.5 * 2 ** 28
MID = 2047.5
KP = 102
ALL = slice(None)
CYCLE, WAKE, HOP = 0.00087, 0.18, 2.0
TRIES = 90000
FAR, WARM = 0.75, 0.012
ROUND = {
    "v": "[BKn [ID4 [P4 [mv*2 [mi32*2 [mu*2 [mw*2 [oI*2 VA*3 XB NB XB NB VA XB NB XB NB VA XA CTI VA XA*5 NR XR*2 NR CA XR DI*2 XR DI*2 NR*2 M16 "
         "(aC FK CT0 (CN FB XR OH NR*2 XR S2 XR*2 NR*2 sL nL FK SW CS rK bf VN pb VN Lb Cb VN SW CTB VN*3 EQ R16 DJ EQ CB EQ DK DJ DK*2 EQ DJ*2 VV DK n16 "
         "FS VR FS DS rS pc DS VV CN l1 SS ZZ LS DS PP DS ZZ ZX*3 FR S0 FB S1 pi OR LI X MR wi ow wj lim",
    "a": "VR VB*4 VR*3 (TR*2 DA*3 VR*2 DR*3 b0 CR V2*3 D2*3 DB CB DB*2 xg FM cnt FM IV QK wf IC zr wb WR ya xa",
    "p": "KI CTI DA*4 CA DA*2 KI*10 CT0 DR*4 OH DR*2 sL KR*2 CR KR bf Fa*2 Fb KR*2 D2*4 CTB D2*2 DB*2 CB DB*4 EQ Fb Fa Fb Fa*3 Fb*2 Fa*9 EQ*4 "
         "KR*2 LS JI*2 KK NI WR*2 NR JR*2 WN KR*2 JI KK JR WN NI*3 NR OW WR WS",
    "g": "[cN [oR*2 CX (ZZ*2 IC MR (IV",
}
ORDER, BANK = [], {}

OWN_TILES = {
    F32: "ow:4288 IC0:192 IC1:192 MR0:192 inA:192 inB:192 inM:192 inC:192 yo:192 ob:256 CR:192 zr:208 IV0:384 IV1:384 aT:192",
    BF: "X:4288 VB:1536 XB:1536 NB:1536 VR:3168 XR:3072 NR:3072 CX:1536 V2:1536 DA:1632 DR:1632 DS:1632 D2:1632 DB:1632 "
        "on5:512 m01:384 m512:384 EX:1536",
    F16: "VA:1632 VN:1632 XA:816 NA:816 DI:1632 DJ:1632 DK:1632",
    I32: "nbw:4096 od:256 mi32:192 thi:8",
    U16: "oR0:192 oI0:192",
}
BOXES = {"EQ": ([12, 192], BF), "FM": ([2, 256], BF), "VV": ([2, 48], BF)}
POOLS = {
    F32: "p15:1 p16:1 kc:1 cB:1 cS:1 aC:24 IDf:128 FS:1024/102 FK:512/102 FR:256/102 FB:256/102 rS:64/102 rK:32/102 SW:24 l1:24 "
         "xa:192 ya:192 WR:192 wc:1 lim:1/102",
    BF: "BLK:128 BK8:128 BKm:128 ID:128 IDn:128 IDh:128 ID8:128 IDw:128 G64:8 G32:8 Gm:16 W1:144 MK:192 pb:256 pi:192 "
        "mB:256/102 mD:256/102 mE:256/102 krow:256/1 kneg:256/1 TR:256/3 thd:3 cI:128/1 cR:128/1 cW:128/1 cE:128/1 cq:128/1 cN:128/1 BKn:128 ID4:128 P4:96/102 half:192/1 h0:192/1 h1:192/1 BKh:128 "
        "lev:256 levA:102/1 SS:48/102 PP:48/102 ZZ:1024/102 ZX:768/102 OH:256/102 OR:256/102 b0:192 bf:192 cnt:192 Cb:192 QK:192 P0:96/102 "
        "wf:192 wb:1 xg:192 CS:96",
    F16: "IDg:128 pc:192 R16:192 M16:192 n16:192 S0:192 S1:192 S2:192 CA:204 CB:204 CTI:128/96 CTB:128/96 CT0:128/96 CN:272/102",
    I32: "pI:1 pJ:1 wi:1/102 wj:1/102 td:2 mw:192 mv:192 mu:192 MR1:192",
    U16: "oI1:192 oR1:192 sL:12 nL:192 Lb:12 LS:24 LI:12",
}
SCRATCH, SHAPE, PLACE = {}, {}, {}
for _n, (_w, _d) in BOXES.items():
    SCRATCH[_n] = ("sbuf", [128] + _w, _d)
for _d, _names in OWN_TILES.items():
    for _n in _names.split():
        _n, _w = _n.split(":")
        SCRATCH[_n] = ("sbuf", [128, int(_w)], _d)
        SHAPE[_n], PLACE[_n] = (128, int(_w)), (_n, 0)
for _d, _names in POOLS.items():
    _at = 0
    for _n in _names.split():
        _n, _w = _n.split(":")
        _w = (_w + "/128").split("/")
        SHAPE[_n], PLACE[_n] = (int(_w[1]), int(_w[0])), ("pool_" + _d, _at)
        _at += -(-int(_w[0]) // 16) * 16
    SCRATCH["pool_" + _d] = ("sbuf", [128, _at], _d)
PSUM = ["b%d_" % _i for _i in range(8)]
for _n in PSUM:
    SCRATCH[_n] = ("psum", [128, 512], F32)
SEMAPHORES = ["qv", "qa", "qp", "qg"] + ["d%d" % i for i in range(8)] + ["rM", "rN", "rA", "rB", "rR", "rC"] + ["l%d" % i for i in range(5)]


def arrange(calls, other, span, use, marks):
    n = len(calls)
    qs = [c[0] for c in calls]
    name = [c[3][0].split("@")[0] for c in calls]
    users = [[] for _ in calls]
    for i, c in enumerate(calls):
        for d in c[5]:
            users[d].append(i)
    held = {}
    for i, u in use.items():
        held.setdefault(u, []).append(i)
    opens = {lst[0]: u for u, lst in held.items()}
    readers = {u: [d for d in lst if qs[d] != "p"] for u, lst in held.items()}
    short, long = 0.7 * WAKE, 1.3 * WAKE
    gap = [[(d, calls[d][2] - calls[d][1] + short * w, calls[d][2] - calls[d][1] + long * w)
            for d in c[5] for w in [qs[d] != "x" and not qs[d] == qs[i] == "p"]] for i, c in enumerate(calls)]
    busy = [{q: (x - span.get(i, 0.0), x + span.get(i, 0.0)) for q in qs[i] for x in [c[1] if q == qs[i][0] else other.get(i, c[1])]} for i, c in enumerate(calls)]
    blank = ([0.0] * (n + 1), [0.0] * (n + 1), [n] * n, [n] * n, {}, {},
             [(dict.fromkeys("vapgsx", n), [(0.0, b, "") for b in range(len(PSUM))], {u: len(lst) for u, lst in held.items()})])

    def length(seq, eng, lo=0, known=blank):
        ends, endl, whys, whyl, at, after = [x.copy() for x in known[:6]]
        stops = known[6][:lo // 32 + 1]
        last, banks, rest = [x.copy() for x in stops[-1]]
        for x in range(lo // 32 * 32, n):
            if x % 32 == 0 and x > lo:
                stops.append((last.copy(), banks.copy(), rest.copy()))
            i = seq[x]
            q = eng[i]
            ws = wl = last[q]
            s, l = ends[ws], endl[wl]
            for d, a, b in gap[i]:
                if ends[d] + a > s:
                    s, ws = ends[d] + a, d
                if endl[d] + b > l:
                    l, wl = endl[d] + b, d
            if i in opens:
                if not banks:
                    return 1e9, None, None
                banks.sort()
                _, at[opens[i]], was = banks.pop(0)
                after[i] = readers.get(was, ())
                for d in after[i]:
                    if ends[d] + short > s:
                        s, ws = ends[d] + short, d
                    if endl[d] + long > l:
                        l, wl = endl[d] + long, d
            a, b = busy[i][q]
            ends[i], endl[i], whys[i], whyl[i], last[q] = s + a, l + b, ws, wl, i
            if i in use:
                rest[use[i]] -= 1
                if not rest[use[i]]:
                    banks.append((ends[i], at[use[i]], use[i]))
        total, steps = 0.0, []
        for end, why in ((ends, whys), (endl, whyl)):
            e, i = max((end[i] + calls[i][2] - calls[i][1], i) for i in range(n - 2, n))
            total += e
            while why[i] < n:
                steps.append((i, why[i]))
                i = why[i]
        return total, steps, (ends, endl, whys, whyl, at, after, stops)

    eng, lists, taken = [q[0] for q in qs], {q: [i for i in range(marks[0]) if qs[i][0] == q] for q in "vapgsx"}, set(range(marks[0]))
    for lo, mid, hi in ((marks[0], marks[0], marks[1]), (marks[1], marks[2], marks[3])):
        for q, text in ROUND.items():
            for word in text.split():
                word, _, k = word.partition("*")
                a, b = (lo, mid) if word[0] == "[" else (mid, hi if word[0] != "(" or lo == mid else mid)
                fit = [i for i in range(a, b) if i not in taken and q in qs[i] and word.lstrip("[(") in (name[i], name[i][:-1])]
                for i in sorted(fit, key=lambda i: len(qs[i]))[:int(k or 1)]:
                    taken.add(i)
                    lists[q].append(i)
                    eng[i] = q
    for i in range(n):
        if i not in taken:
            lists[eng[i]].append(i)
    seq, end, free, left, count = [], {}, dict.fromkeys(lists, 0.0), {u: len(lst) for u, lst in held.items()}, len(PSUM)
    while len(seq) < n:
        t, i = min((max([free[q]] + [end[d] + WAKE for d in calls[lst[0]][5]]), lst[0]) for q, lst in lists.items()
                   if lst and all(d in end for d in calls[lst[0]][5]) and (count or lst[0] not in opens))
        lists[eng[i]].pop(0)
        free[eng[i]], end[i] = t + calls[i][1], t + calls[i][2]
        seq.append(i)
        if i in use:
            left[use[i]] -= 1
            count += (not left[use[i]]) - (i in opens)
    best, steps, known = length(seq, eng)
    top = (best, seq, eng, known)
    both = [i for i in range(marks[0], n) if len(qs[i]) > 1]
    pos = {i: x for x, i in enumerate(seq)}
    rng = np.random.RandomState(5)
    for it in range(TRIES):
        new, turn, r = seq, None, rng.rand()
        if r < 0.75:
            x = int(rng.randint(len(steps)))
            i, j = steps[x]
            early = rng.rand() < 0.5
            while rng.rand() < FAR:
                x += 1 if early else -1
                if not 0 <= x < len(steps) or eng[steps[x][early]] != eng[i if early else j] or steps[x][not early] != (j if early else i):
                    break
                i, j = (i, steps[x][1]) if early else (steps[x][0], j)
            if j < marks[0]:
                continue
            if len(qs[j]) > 1 and (j in calls[i][5] or rng.rand() < 0.3):
                turn = j
            elif len(qs[i]) > 1 and rng.rand() < 0.3:
                turn = i
            else:
                lo, hi = pos[j], pos[i] if early or rng.rand() < 0.5 else min(n - 1, pos[i] + int(rng.exponential(10)))
                piece, moved = seq[lo:hi + 1], {i if early else j}
                for k in piece[::-1] if early else piece:
                    if k in moved:
                        moved.update(calls[k][5] if early else users[k])
                if i in moved and j in moved:
                    continue
                new = seq[:lo] + [k for k in piece if (k in moved) == early] + [k for k in piece if (k in moved) != early] + seq[hi + 1:]
        elif r < 0.82:
            turn = both[int(rng.randint(len(both)))]
        else:
            i = int(rng.randint(marks[0], n))
            lo, hi = max([pos[d] for d in calls[i][5]] + [1]) + 1, min([pos[d] for d in users[i]] + [n]) - 1
            new = seq[:pos[i]] + seq[pos[i] + 1:]
            x = int(min(hi, max(lo, pos[i] + rng.normal() * (100 if rng.rand() < 0.3 else 20))))
            new.insert(x, i)
            lo = min(x, pos[i])
        on = eng
        if turn is not None:
            on, lo = eng[:turn] + [qs[turn].replace(eng[turn], "")] + eng[turn + 1:], pos[turn]
        e, s, k = length(new, on, lo, known)
        if e <= best + (0.002 + WARM * (1 - it / TRIES)) * rng.exponential():
            seq, eng, best, steps, known = new, on, e, s, k
            if e < top[0]:
                top = (e, seq, eng, known)
            if it % 16 == 0:
                new = [seq[x] for x in sorted(range(n), key=lambda x: (k[0][seq[x]] - busy[seq[x]][eng[seq[x]]][0], x))]
                e, s, k = length(new, eng)
                if e <= best:
                    seq, best, steps, known = new, e, s, k
            pos = {i: x for x, i in enumerate(seq)}
    best, seq, eng, known = top
    return [(i, eng[i], known[5].get(i, ())) for i in seq], known[4], best / 2


def rank_program(g, core, T, topo):
    rank = T.rank_of(core)
    if rank is None:
        return
    if not ORDER:
        program(g, core, rank, T, topo)
    program(g, core, rank, T, topo)


def program(g, core, rank, T, topo):
    n_ranks = len(T.cores)
    S = T.sem
    queue = {"v": g.vector, "a": g.scalar, "p": g.tensor, "g": g, "s": g.sync}
    uses = []

    def bank_for(what):
        uses.append(what)
        return "%s@%d" % (what, len(uses))

    def R(name, lo=0, hi=None, step=1, p=None):
        shape = SHAPE.get(name, (128, 512))
        hi = shape[1] if hi is None else hi
        p = shape[0] if p is None else p
        buf, at = PLACE.get(name) or (PSUM[BANK.get(name, 0)], 0)
        ap = T[buf][0:p, at + lo:at + hi:step] if step > 1 else T[buf][0:p, at + lo:at + hi]
        return (ap, [(name, lo, hi)], -(-(hi - lo) // step), SIZE[SCRATCH[buf][2]], "@" in name, False)

    def back(name, lo, hi, step=1):
        buf, at = PLACE[name]
        return (T[buf][0:SHAPE[name][0], at + hi - 1:at + lo - 1:-step],) + R(name, lo, hi, step)[1:]

    def BX(name, *at, p=128):
        shape, d = BOXES[name]
        cols = np.sort(np.arange(shape[0] * shape[1]).reshape(shape)[at].reshape(-1))
        cut = [0] + [int(i) + 1 for i in np.nonzero(np.diff(cols) > 16)[0]] + [len(cols)]
        return (T[name][(slice(0, p),) + at], [(name, int(cols[a]), int(cols[b - 1]) + 1) for a, b in zip(cut, cut[1:])], len(cols), SIZE[d], False, False)

    def IND(win, n, off, c0=0, c1=12):
        buf, at = PLACE[off]
        return (T[win][:, 0:n].indirect(T[buf][:, at + c0:at + c1]), [(win, 0, n), (off, c0, c1)], 16 * (c1 - c0), 4, False, True)

    def hbm(name):
        return (T[name][:], [(name, 0, 1)])

    def spans(refs):
        return [s for r in refs if isinstance(r, tuple) for s in r[1]]

    def ap(x):
        return x[0] if isinstance(x, tuple) else x

    calls = []
    seen = {}
    group = {}
    other = {}
    bundle = []
    use = {}
    span = {}

    def put(q, busy, late, outs, ins, issue, loose=False, after=()):
        if bundle:
            return bundle[0].append((q, busy, outs, ins, issue))
        rd, wr = spans(ins), spans(outs)
        deps = set(after)
        for lst, w in ((rd, False), (wr, True)):
            for name, lo, hi in lst:
                for e in seen.get(name, ()):
                    if "@" in name and (q != e[1] or q == "p" or len(q) > 1):
                        hit = not (loose and e[5])
                    else:
                        hit = (w or e[0]) and e[3] < hi and lo < e[4] and not (w and loose and e[5])
                    if hit:
                        deps.add(e[2])
        for lst, w in ((rd, False), (wr, True)):
            for name, lo, hi in lst:
                old = seen.setdefault(name, [])
                if w and not loose:
                    old[:] = [e for e in old if not (lo <= e[3] and e[4] <= hi) and "@" not in name]
                old.append([w, q, len(calls), lo, hi, loose])
                if "@" in name:
                    use[len(calls)] = name
        calls.append((q, busy, late, (wr + rd)[0], issue, sorted(deps)))
        return len(calls) - 1

    def together(f, items, n):
        items = list(items)
        for lo in range(0, len(items), n):
            bundle.append([])
            for x in items[lo:lo + n]:
                f(x)
            lst = bundle.pop()
            c = sum(e[1] for e in lst)
            put(lst[0][0], c, c, [o for e in lst for o in e[2]], [a for e in lst for a in e[3]], lambda lst=lst: [e[4]() for e in lst])

    def emit(q, call, outs, ins, each=1.0, second=None):
        o = outs[0]
        full = [x for x in ins if isinstance(x, tuple) and x[2] > 1] or [o]
        if o[5]:
            outs, ins = [(0, o[1][:1])], ins + [(0, o[1][1:])]
            c = 60 + 3.5 * o[2]
        elif full[0][5]:
            c = 70 + 1.5 * o[2]
        else:
            c = max(64, o[2] * (0.5 if each == 0.5 and all(x[3] == 2 for x in full + [o]) else max(each, 1.0)))
        i = put(q, c * CYCLE, c * CYCLE, outs, ins, call)
        if second:
            other[i] = second
        span[i] = (2.0 * o[2] if o[5] else 0.45 * o[2] if full[0][5] else 0.0) * CYCLE

    def tt(o, a, b, op):
        emit("v", lambda: g.vector.tensor_tensor(o[0], a[0], b[0], op), [o], [a, b], 1.0 if a[4] or b[4] else 2.0)

    def ts(o, a, s1, op0, s2=None, op1=None):
        if op1 is None:
            emit("v", lambda: g.vector.tensor_scalar(o[0], a[0], ap(s1), None, op0), [o], [a, s1], 0.5)
        else:
            emit("v", lambda: g.vector.tensor_scalar(o[0], a[0], ap(s1), ap(s2), op0, op1), [o], [a, s1, s2], 0.5)

    def cp(o, a):
        emit("v", lambda: g.vector.tensor_copy(o[0], a[0]), [o], [a], 0.5)

    def ms(o, c):
        emit("v", lambda: g.vector.memset(o[0], c), [o], [], 0.5)

    def scan(o, d0, d1, op0, op1, first=0.0):
        emit("v", lambda: g.vector.tensor_tensor_scan(o[0], d0[0], d1[0], first, op0, op1), [o], [d0, d1], 0.5)

    def act(o, a, func=AF.Copy, bias=0.0, scale=1.0, acc=None):
        if o[5]:
            emit("a", lambda: g.scalar.activation(o[0], a[0], func), [o], [a])
        elif acc is None:
            emit("a", lambda: g.scalar.activation(o[0], a[0], func, bias=ap(bias), scale=ap(scale)), [o], [a, bias, scale])
        else:
            emit("a", lambda: g.scalar.activation(o[0], a[0], func, bias=ap(bias), scale=ap(scale), accum_out=acc[0]), [o, acc], [a, bias, scale])

    def either(o, a):
        emit("av", {"a": lambda: g.scalar.activation(o[0], a[0], AF.Copy), "v": lambda: g.vector.tensor_copy(o[0], a[0])}, [o], [a])

    def fill(o, c):
        t = 0.13 + 2 * o[2] * CYCLE
        other[put("gv", t, t, [o], [], {"g": lambda: g.iota(o[0], [[0, o[2]]], c, 0, allow_small_or_imprecise_dtypes=True),
                                        "v": lambda: g.vector.memset(o[0], float(c))})] = max(64, o[2] * o[3] / 4) * CYCLE

    def lin(o, a, mul, add=0.0):
        emit("va", {"v": lambda: g.vector.tensor_scalar(o[0], a[0], mul, add, OP.mult, OP.add),
                    "a": lambda: g.scalar.activation(o[0], a[0], AF.Copy, bias=add, scale=mul)}, [o], [a], 0.5,
             None if a[5] else max(64, o[2]) * CYCLE)

    def mms(lst, start=False):
        bank = lst[0][0][1][0][0]
        if start:
            group[bank] = [0]
        left = group[bank]
        left[0] += len(lst)

        def issue():
            for i, (o, l, r) in enumerate(lst):
                left[0] -= 1
                ins = g.tensor.matmul(o[0], l[0], r[0], start and i == 0, left[0] == 0)
            return ins
        c = sum(max(min(64, l[2]), r[2]) * (4 if l[3] == 4 else 1) for o, l, r in lst) * CYCLE / 2
        put("p", c, c, [m[0] for m in lst], [x for m in lst for x in m[1:]], issue, not start)

    def mm(o, l, r, start=False):
        mms([(o, l, r)], start)

    def iota(o, pat, base=0, cm=0, flag=True):
        kw = {"allow_small_or_imprecise_dtypes": True} if flag else {}
        c = 0.13 + 2 * o[2] * CYCLE
        put("g", c, c, [o], [], lambda: g.iota(o[0], pat, base, cm, **kw))

    def select(o, a, pat, op, base, cm, loose=False):
        c = 0.17 + 2 * o[2] * CYCLE
        put("g", c, c, [o], [a], lambda: g.affine_select(o[0], a[0], pat, op, 0.0, base, cm), loose)

    dmas, sent = [], []

    def dma(q, late, *pairs):
        sem = "d%d" % len(dmas)
        dmas.append(sem)

        def issue():
            for a, b in pairs:
                queue[q].dma_start(a[0], b[0]).then_inc(S[sem], 16)
            return (sem, 16 * len(pairs))
        put(q, 0.05 * len(pairs), late, [a for a, b in pairs], [b for a, b in pairs], issue)
        return sem

    def send(src, outs, late, half=None):
        ls = "l%d" % len(sent)
        lo, hi = (0, 192) if half is None else (96 * half, 96 * half + 96)
        tr = []
        for i, (d, land, rs) in enumerate(outs):
            dst = T.cores[d]
            rid, pid, _ = topo.addr(dst)
            es = topo.engines(core, dst)
            m = len(es) // (len(outs) if half is None else 2)
            i += half or 0
            tr.append((rid, pid, sum(1 << e for e in es[i * m:(i + 1) * m]), land, rs))
        sent.append((ls, m * len(outs)))

        def issue():
            if len(tr) == 1:
                rid, pid, mask, land, rs = tr[0]
                g.remote_dma(T[land][:, lo:hi], T[src][:, lo:hi], S[rs], S[ls], pid, rid, mask)
            else:
                g.remote_dma_fused([RemoteDMATransfer(dst_ids=[DstId(rid=rid, pnc=pid)], dma_engine_mask=mask, remote_sem=S[rs],
                                                      src=T[src][:, lo:hi], dst=T[land][:, lo:hi]) for rid, pid, mask, land, rs in tr], local_sem=S[ls])
            return (ls, m * len(outs))
        busy = 0.4 if half is None else 0.9
        me = put("g", busy, busy, [], [R(src, lo, hi)], issue)
        for d, land, rs in outs:
            put("x", 0.0, late - busy, [R(land, lo, hi)], [], (rs, m), False, [me])

    def issue_all():
        count = {q: 0 for q in "vapg"}
        known = {q: {} for q in queue}
        snap, done = {}, {}
        for i, q, after in ORDER:
            qs, _, _, lab, issue, deps = calls[i]
            if len(qs) > 1:
                issue = issue[q]
            if q == "x":
                done[i] = issue
                continue
            want = {}
            for d in list(deps) + list(after):
                if not q == calls[d][0] == "p":
                    sem, val = done[d]
                    want[sem] = max(want.get(sem, 0), val)
            k = known[q]
            for sem, val in sorted(want.items(), key=lambda d: -len(snap.get(d, {}))):
                if k.get(sem, 0) < val:
                    queue[q].wait_ge(S[sem], val)
                    for s2, v2 in snap.get((sem, val), {}).items():
                        k[s2] = max(k.get(s2, 0), v2)
                    k[sem] = val
            r = issue()
            if not isinstance(r, tuple):
                for ins in r if isinstance(r, list) else [r]:
                    count[q] += 1
                    ins.then_inc(S["q" + q], 1)
                r = ("q" + q, count[q])
            done[i] = r
            snap[r] = dict(k)
        return count

    up1, up2 = (rank + 1) % n_ranks, (rank + 2) % n_ranks
    dn1, dn2 = (rank - 1) % n_ranks, (rank - 2) % n_ranks

    dma("s", 1.8, (R("mi32"), hbm("m0")))
    dma("s", 4.4, (R("X", 0, 4096), hbm("x0")))
    ms(R("thi"), 0)
    dma("a", 2.0, ((T.thi[0:128:16, 0:1], [("thi", 0, 8)]), hbm("th")))
    ms(R("on5"), 1.0)
    iota(R("pI"), [[0, 1]], 0, 1, False)
    iota(R("lev"), [[-256, 16], [0, 16]], 1792)
    select(R("ID"), R("on5", 0, 128), [[-1, 128]], OP.is_equal, 0, 1)
    select(R("BLK"), R("on5", 0, 128), [[-16, 8], [0, 16]], OP.is_ge, 0, 1)
    select(R("BLK"), R("BLK"), [[16, 8], [0, 16]], OP.is_ge, 15, -1)
    ms(R("m01"), 1.0)
    together(lambda lo: ms(R("VA", lo, lo + 16), 2048.0), range(0, 1632, 272), 6)
    ms(R("XA", 0, 816, 136), 0.0)
    ms(R("NA", 7, 816, 136), 0.0)
    ms(R("cq"), -0.25)
    ms(R("m01", 0, 384, 16), 0.0)
    ts(R("pJ"), R("pI"), 15, OP.bitwise_and)
    ms(R("W1"), 0.0)
    lin(R("m512"), R("m01"), -512.0, 512.0)
    cp(R("p15"), R("pJ"))
    ts(R("p16"), R("pJ"), 1.0, OP.add)
    lin(R("mB"), R("m01", 0, 256, 1, KP), -BIG, BIG)
    scan(R("pb"), R("m01", 0, 256), R("m01", 0, 256), OP.mult, OP.add)
    lin(R("mD"), R("m01", 0, 256, 1, KP), BIG + 2.0, -BIG)
    put("a", 1.5, 1.5, [R("IV0")], [R("on5")], lambda: g.scalar.activation(T.IV0[:, 0:192], T.on5[:, 0:192], AF.Silu, scale=256.0))
    for lo in range(0, 3584, 512):
        act(R("ow", lo, lo + 512), R("on5"), AF.Copy, 0.0, 0.0)
    for h, rs in enumerate(("rM", "rN")):
        cp(R("oR0", 96 * h, 96 * h + 96), R("mi32", 96 * h, 96 * h + 96))
        send("oR0", [(up1, "oI0", rs)], 2.8 - 0.4 * h, h)
    behind = [("X", 0, 1)]
    dma("s", 2.0, (R("od"), (T.own0[:], behind)))
    dma("s", 4.5, (R("nbw", 0, 2048), (T.nb[:, 0:2048], behind)))
    lin(R("mE"), R("m01", 0, 256, 1, KP), BIG, -BIG)
    lin(R("krow"), R("pb", p=1), 1.0, -15.0)
    lin(R("kneg"), R("pb", p=1), -1.0, 15.0)
    ms(R("cE"), -2.5)
    ts(R("kc"), R("pJ"), -1024.0, OP.mult, 1024.0 * (8192 + 15), OP.add)
    ts(R("cB"), R("p15"), 15.0, OP.is_lt, 256.0, OP.mult)
    ts(R("IDg"), R("ID"), 511.0 / 1024.0, OP.mult)
    lin(R("IDh"), R("ID"), 0.5)
    ts(R("cS"), R("cB"), 8192.0, OP.mult, MID + 8192.0, OP.add)
    for name, lo, c in (("G64", 0, 64.0), ("G32", 0, 32.0), ("Gm", 0, -32.0), ("Gm", 8, -32.0)):
        lin(R(name, lo, lo + 8), R("BLK", 0, 128, 16), c)
    lin(R("W1", 15, 143, 16), R("BLK", 0, 128, 16), 1.0)
    iota(R("aC", 0, 12), [[16, 12]], 4096)
    iota(R("aC", 12, 24), [[16, 12]], 192)
    ts(R("pc"), R("pb", 0, 192), R("p15"), OP.is_equal, 1024.0, OP.mult)
    ts(R("pi"), R("pb", 0, 192), R("p16"), OP.is_equal, -0.25, OP.mult)
    lin(R("h0"), R("m01", 0, 192, 1, 1), 0.5)
    lin(R("h1"), R("m01", 0, 192, 1, 1), -1.0, 1.0)
    scan(R("MK"), R("pi"), R("pc"), OP.mult, OP.add)
    scan(R("half"), R("h0"), R("h1"), OP.mult, OP.add)
    ts(R("td", 0, 1), R("thi", 0, 1), 6, OP.arith_shift_right)
    ts(R("td", 1, 2), R("thi", 0, 1), 63, OP.bitwise_and)
    ms(R("thd", 0, 1), 0.0)
    ts(R("thd", 1, 2), R("td", 0, 1), -2048.0, OP.mult)
    ts(R("thd", 2, 3), R("td", 1, 2), -32.0, OP.mult)
    for name, c in (("IDn", -1.0), ("IDf", 1.0), ("ID8", 8192.0), ("IDw", -2.0 ** 17)):
        lin(R(name), R("ID"), c)
    o = R(bank_for("BKh"), 0, 1)
    mm(o, R("half", 0, 128), R("on5", 0, 1, 1, 1), True)
    lin(R("BK8"), R("BLK"), 8192.0)
    lin(R("BKm"), R("BLK"), -32.0)
    ts(R("BKh"), R("BLK"), o, OP.mult)
    rows = R(bank_for("TR"), 0, 128, 1, 3)
    mms([(rows, R("thd"), R("BLK")), (rows, R("h1", 0, 3), R("krow", 0, 128))], True)
    fill(R("ow", 3584), 0)
    for i in range(3):
        select(R("EX", 512 * i, 512 * i + 512, 1, 96), R("on5", p=96), [[-1, 32], [0, 16]], OP.is_equal, -32 * i, 1)
        if not i:
            select(R("ob"), R("od"), [[0, 256]], OP.is_ge, 0, 0)
            dma("s", 6.0, ((T.ow[0:128:16, 0:4096], [("ow", 0, 4096)]), R("ob")), (R("nbw", 2048), (T.nb[:, 2048:4096], [])))
    fill(R("DA", 1536), 0)
    select(R("P0"), R("on5", 0, 96, 1, KP), [[-17, 6], [-1, 16]], OP.is_equal, -1, 1)
    iota(R("levA"), [[0, 6], [-256, 17]], 2048)
    together(lambda lo: iota(R("VN", lo, lo + 16), [[0, 16]], 2048), range(0, 1632, 272), 6)
    for v in ("VR", "DR", "D2", "DB", "DS"):
        fill(R(v, SHAPE[v][1] - 96), 0)
    iota(R("aT"), [[1, 192]], 64)
    for name, c in (("cI", 2 ** 18 + 32768), ("cR", 2 ** 16 + 32768), ("cW", 2 ** 17 + 2048)):
        fill(R(name), c)
    for o in (R("zr", 192), R("X", 4096)):
        fill(o, 0)

    def by_block(v, off):
        for b in range(6):
            tt(R(v, 272 * b + 16, 272 * b + 272), IND("X", 4096, off, 16 * b, 16 * b + 16), R("lev"), OP.add)

    def gather(v, off, lo, hi, n, at=96):
        for a in range(lo, hi, n):
            either(R(v, 16 * (a - at), 16 * (a - at + n)), IND("X", 4096, off, a, a + n))

    def extremes(v, mx, mn, n):
        for lo in range(0, 384 * n, 384):
            scan(R(mx, lo, lo + 384), R("m01"), R(v, lo, lo + 384), OP.mult, OP.max)
            scan(R(mn, lo, lo + 384), R("m512"), R(v, lo, lo + 384), OP.add, OP.min)

    def on_levels(lo):
        hi = lo + 256
        scan(back("XA", lo // 2, hi // 2), back("VA", lo, hi, 2), back("VA", lo, hi - 1, 2), OP.max, OP.max, -4096.0)
        scan(R("NA", lo // 2, hi // 2), R("VA", lo, hi, 2), R("VA", lo + 1, hi, 2), OP.min, OP.min, 4096.0)

    def row(bank, l):
        mm(R(bank, 0, 192), R(l, 0, 128), R("on5", 0, 192, 1, 1), True)

    def opened(bank, n, rows):
        mm(R(bank, 0, 256, 1, KP), R("on5", 0, KP, 1, n), R(rows), True)

    def group_sum(bank, at, src, w, n=4):
        ks = [k // 2 + 8 * (k % 2) for k in range(16)]
        for k0 in range(0, 16, n):
            mms([(R(bank, at + k, at + 16 * w[2], 16, KP), src(k), w) for k in ks[k0:k0 + n]])

    def rows_of(d):
        return lambda k: R(d, 204 * (k % 8) + k // 8, 204 * (k % 8) + 204, 2)

    def plain(d, at=0):
        return lambda k: R(d, at + k, at + 1632, 16)

    def Z(i):
        return R("ZZ", 256 * i, 256 * i + 256, 16)

    def turn_over(bank, src, at, start):
        mms([(R(bank, 0, 96), R(src, at, at + 128), R("P0")), (R(bank, 96, 192), R(src, at + 128, at + 256, 1, 96), R("ID", 0, 96, 1, 96))], start)

    def from_keys(bank, i):
        scan(R("ZX", 256 * i, 256 * i + 256), R("m01", 0, 256, 1, KP), R("ZZ", 256 * i, 256 * i + 256), OP.mult, OP.add)
        turn_over(bank, "ZX", 256 * i, False)

    def picked(out, src):
        scan(R(out, 0, 192), R("MK"), R(src, 0, 192), OP.add, OP.min)
        return R(out, 15, 192, 16)

    def turned_centres(mx, mn, ct):
        o = R(bank_for(ct), 0, 128, 1, 96)
        mms([(o, R(m, 15, 1536, 16), R("IDg")) for m in (mx, mn)], True)
        lin(R(ct), o, 1.0, 1024.0)

    def apart(v, ct, d):
        for lo in (0, 512, 1024):
            o = R(bank_for(d))
            two = [(o, R("IDn"), R(v, lo, lo + 512)), (o, R(ct), R("EX", lo, lo + 512, 1, 96))]
            mm(*two[d == "D2"], True)
            mm(*two[d != "D2"])
            act(R(d, lo, lo + 512), o, AF.Abs, -1024.0)

    def larger(v, c, d):
        together(lambda k: scan(R(d, 204 * k, 204 * k + 204), R(c), R(v, k, 1632, 8), OP.min, OP.max), range(8), 2)

    def least(f, at, bank, lo=0, n=256):
        scan(R(f, at, at + n), R("mB", 0, n), R(bank, lo, lo + n, 1, KP), OP.add, OP.min)

    def largest(f, at, bank, lo=0, n=256):
        scan(R(f, at, at + n), R("mD", 0, n), R(bank, lo, lo + n, 1, KP), OP.add, OP.max)

    def rest(o, f, r):
        ends = R(f, 15, None, 16)
        ts(R(r), ends, R32, OP.add, R32, OP.subtract)
        tt(o, ends, R(r), OP.subtract)

    def play(t):
        oI, oR = "oI%d" % t, "oR%d" % t
        IC, MR, IV = "IC%d" % t, "MR%d" % t, "IV%d" % t
        last = t == 1
        KI, KR, F0, F1 = [bank_for(b) for b in ("KI", "KR", "Fa", "Fb")]
        by_block("VA", oI)
        gather("VB", oI, 96, 192, 24)
        for lo, hi, n in ((0, 96, 24), (96, 192, 48)):
            gather("VR", oR, lo, hi, n, 0)
        opened(KI, 1, "krow")
        ts(R("M16"), R(oI), -2048.0, OP.add)
        group_sum(KI, 0, plain("VA"), R("Gm", 0, 8))
        together(on_levels, range(16, 1632, 272), 1)
        extremes("VB", "XB", "NB", 4)
        b = bank_for("CA")
        mms([(R(b, 0, 204), R("cq"), R("on5", 0, 204, 1, 1))]
            + [(R(b, i, 204, 2), R("IDh"), m) for m in (R("XA", 0, 816, 8), R("NA", 7, 816, 8)) for i in (0, 1)], True)
        ts(R("CA"), R(b, 0, 204), R1, OP.add, R1, OP.subtract)
        turned_centres("XB", "NB", "CTI")
        larger("VA", "CA", "DI")
        apart("VB", "CTI", "DA")
        group_sum(KI, 0, rows_of("DI"), R("G64"))
        group_sum(KI, 128, plain("DA"), R("G32"), 8)
        extremes("VR", "XR", "NR", 8)
        o = R(bank_for("CR"), 0, 192)
        mms([(o, R("IDg"), R(m, 15, 3072, 16)) for m in ("XR", "NR")], True)
        lin(R("CR"), o, 1.0, R1)
        turned_centres("XR", "NR", "CT0")
        opened(KR, 1, "kneg")
        lin(R("CS"), R("CR", 96, 192), 1.0, -R1)
        together(lambda k: select(R("CX", k, 1536, 16), R("CS"), [[0, 96]], OP.is_ge, 0, 0), range(16), 16)
        group_sum(KR, 128, plain("VR", 1536), R("Gm", 0, 8))
        opened(F0, 3, "TR")
        opened(F1, 3, "TR")
        mm(R(F0, 0, 128, 1, KP), R("CA", 0, 204, 2), R("BKm"))
        least("FK", 256, KI)
        scan(back("FB", 0, 256), R("mB"), back("FK", 256, 512), OP.add, OP.min)
        tt(R("OH"), R(KI, 0, 256, 1, KP), R("FB"), OP.is_equal)
        b = bank_for("OH")
        turn_over(b, "OH", 0, True)
        tt(R("S2"), R(b, 0, 192), R("M16"), OP.mult)
        o = R(bank_for("sL"), 0, 12)
        mms([(o, R("W1", 15 - j, 143 - j), R("S2", j, 192, 16)) for j in range(16)], True)
        ts(R("sL"), o, 2048.0, OP.add)
        ts(R("SW", 0, 12), o, 2048.0 - MID, OP.add)
        either(R("b0"), IND("ow", 4096, "sL"))
        cp(R("nL"), IND("nbw", 4096, "sL"))
        largest("FK", 0, KI)
        rest(BX("VV", ALL, slice(32, 48), p=KP), "FK", "rK")
        by_block("VN", "nL")
        gather("V2", "nL", 96, 192, 32)
        o = R(bank_for("bf"), 0, 192)
        mm(o, R("BLK"), R("b0"), True)
        either(R("bf"), o)
        ends = picked("pb", "bf")
        ts(R("SW", 12, 24), ends, R("cB"), OP.add, -MID, OP.add)
        ts(R("Lb"), ends, R("cB"), OP.add)
        lin(R("Cb"), IND("CR", 192, "Lb"), 1.0, -R1)
        o = R(bank_for("CTB"), 0, 128, 1, 96)
        mm(o, R("Cb", 96, 192), R("ID"), True)
        lin(R("CTB"), o, 1.0, 1024.0)
        b = bank_for("CB")
        mms([(R(b, 0, KP), R("on5", 0, 128, 1, 1), R("levA"))]
            + [(R(b, 17 * j + 1, 17 * j + 17), R("ID"), R("Cb", 16 * j, 16 * j + 16)) for j in range(6)], True)
        for i in (0, 1):
            either(R("CB", i, 204, 2), R(b, 0, KP))
        mm(R(F0, 128, 256, 1, KP), R("CB", 0, 204, 2), R("BKm"))
        ts(R("n16"), R("nL"), -2048.0, OP.add, 2.0 ** -13, OP.mult)
        together(lambda c: ts(BX("EQ", c, slice(0, 192 - 16 * c)), R("bf", 16 * c, 192), -MID, OP.add, R("SW", 12 + c, 13 + c), OP.is_equal), range(12), 3)
        b = bank_for("EQ")
        mm(R(b, 0, 192), R("cE"), R("half"), True)
        for c0, c1 in ((0, 3), (3, 6), (6, 11)):
            mms([(R(b, 16 * c + 16, 192), R("BK8"), BX("EQ", c, slice(16, 192 - 16 * c))) for c in range(c0, c1)])
        mm(R(b, 0, 192), R("BKh"), BX("EQ", ALL, slice(0, 16)))
        act(R("cnt"), R(b, 0, 192), AF.Sign)
        ends = picked("pc", "cnt")
        b = bank_for("LS")
        mms([(R(b, 0, 24), R("IDf"), R("SW"))] + [(R(b, lo, lo + 12), R("ID8"), ends) for lo in (0, 12)], True)
        tt(R("l1"), R(b, 0, 24), R("aC"), OP.min)
        ts(R("LS"), R("l1"), R("cS"), OP.add)
        act(IND(IV, 384, "LS", 12, 24), R("aT"), AF.Silu)
        ts(R("LI"), picked("pi", IV), R("cB"), OP.add, -63.75, OP.add)
        group_sum(F0, 0, plain("VN"), R("Gm"))
        apart("V2", "CTI", "D2")
        apart("V2", "CTB", "DB")
        larger("VN", "CA", "DJ")
        larger("VN", "CB", "DK")
        group_sum(F0, 0, rows_of("DJ"), R("G64"))
        group_sum(F0, 128, rows_of("DK"), R("G64"))
        group_sum(F1, 0, plain("D2"), R("G32"), 8)
        group_sum(F1, 128, plain("DB"), R("G32"), 8)
        apart("VR", "CT0", "DR")
        first = R("VR", 1536, 3072, 16)
        tt(first, first, R("CX", 0, 1536, 16), OP.max)
        for lo in range(0, 1536, 384):
            scan(R("DS", lo, lo + 384), R("CX", lo, lo + 384), R("VR", 1536 + lo, 1920 + lo), OP.min, OP.max)
        group_sum(KR, 0, plain("DR"), R("G32"), 8)
        group_sum(KR, 128, plain("DS"), R("G64"), 8)
        if not last:
            act(R("xg"), IND("X", 4096, "sL"), AF.Relu, -16.0)
            cp(IND("X", 4288, "LS"), R("xg"))
        JI, JR, KK, WN, NI, NR, OW, WS = [bank_for(b) for b in ("JI", "JR", "KK", "WN", "NI", "NR", "OW", "WS")]
        for bank, l in ((JI, "krow"), (JR, "kneg")):
            row(bank, l)
            mm(R(bank, 0, 192), R("ID"), R("n16"))
        mm(R(WN, 0, 192), R("IDn"), R("cnt"), True)
        mm(R(KK, 0, 192), R("ID8"), R("cnt"), True)
        row(NI, "cN" if last else "cI")
        for h, bank in ((1, F1), (0, F0)):
            for turn in (h, 1 - h):
                if turn:
                    act(BX("FM", ALL, slice(128 * h, 128 * h + 128), p=KP), R(bank, 0, 256, 1, KP), AF.Sign, R("lim") if t else -15.5, -1.0)
                else:
                    together(lambda side: (least("FS", 768 * side + 128 * h, bank, 128 * side, 128),
                                           largest("FS", 256 + 256 * side + 128 * h, bank, 128 * side, 128)), (0, 1), 2)
        scan(R("CN", 16, 272), BX("FM", 0, p=KP), BX("FM", 1, p=KP), OP.add, OP.subtract)
        rest(BX("VV", ALL, slice(0, 32), p=KP), "FS", "rS")
        tt(Z(3), R("CN", 31, 272, 16), R("CN", 15, 256, 16), OP.is_gt)
        tt(R("SS"), BX("VV", 0, p=KP), BX("VV", 1, p=KP), OP.add)
        together(lambda lo: tt(R("PP", lo, lo + 16), R("SS", lo, lo + 16), Z(3), OP.mult), (0, 16, 32), 3)
        tt(R("ZZ", 0, 768, 16), BX("VV", 1, p=KP), R("PP"), OP.subtract)
        for i, bank in enumerate((JI, JR, KK)):
            from_keys(bank, i)
        turn_over(WN, "ZZ", 768, False)
        for s, bank in (("S0", JI), ("S1", JR)):
            ts(R(s), R(bank, 0, 192), -0.25, OP.max, 0.25, OP.min)
        act(R("QK"), R(KK, 0, 192), AF.Square, R("kc"), 1024.0)
        if not last:
            mm(R(NI, 0, 192), R("BK8"), R("S0"))
            mm(R(NI, 0, 192), R("IDn"), R("QK"))
            act(R(IC), R(NI, 0, 192), AF.Relu)
            send(IC, [(dn1, "inA", "rA"), (up1, "inB", "rB")], HOP)
        else:
            mms([(R(NI, 0, 96), R("ZX", 0, 128), R("P4")), (R(NI, 96, 192), R("ZX", 128, 256, 1, 96), R("ID4", 0, 96, 1, 96))])
            mm(R(NI, 0, 192), R("BKn"), R("S0"))
            mm(R(NI, 0, 192), R("ID"), R("QK"))
            either(R(IC), R(NI, 0, 192))
            send(IC, [(dn2, "inC", "rC")], 0.8 * HOP)
        scan(R("FR"), R("mE"), R(KR, 0, 256, 1, KP), OP.add, OP.max)
        scan(back("FB", 0, 256), R("mE"), back("FR", 0, 256), OP.add, OP.max)
        tt(R("OR"), R(KR, 0, 256, 1, KP), R("FB"), OP.is_equal)
        b = bank_for("WR")
        ts(R("R16"), R(oR), -2048.0, OP.add)
        row(b, "cW")
        mm(R(b, 0, 192), R("ID"), R("R16"))
        mms([(R(b, 96 * h, 96 * h + 96), R("OR", 128 * h, 128 * h + 128, 1, 96), R("IDw", 0, 96, 1, 96)) for h in (0, 1)])
        either(R("WR"), R(b, 0, 192))
        row(NR, "cR")
        mm(R(NR, 0, 192), R("BK8"), R("S1"))
        either(R("zr", 0, 192), R(NR, 0, 192))
        tt(R(MR), IND("zr", 208, "LI"), R("WR"), OP.max)
        if not last:
            send(MR, [(up2, "inM", "rR")], 0.8 * HOP)
        act(R("wf"), R(WN, 0, 192), AF.Relu, -1.0, acc=R("wc"))
        mms([(R(OW, 0, 192), R("ID"), R("b0")), (R(OW, 0, 192), R("ID"), R("wf"))], True)
        act(R("xa"), R(OW, 0, 192))
        act(R("ya"), R(OW, 0, 192), AF.Relu, -192.0 * 191.0, 192.0)
        tt(IND("ow", 4288, "LS"), R("xa"), R("ya"), OP.subtract)
        if not last:
            act(R("wb"), R("wc"))
            mm(R(WS, 0, 1, 1, KP), R("on5", 0, KP), R("wb"), True)
            cp(R("wi"), R(WS, 0, 1, 1, KP))
            ts(R("wj"), R("wi"), 63, OP.bitwise_and)
            ts(R("lim"), R("wj"), 32.0, OP.mult, -15.5, OP.add)

    def merged(old, new, both, words, out, halves):
        for lo in halves:
            tt(R(both, lo, lo + 96), R(old, lo, lo + 96), R(new, lo, lo + 96), OP.max)
            ts(R(words, lo, lo + 96), R(both, lo, lo + 96), 4095, OP.bitwise_and)
            o, a = R(out, lo, lo + 96), R(words, lo, lo + 96)
            emit("vg", {"v": lambda o=o, a=a: g.vector.tensor_copy(o[0], a[0]),
                        "g": lambda o=o, a=a: g.affine_select(o[0], a[0], [[0, 96]], OP.is_ge, 0.0, 0, 0)}, [o], [a], 1.0, 0.17 + 192 * CYCLE)

    marks = [len(calls)]
    ts(R("aC"), R("aC"), R("p15"), OP.add, R("cS"), OP.subtract)
    ms(R("CN", 0, 16), 0.0)
    for h in (0, 1):
        either(R("TR", 128 * h, 128 * h + 128), rows)
    for o, c in ((R("ZZ", 0, 512), 0), (R("ZZ", 512), 0), (R("IV1", 0, 192), 256)):
        fill(o, c)
    play(0)
    marks.append(len(calls))
    fill(R("cN"), -32768)
    for name, of, c in (("BKn", "BLK", -8192.0), ("ID4", "ID", 4096.0), ("P4", "P0", 4096.0)):
        lin(R(name), R(of), c)
    merged("inM", "inB", "mu", "mw", "oI1", (96, 0))
    merged("MR0", "inA", "mv", "mi32", "oR1", (0, 96))
    marks.append(len(calls))
    play(1)
    marks.append(len(calls))
    ts(R("mw"), R("MR1"), 4095, OP.bitwise_and)
    for lo in (96, 0):
        tt(R("inA", lo, lo + 96), R("mw", lo, lo + 96), R("inC", lo, lo + 96), OP.min)
        act(R("yo", lo, lo + 96), R("inA", lo, lo + 96), AF.Abs)
    stores = [dma("a", 2.5, (hbm("yown"), (T.ow[0:128:16, 0:4096], [("ow", 0, 4096)]))), dma("s", 2.5, (hbm("ym"), R("yo")))]
    if not ORDER:
        order, place, _ = arrange(calls, other, span, use, marks)
        ORDER.extend(order)
        BANK.update(place)
        return
    count = issue_all()
    for q in count:
        g.wait_ge(S["q" + q], count[q])
    for sem, val in sent:
        g.wait_ge(S[sem], val)
    for sem in stores:
        g.sync.wait_ge(S[sem], 16)
